import numpy as np
import ml_dtypes


def mxq(x, axis, fmt="e4m3"):
    dtype, down = {"e4m3": (ml_dtypes.float8_e4m3fn, 7), "e5m2": (ml_dtypes.float8_e5m2, 14)}[fmt]
    v = np.moveaxis(np.asarray(x, np.float32).astype(ml_dtypes.bfloat16).astype(np.float64), axis, -1)
    blocks = v.reshape(v.shape[:-1] + (-1, 32))
    amax = np.abs(blocks).max(-1, keepdims=True)
    byte = np.maximum(np.where(amax > 0, np.frexp(amax)[1] - 1 + 127, 0) - down, 1)
    scale = np.exp2(byte - 127.0)
    codes = (blocks / scale).astype(np.float32).astype(dtype).astype(np.float64)
    return np.moveaxis((codes * scale).reshape(v.shape), -1, axis)


WIDE = False


def mx_kscale(k):
    if not WIDE:
        return np.ones(k)
    levels = np.array([10, -10, 5, -5, 0])
    if k % 512:
        return np.exp2(np.random.permutation(np.resize(levels, k // 32))).repeat(32)
    a = np.empty((k // 512, 16))
    for p in range(k // 512):
        a[p, :8] = np.random.permutation(np.resize(levels, 8))
        for g in range(8):
            far = levels[np.abs(levels - a[p, g]) >= 10]
            a[p, g + 8] = far[np.random.randint(len(far))]
    return np.exp2(a.ravel()).repeat(32)


def f64(x):
    return np.asarray(x).astype(np.float64)


def striped(idx):
    return np.tile(idx.reshape(-1, 16).T, (8, 1)).astype(np.uint16)


def unstriped(offs):
    return offs[:16].T.reshape(-1).astype(np.int64)


E2M1 = np.array([0.0, 0.5, 1.0, 1.5, 2.0, 3.0, 4.0, 6.0, -0.0, -0.5, -1.0, -1.5, -2.0, -3.0, -4.0, -6.0])


def pack_weight(w, fmt):
    k, n = w.shape
    w = f64(np.asarray(w, np.float32).astype(ml_dtypes.bfloat16)).reshape(k // 32, 32, n)
    amax = np.abs(w).max(1)
    if fmt == "e4m3":
        byte = np.frexp(amax)[1] - 1 + 127 - 7
    else:
        mant, ex = np.frexp(amax / 6.0)
        byte = np.where(mant > 0.5, ex, ex - 1) + 127
    byte = np.clip(np.where(amax > 0, byte, 1), 1, 254)
    scaled = (w * np.exp2(127.0 - byte)[:, None, :]).reshape(k, n).astype(np.float32)
    by_word = np.ascontiguousarray(scaled.reshape(k // 512, 128, 4, n).transpose(0, 1, 3, 2))
    if fmt == "e4m3":
        words = by_word.astype(ml_dtypes.float8_e4m3fn).view(np.uint8)
    else:
        c = by_word.astype(ml_dtypes.float4_e2m1fn).view(np.uint8) & 0xF
        words = (c[..., 0::2] | (c[..., 1::2] << 4)).reshape(k // 512, 128, 2 * n)
    return np.ascontiguousarray(words), np.ascontiguousarray(byte.astype(np.uint8).reshape(k // 512, 16, n))


def unpack_weight(words, scales, fmt):
    g, _, n = scales.shape
    words = np.ascontiguousarray(words).reshape(g, 128, n, -1)
    if fmt == "e4m3":
        vals = words.view(ml_dtypes.float8_e4m3fn).astype(np.float64)
    else:
        nib = np.empty((g, 128, n, 4), np.uint8)
        nib[..., 0::2] = words & 0xF
        nib[..., 1::2] = words >> 4
        vals = E2M1[nib]
    vals = vals * np.repeat(np.exp2(scales.astype(np.float64) - 127.0), 8, axis=1)[..., None]
    return vals.transpose(0, 1, 3, 2).reshape(g * 512, n)


def d_relu(v):
    return (v > 0).astype(np.float64)


K, T, E, C, H, N = 512, 512, 2, 256, 512, 1024


def by_expert(wq, xq):
    return np.concatenate([wq[e].T @ xq[:, e * C:(e + 1) * C] for e in range(E)], axis=1)


def setup_inputs():
    n = np.random.standard_normal
    v = mx_kscale(N)
    u = mx_kscale(H)
    slot_token = np.random.permutation(T)[:E * C]
    w_slot = np.random.uniform(0.2, 1.0, E * C)
    partner = np.random.permutation(T)[:E * C]
    dy = pack_weight(n((N, T)) * v[:, None], "e4m3")
    w2t = [pack_weight(m, "e4m3") for m in n((E, N, H)) / np.sqrt(N) / v[None, :, None] * u]
    w1t = [pack_weight(m, "e4m3") for m in n((E, H, K)) / np.sqrt(H) / u[None, :, None]]
    return {
        "dy_words": dy[0],
        "dy_scales": dy[1],
        "w2t_words": np.stack([m[0] for m in w2t]),
        "w2t_scales": np.stack([m[1] for m in w2t]),
        "w1t_words": np.stack([m[0] for m in w1t]),
        "w1t_scales": np.stack([m[1] for m in w1t]),
        "wpt": (n((E, H, K)) / np.sqrt(H) / u[None, :, None]).astype(np.float32),
        "a": (n((H, E * C))).astype(np.float32),
        "gate": (np.tile(w_slot, (128, 1))).astype(np.float32),
        "offs": striped(slot_token),
        "offs2": striped(partner),
    }


def reference(dy_words, dy_scales, w2t_words, w2t_scales, w1t_words, w1t_scales, wpt, a, gate, offs, offs2):
    w2t = np.stack([unpack_weight(w2t_words[e], w2t_scales[e], "e4m3") for e in range(E)])
    w1t = np.stack([unpack_weight(w1t_words[e], w1t_scales[e], "e4m3") for e in range(E)])
    wptq = mxq(f64(wpt), 1, "e4m3")
    idx, idx2 = unstriped(offs), unstriped(offs2)
    gq = unpack_weight(dy_words, dy_scales, "e4m3")[:, idx]
    dh = f64(gate[:1]) * by_expert(w2t, gq) * d_relu(f64(a))
    dq = mxq(dh, 0, "e4m3")
    out = np.zeros((K, T))
    out[:, idx] = by_expert(w1t, dq)
    out[:, idx2] += by_expert(wptq, dq)
    return out

@@ -1,0 +1,233 @@
+from contextlib import ExitStack
+
+import concourse.mybir as mybir
+from concourse.masks import make_identity
+
+K, T, E, C, H, N = 512, 512, 2, 256, 512, 1024
+FLOPS = 2 * E * C * (N * H + 2 * H * K)
+
+F32 = mybir.dt.float32
+BF16 = mybir.dt.bfloat16
+I32 = mybir.dt.int32
+U32 = mybir.dt.uint32
+U16 = mybir.dt.uint16
+U8 = mybir.dt.uint8
+FP8X4 = mybir.dt.float8_e4m3fn_x4
+ACT = mybir.ActivationFunctionType
+ALU = mybir.AluOpType
+
+P = 128
+PACK = 4
+PASSES = N // (P * PACK)
+SLOTS = E * C
+TILES = SLOTS // P
+TILES_PER_EXPERT = C // P
+CHUNKS = K // P
+WIDE = 768
+
+
+def tile_moe_dub_relu_kernel(
+    tc, dy_words, dy_scales, w2t_words, w2t_scales, w1t_words, w1t_scales, wpt, a, gate, offs, offs2, out
+):
+    nc = tc.nc
+    with ExitStack() as ctx:
+        keep = ctx.enter_context(tc.tile_pool(name="keep", bufs=1))
+        ring = ctx.enter_context(tc.tile_pool(name="ring", bufs=2))
+        psum = ctx.enter_context(tc.psum_pool(name="psum", bufs=2))
+
+        def words(name, width):
+            return keep.tile([P, width], I32, name=name, align_bytes=64)
+
+        def plane(name):
+            return keep.tile([P, 512], U8, name=name, align_bytes=64)
+
+        offs_sb = keep.tile([P, SLOTS // 16], U16, name="offs_sb")
+        offs2_sb = keep.tile([P, SLOTS // 16], U16, name="offs2_sb")
+        dy_w = [words("dy_w%d" % s, T) for s in range(PASSES)]
+        dy_s = plane("dy_s")
+        w2_w = [words("w2_w%d" % e, PASSES * H) for e in range(E)]
+        w2_s = plane("w2_s")
+        w1_w = [words("w1_w%d" % e, K) for e in range(E)]
+        w1_s = plane("w1_s")
+        gate_col = keep.tile([P, TILES], F32, name="gate_col")
+        a_sb = [keep.tile([P, PACK, C], F32, name="a_sb%d" % e) for e in range(E)]
+        wp_raw = [keep.tile([P, PACK, K], F32, name="wp_raw%d" % e) for e in range(E)]
+
+        def load_scales(queue, dst, src):
+            planes = src.shape[0]
+            for q in range(4):
+                queue.dma_start(
+                    out=dst[32 * q : 32 * q + 4 * planes, :].bitcast(I32),
+                    in_=src[:, 4 * q : 4 * q + 4, :].bitcast(I32),
+                )
+
+        def load_w2(e):
+            nc.sync.dma_start(
+                out=w2_w[e][:].rearrange("p (s i) -> p s i", s=PASSES),
+                in_=w2t_words[e].rearrange("s p i d -> p s (i d)").bitcast(I32),
+            )
+
+        def load_w1(e):
+            nc.sync.dma_start(out=w1_w[e][:], in_=w1t_words[e, 0].rearrange("p k d -> p (k d)").bitcast(I32))
+
+        def load_a(e):
+            nc.sync.dma_start(out=a_sb[e][:], in_=a[:, e * C : (e + 1) * C].rearrange("(p t) j -> p t j", t=PACK))
+
+        ident = keep.tile([P, P], F32, name="ident")
+        make_identity(nc, ident[:])
+        for pl in (dy_s, w2_s, w1_s):
+            nc.vector.memset(pl[:].bitcast(I32), 0)
+
+        load_scales(nc.scalar, dy_s, dy_scales)
+        nc.sync.dma_start(offs_sb[:], offs)
+        for s in range(PASSES):
+            nc.sync.dma_start(out=dy_w[s][:], in_=dy_words[s].rearrange("p t d -> p (t d)").bitcast(I32))
+        load_w2(0)
+        load_scales(nc.scalar, w2_s, w2t_scales.rearrange("e s b i -> (e s) b i"))
+        with nc.allow_non_contiguous_dma(reason="one gate value a partition and slot tile"):
+            nc.sync.dma_start(out=gate_col[:], in_=gate[0].rearrange("(c j) -> j c", j=P))
+        load_a(0)
+        load_w1(0)
+        load_scales(nc.sync, w1_s, w1t_scales.rearrange("e s b k -> (e s) b k"))
+        load_w2(1)
+        load_a(1)
+        load_w1(1)
+        nc.sync.dma_start(offs2_sb[:], offs2)
+        for e in range(E):
+            nc.sync.dma_start(out=wp_raw[e][:], in_=wpt[e].rearrange("(p t) k -> p t k", t=PACK))
+
+
+        g_w = [keep.tile([P, SLOTS], U32, name="g_w%d" % s, align_bytes=64) for s in range(PASSES)]
+        g_s = plane("g_s")
+        dh_w = keep.tile([P, SLOTS], U32, name="dh_w", align_bytes=64)
+        dh_s = plane("dh_s")
+        dx_sb = keep.tile([P, CHUNKS, SLOTS], F32, name="dx_sb")
+        dp_sb = keep.tile([P, CHUNKS, SLOTS], F32, name="dp_sb")
+
+        def gather(lo, hi):
+            picks = offs_sb[:, lo // 16 : hi // 16]
+            nc.vector.tensor_copy(g_s[:, lo:hi], dy_s[:].indirect(picks))
+            for s in range(PASSES):
+                nc.vector.tensor_copy(g_w[s][:, lo:hi], dy_w[s][:].bitcast(U32).indirect(picks))
+
+        def slot_tile(j):
+            e = j // TILES_PER_EXPERT
+            cols = slice(j * P, (j + 1) * P)
+            own = slice((j % TILES_PER_EXPERT) * P, (j % TILES_PER_EXPERT + 1) * P)
+
+            sums = psum.tile([P, H], F32, name="sums")
+            for s in range(PASSES):
+                nc.tensor.matmul_mx(
+                    out=sums[:],
+                    lhsT=g_w[s][:, cols].bitcast(FP8X4),
+                    lhsT_scale=g_s[4 * s : P, cols],
+                    rhs=w2_w[e][:, s * H : (s + 1) * H].bitcast(FP8X4),
+                    rhs_scale=w2_s[4 * (PASSES * e + s) : P, :],
+                    start=(s == 0),
+                    stop=(s == PASSES - 1),
+                )
+            gated = ring.tile([P, H], BF16, name="gated", align_bytes=64)
+            nc.scalar.activation(
+                gated[:].rearrange("j (u p d) -> j u p d", u=2, d=2),
+                sums[:].rearrange("j (p u d) -> j u p d", u=2, d=2),
+                ACT.Copy,
+                scale=gate_col[:, j : j + 1],
+            )
+            turned = psum.tile([P, 2, P], F32, name="turned", tag="turned")
+            for u in range(2):
+                nc.tensor.transpose(turned[:, u, :], gated[:].bitcast(F32)[:, u * P : (u + 1) * P], ident[:])
+
+            sign = ring.tile([P, P, PACK], BF16, name="sign")
+            nc.scalar.activation(sign[:], a_sb[e][:, :, own].rearrange("p t j -> p j t"), ACT.Sign)
+            mask = ring.tile([P, P, PACK], BF16, name="mask")
+            nc.scalar.activation(mask[:], sign[:], ACT.Relu)
+
+            dh = keep.tile([P, P * PACK], BF16, name="dh", tag="dh%d" % j, align_bytes=64)
+            nc.vector.tensor_tensor(
+                dh[:].rearrange("p (j u d) -> p j u d", u=2, d=2),
+                turned[:].bitcast(BF16).rearrange("p u (j d) -> p j u d", d=2),
+                mask[:].rearrange("p j (u d) -> p j u d", d=2),
+                ALU.mult,
+            )
+            nc.vector.quantize_mx(out=dh_w[:, cols].bitcast(FP8X4), scales=dh_s[:, cols], in_=dh[:])
+
+            dx_ps = psum.tile([P, CHUNKS, P], F32, name="dx_ps", tag="product", bufs=4)
+            for c in range(CHUNKS):
+                kc = slice(c * P, (c + 1) * P)
+                nc.tensor.matmul_mx(
+                    out=dx_ps[:, c, :],
+                    lhsT=w1_w[e][:, kc].bitcast(FP8X4),
+                    lhsT_scale=w1_s[4 * e : P, kc],
+                    rhs=dh_w[:, cols].bitcast(FP8X4),
+                    rhs_scale=dh_s[:, cols],
+                    start=True,
+                    stop=True,
+                )
+            nc.scalar.copy(dx_sb[:, :, cols], dx_ps[:])
+
+        gather(0, P)
+        slot_tile(0)
+        gather(P, C)
+        slot_tile(1)
+        gather(C, SLOTS)
+        slot_tile(2)
+        slot_tile(3)
+
+        by_token = [keep.tile([P, T], F32, name="by_token%d" % c) for c in range(2)]
+        by_token.append(keep.tile([P, T], F32, name="by_token2", tag="dh%d" % (TILES - 1), align_bytes=64))
+        by_partner = [keep.tile([P, T], F32, name="by_partner%d" % c) for c in range(CHUNKS)]
+
+        def scatter_dx(c, lo, hi):
+            nc.vector.tensor_copy(by_token[c][:].indirect(offs_sb[:, lo // 16 : hi // 16]), dx_sb[:, c, lo:hi])
+
+        def partner_product(e):
+            grouped = keep.tile([P, K, PACK], BF16, name="grouped", tag="grouped%d" % e, align_bytes=64)
+            for c in range(CHUNKS):
+                kc = slice(c * P, (c + 1) * P)
+                nc.scalar.copy(grouped[:, kc, :], wp_raw[e][:, :, kc].rearrange("p t k -> p k t"))
+            wp_w = ring.tile([P, K], U32, name="wp_w", align_bytes=64)
+            wp_s = ring.tile([P, K], U8, name="wp_s", align_bytes=64)
+            nc.vector.quantize_mx(
+                out=wp_w[:].bitcast(FP8X4), scales=wp_s[:], in_=grouped[:].rearrange("p k t -> p (k t)")
+            )
+            cols = slice(e * C, (e + 1) * C)
+            for h in range(CHUNKS // 2):
+                dp_ps = psum.tile([P, 2, C], F32, name="dp_ps", tag="product", bufs=4)
+                for b in range(2):
+                    kc = slice((2 * h + b) * P, (2 * h + b + 1) * P)
+                    nc.tensor.matmul_mx(
+                        out=dp_ps[:, b, :],
+                        lhsT=wp_w[:, kc].bitcast(FP8X4),
+                        lhsT_scale=wp_s[:, kc],
+                        rhs=dh_w[:, cols].bitcast(FP8X4),
+                        rhs_scale=dh_s[:, cols],
+                        start=True,
+                        stop=True,
+                    )
+                nc.scalar.copy(dp_sb[:, 2 * h : 2 * h + 2, cols], dp_ps[:])
+
+        for lo in (0, P):
+            for c in range(2):
+                scatter_dx(c, lo, lo + P)
+        scatter_dx(2, 0, C)
+        for c in range(3):
+            scatter_dx(c, C, SLOTS)
+        partner_product(0)
+        partner_product(1)
+        by_token.append(keep.tile([P, WIDE], F32, name="by_token3", tag="grouped%d" % (E - 1), align_bytes=64))
+        scatter_dx(3, 0, SLOTS)
+
+        def finish(c):
+            total = ring.tile([P, T], F32, name="total")
+            nc.vector.tensor_tensor(total[:], by_token[c][:, 0:T], by_partner[c][:, 0:T], ALU.add)
+            nc.sync.dma_start(out=out[c * P : (c + 1) * P, :], in_=total[:])
+
+        def scatter_dp(c, lo, hi):
+            nc.vector.tensor_copy(by_partner[c][:].indirect(offs2_sb[:, lo // 16 : hi // 16]), dp_sb[:, c, lo:hi])
+
+        for c in range(CHUNKS):
+            scatter_dp(c, 0, C)
+            if c > 0:
+                finish(c - 1)
+            scatter_dp(c, C, SLOTS)
+        finish(CHUNKS - 1)

@@ -43,8 +43,8 @@ def tile_moe_dub_relu_kernel(
 
         offs_sb = keep.tile([P, SLOTS // 16], U16, name="offs_sb")
         offs2_sb = keep.tile([P, SLOTS // 16], U16, name="offs2_sb")
-        dy_w = [words("dy_w%d" % s, T) for s in range(PASSES)]
-        dy_s = plane("dy_s")
+        dy_w = words("dy_w", PASSES * T)
+        dy_s = keep.tile([P, WIDE], U8, name="dy_s")
         w2_w = [words("w2_w%d" % e, PASSES * H) for e in range(E)]
         w2_s = plane("w2_s")
         w1_w = [words("w1_w%d" % e, K) for e in range(E)]
@@ -57,7 +57,7 @@ def tile_moe_dub_relu_kernel(
             planes = src.shape[0]
             for q in range(4):
                 queue.dma_start(
-                    out=dst[32 * q : 32 * q + 4 * planes, :].bitcast(I32),
+                    out=dst[32 * q : 32 * q + 4 * planes, 0:512].bitcast(I32),
                     in_=src[:, 4 * q : 4 * q + 4, :].bitcast(I32),
                 )
 
@@ -73,24 +73,28 @@ def tile_moe_dub_relu_kernel(
         def load_a(e):
             nc.sync.dma_start(out=a_sb[e][:], in_=a[:, e * C : (e + 1) * C].rearrange("(p t) j -> p t j", t=PACK))
 
+        for pl in (dy_s, w2_s, w1_s):
+            nc.gpsimd.memset(pl[:].bitcast(I32), 0)
         ident = keep.tile([P, P], F32, name="ident")
         make_identity(nc, ident[:])
-        for pl in (dy_s, w2_s, w1_s):
-            nc.vector.memset(pl[:].bitcast(I32), 0)
+        warm = keep.tile([P, 1], F32, name="warm")
+        nc.scalar.activation(warm[:], ident[:, 0:1], ACT.Copy)
 
-        load_scales(nc.scalar, dy_s, dy_scales)
         nc.sync.dma_start(offs_sb[:], offs)
-        for s in range(PASSES):
-            nc.sync.dma_start(out=dy_w[s][:], in_=dy_words[s].rearrange("p t d -> p (t d)").bitcast(I32))
+        load_scales(nc.sync, dy_s, dy_scales)
+        nc.sync.dma_start(
+            out=dy_w[:].rearrange("p (s t) -> p s t", s=PASSES),
+            in_=dy_words.rearrange("s p t d -> p s (t d)").bitcast(I32),
+        )
         load_w2(0)
-        load_scales(nc.scalar, w2_s, w2t_scales.rearrange("e s b i -> (e s) b i"))
+        load_scales(nc.sync, w2_s, w2t_scales.rearrange("e s b i -> (e s) b i"))
         with nc.allow_non_contiguous_dma(reason="one gate value a partition and slot tile"):
             nc.sync.dma_start(out=gate_col[:], in_=gate[0].rearrange("(c j) -> j c", j=P))
         load_a(0)
         load_w1(0)
+        load_a(1)
         load_scales(nc.sync, w1_s, w1t_scales.rearrange("e s b k -> (e s) b k"))
         load_w2(1)
-        load_a(1)
         load_w1(1)
         nc.sync.dma_start(offs2_sb[:], offs2)
         for e in range(E):
@@ -106,16 +110,20 @@ def tile_moe_dub_relu_kernel(
 
         def gather(lo, hi):
             picks = offs_sb[:, lo // 16 : hi // 16]
-            nc.vector.tensor_copy(g_s[:, lo:hi], dy_s[:].indirect(picks))
             for s in range(PASSES):
-                nc.vector.tensor_copy(g_w[s][:, lo:hi], dy_w[s][:].bitcast(U32).indirect(picks))
+                nc.vector.tensor_copy(g_w[s][:, lo:hi], dy_w[:, s * T : (s + 1) * T].bitcast(U32).indirect(picks))
 
-        def slot_tile(j):
+        active = [keep.tile([P, C, PACK], BF16, name="mask%d" % e) for e in range(E)]
+
+        def make_mask(e):
+            nc.vector.tensor_scalar(active[e][:], a_sb[e][:].rearrange("p t j -> p j t"), 0.0, None, ALU.is_gt)
+
+        def hidden_gradient(j, dh):
             e = j // TILES_PER_EXPERT
             cols = slice(j * P, (j + 1) * P)
             own = slice((j % TILES_PER_EXPERT) * P, (j % TILES_PER_EXPERT + 1) * P)
 
-            sums = psum.tile([P, H], F32, name="sums")
+            sums = psum.tile([P, H], F32, name="sums", tag="sums")
             for s in range(PASSES):
                 nc.tensor.matmul_mx(
                     out=sums[:],
@@ -126,56 +134,63 @@ def tile_moe_dub_relu_kernel(
                     start=(s == 0),
                     stop=(s == PASSES - 1),
                 )
-            gated = ring.tile([P, H], BF16, name="gated", align_bytes=64)
-            nc.scalar.activation(
-                gated[:].rearrange("j (u p d) -> j u p d", u=2, d=2),
-                sums[:].rearrange("j (p u d) -> j u p d", u=2, d=2),
-                ACT.Copy,
-                scale=gate_col[:, j : j + 1],
-            )
+            gated = ring.tile([P, 2, P, 2], BF16, name="gated", align_bytes=64)
             turned = psum.tile([P, 2, P], F32, name="turned", tag="turned")
             for u in range(2):
-                nc.tensor.transpose(turned[:, u, :], gated[:].bitcast(F32)[:, u * P : (u + 1) * P], ident[:])
+                nc.scalar.activation(
+                    gated[:, u, :, :],
+                    sums[:].rearrange("j (p u d) -> j u p d", u=2, d=2)[:, u, :, :],
+                    ACT.Copy,
+                    scale=gate_col[:, j : j + 1],
+                )
+                nc.tensor.transpose(turned[:, u, :], gated[:, u, :, :].rearrange("j p d -> j (p d)").bitcast(F32), ident[:])
 
-            sign = ring.tile([P, P, PACK], BF16, name="sign")
-            nc.scalar.activation(sign[:], a_sb[e][:, :, own].rearrange("p t j -> p j t"), ACT.Sign)
-            mask = ring.tile([P, P, PACK], BF16, name="mask")
-            nc.scalar.activation(mask[:], sign[:], ACT.Relu)
-
-            dh = keep.tile([P, P * PACK], BF16, name="dh", tag="dh%d" % j, align_bytes=64)
             nc.vector.tensor_tensor(
-                dh[:].rearrange("p (j u d) -> p j u d", u=2, d=2),
+                dh.rearrange("p (j u d) -> p j u d", u=2, d=2),
                 turned[:].bitcast(BF16).rearrange("p u (j d) -> p j u d", d=2),
-                mask[:].rearrange("p j (u d) -> p j u d", d=2),
+                active[e][:, own, :].rearrange("p j (u d) -> p j u d", d=2),
                 ALU.mult,
             )
-            nc.vector.quantize_mx(out=dh_w[:, cols].bitcast(FP8X4), scales=dh_s[:, cols], in_=dh[:])
 
-            dx_ps = psum.tile([P, CHUNKS, P], F32, name="dx_ps", tag="product", bufs=4)
-            for c in range(CHUNKS):
+        def product(weights, scales, cols, chunks, dst):
+            width = cols.stop - cols.start
+            acc = psum.tile([P, len(chunks), width], F32, name="acc", tag="product", bufs=4)
+            for b, c in enumerate(chunks):
                 kc = slice(c * P, (c + 1) * P)
                 nc.tensor.matmul_mx(
-                    out=dx_ps[:, c, :],
-                    lhsT=w1_w[e][:, kc].bitcast(FP8X4),
-                    lhsT_scale=w1_s[4 * e : P, kc],
+                    out=acc[:, b, :],
+                    lhsT=weights[:, kc].bitcast(FP8X4),
+                    lhsT_scale=scales[:, kc],
                     rhs=dh_w[:, cols].bitcast(FP8X4),
                     rhs_scale=dh_s[:, cols],
                     start=True,
                     stop=True,
                 )
-            nc.scalar.copy(dx_sb[:, :, cols], dx_ps[:])
+            nc.scalar.copy(dst[:, chunks[0] : chunks[-1] + 1, cols], acc[:])
 
+        def token_product(tiles, groups):
+            e = tiles[0] // TILES_PER_EXPERT
+            cols = slice(tiles[0] * P, (tiles[-1] + 1) * P)
+            dh = keep.tile([P, len(tiles) * P * PACK], BF16, name="dh", tag="dh%d" % tiles[-1], align_bytes=64)
+            for n, j in enumerate(tiles):
+                hidden_gradient(j, dh[:, n * P * PACK : (n + 1) * P * PACK])
+            nc.vector.quantize_mx(out=dh_w[:, cols].bitcast(FP8X4), scales=dh_s[:, cols], in_=dh[:])
+            for chunks in groups:
+                product(w1_w[e], w1_s[4 * e : P, :], cols, chunks, dx_sb)
+
+        nc.vector.tensor_copy(g_s[:], dy_s[:].indirect(offs_sb[:]))
         gather(0, P)
-        slot_tile(0)
         gather(P, C)
-        slot_tile(1)
+        make_mask(0)
+        token_product([0], [[0], [1, 2, 3]])
+        token_product([1], [[0, 1, 2, 3]])
         gather(C, SLOTS)
-        slot_tile(2)
-        slot_tile(3)
+        make_mask(1)
+        token_product([2, 3], [[0, 1], [2, 3]])
 
         by_token = [keep.tile([P, T], F32, name="by_token%d" % c) for c in range(2)]
         by_token.append(keep.tile([P, T], F32, name="by_token2", tag="dh%d" % (TILES - 1), align_bytes=64))
-        by_partner = [keep.tile([P, T], F32, name="by_partner%d" % c) for c in range(CHUNKS)]
+        by_partner = []
 
         def scatter_dx(c, lo, hi):
             nc.vector.tensor_copy(by_token[c][:].indirect(offs_sb[:, lo // 16 : hi // 16]), dx_sb[:, c, lo:hi])
@@ -190,21 +205,8 @@ def tile_moe_dub_relu_kernel(
             nc.vector.quantize_mx(
                 out=wp_w[:].bitcast(FP8X4), scales=wp_s[:], in_=grouped[:].rearrange("p k t -> p (k t)")
             )
-            cols = slice(e * C, (e + 1) * C)
-            for h in range(CHUNKS // 2):
-                dp_ps = psum.tile([P, 2, C], F32, name="dp_ps", tag="product", bufs=4)
-                for b in range(2):
-                    kc = slice((2 * h + b) * P, (2 * h + b + 1) * P)
-                    nc.tensor.matmul_mx(
-                        out=dp_ps[:, b, :],
-                        lhsT=wp_w[:, kc].bitcast(FP8X4),
-                        lhsT_scale=wp_s[:, kc],
-                        rhs=dh_w[:, cols].bitcast(FP8X4),
-                        rhs_scale=dh_s[:, cols],
-                        start=True,
-                        stop=True,
-                    )
-                nc.scalar.copy(dp_sb[:, 2 * h : 2 * h + 2, cols], dp_ps[:])
+            for chunks in ([0], [1], [2, 3]):
+                product(wp_w, wp_s, slice(e * C, (e + 1) * C), chunks, dp_sb)
 
         for lo in (0, P):
             for c in range(2):
@@ -213,21 +215,44 @@ def tile_moe_dub_relu_kernel(
         for c in range(3):
             scatter_dx(c, C, SLOTS)
         partner_product(0)
-        partner_product(1)
-        by_token.append(keep.tile([P, WIDE], F32, name="by_token3", tag="grouped%d" % (E - 1), align_bytes=64))
+        by_token.append(keep.tile([P, WIDE], F32, name="by_token3", tag="grouped0", align_bytes=64))
         scatter_dx(3, 0, SLOTS)
-
-        def finish(c):
-            total = ring.tile([P, T], F32, name="total")
-            nc.vector.tensor_tensor(total[:], by_token[c][:, 0:T], by_partner[c][:, 0:T], ALU.add)
-            nc.sync.dma_start(out=out[c * P : (c + 1) * P, :], in_=total[:])
 
         def scatter_dp(c, lo, hi):
             nc.vector.tensor_copy(by_partner[c][:].indirect(offs2_sb[:, lo // 16 : hi // 16]), dp_sb[:, c, lo:hi])
 
-        for c in range(CHUNKS):
-            scatter_dp(c, 0, C)
-            if c > 0:
-                finish(c - 1)
+        def finish_on_tensor(c):
+            both = psum.tile([P, T // P, P], F32, name="both", tag="sums")
+            for b in range(T // P):
+                tb = slice(b * P, (b + 1) * P)
+                nc.tensor.matmul(both[:, b, :], by_token[c][:, tb], ident[:], start=True, stop=False, is_transpose=True)
+                nc.tensor.matmul(both[:, b, :], by_partner[c][:, tb], ident[:], start=False, stop=True, is_transpose=True)
+            both_sb = ring.tile([P, T // P, P], F32, name="both_sb")
+            nc.scalar.copy(both_sb[:], both[:])
+            back = psum.tile([P, T // P, P], F32, name="back", tag="turned")
+            for b in range(T // P):
+                nc.tensor.transpose(back[:, b, :], both_sb[:, b, :], ident[:])
+            total = keep.tile([P, T], F32, name="total%d" % c)
+            nc.scalar.copy(total[:], back[:].rearrange("p b t -> p (b t)"))
+            nc.scalar.dma_start(out=out[c * P : (c + 1) * P, :], in_=total[:])
+
+        def finish_on_vector(c):
+            for h in range(2):
+                half = slice(h * T // 2, (h + 1) * T // 2)
+                part = ring.tile([P, T // 2], F32, name="part")
+                nc.vector.tensor_tensor(part[:], by_token[c][:, half], by_partner[c][:, half], ALU.add)
+                nc.sync.dma_start(out=out[c * P : (c + 1) * P, half], in_=part[:])
+
+        by_partner.append(keep.tile([P, T], F32, name="by_partner0"))
+        scatter_dp(0, 0, C)
+        partner_product(1)
+        by_partner.append(keep.tile([P, T], F32, name="by_partner1", tag="grouped1", align_bytes=64))
+        scatter_dp(1, 0, C)
+        for c in range(2):
             scatter_dp(c, C, SLOTS)
-        finish(CHUNKS - 1)
+            finish_on_tensor(c)
+        by_partner.extend([keep.tile([P, WIDE], F32, name="by_partner%d" % c) for c in (2, 3)])
+        scatter_dp(2, 0, SLOTS)
+        finish_on_tensor(2)
+        scatter_dp(3, 0, SLOTS)
+        finish_on_vector(3)

@@ -49,6 +49,7 @@ def tile_moe_dub_relu_kernel(
         w2_s = plane("w2_s")
         w1_w = [words("w1_w%d" % e, K) for e in range(E)]
         w1_s = plane("w1_s")
+        gate_rows = keep.tile([P, P], F32, name="gate_rows")
         gate_col = keep.tile([P, TILES], F32, name="gate_col")
         a_sb = [keep.tile([P, PACK, C], F32, name="a_sb%d" % e) for e in range(E)]
         wp_raw = [keep.tile([P, PACK, K], F32, name="wp_raw%d" % e) for e in range(E)]
@@ -75,10 +76,9 @@ def tile_moe_dub_relu_kernel(
 
         for pl in (dy_s, w2_s, w1_s):
             nc.gpsimd.memset(pl[:].bitcast(I32), 0)
+        nc.gpsimd.memset(gate_rows[:], 0.0)
         ident = keep.tile([P, P], F32, name="ident")
         make_identity(nc, ident[:])
-        warm = keep.tile([P, 1], F32, name="warm")
-        nc.scalar.activation(warm[:], ident[:, 0:1], ACT.Copy)
 
         nc.sync.dma_start(offs_sb[:], offs)
         load_scales(nc.sync, dy_s, dy_scales)
@@ -87,9 +87,8 @@ def tile_moe_dub_relu_kernel(
             in_=dy_words.rearrange("s p t d -> p s (t d)").bitcast(I32),
         )
         load_w2(0)
+        nc.sync.dma_start(out=gate_rows[0:TILES, :], in_=gate[0].rearrange("(c j) -> c j", j=P))
         load_scales(nc.sync, w2_s, w2t_scales.rearrange("e s b i -> (e s) b i"))
-        with nc.allow_non_contiguous_dma(reason="one gate value a partition and slot tile"):
-            nc.sync.dma_start(out=gate_col[:], in_=gate[0].rearrange("(c j) -> j c", j=P))
         load_a(0)
         load_w1(0)
         load_a(1)
@@ -100,6 +99,10 @@ def tile_moe_dub_relu_kernel(
         for e in range(E):
             nc.sync.dma_start(out=wp_raw[e][:], in_=wpt[e].rearrange("(p t) k -> p t k", t=PACK))
 
+
+        gate_turned = psum.tile([P, P], F32, name="gate_turned", tag="turned")
+        nc.tensor.transpose(gate_turned[:], gate_rows[:], ident[:])
+        nc.scalar.activation(gate_col[:], gate_turned[:, 0:TILES], ACT.Copy)
 
         g_w = [keep.tile([P, SLOTS], U32, name="g_w%d" % s, align_bytes=64) for s in range(PASSES)]
         g_s = plane("g_s")
@@ -222,19 +225,20 @@ def tile_moe_dub_relu_kernel(
             nc.vector.tensor_copy(by_partner[c][:].indirect(offs2_sb[:, lo // 16 : hi // 16]), dp_sb[:, c, lo:hi])
 
         def finish_on_tensor(c):
-            both = psum.tile([P, T // P, P], F32, name="both", tag="sums")
-            for b in range(T // P):
-                tb = slice(b * P, (b + 1) * P)
-                nc.tensor.matmul(both[:, b, :], by_token[c][:, tb], ident[:], start=True, stop=False, is_transpose=True)
-                nc.tensor.matmul(both[:, b, :], by_partner[c][:, tb], ident[:], start=False, stop=True, is_transpose=True)
-            both_sb = ring.tile([P, T // P, P], F32, name="both_sb")
-            nc.scalar.copy(both_sb[:], both[:])
-            back = psum.tile([P, T // P, P], F32, name="back", tag="turned")
-            for b in range(T // P):
-                nc.tensor.transpose(back[:, b, :], both_sb[:, b, :], ident[:])
-            total = keep.tile([P, T], F32, name="total%d" % c)
-            nc.scalar.copy(total[:], back[:].rearrange("p b t -> p (b t)"))
-            nc.scalar.dma_start(out=out[c * P : (c + 1) * P, :], in_=total[:])
+            for h in range(2):
+                both = psum.tile([P, 2, P], F32, name="both", tag="sums")
+                for b in range(2):
+                    tb = slice((2 * h + b) * P, (2 * h + b + 1) * P)
+                    nc.tensor.matmul(both[:, b, :], by_token[c][:, tb], ident[:], start=True, stop=False, is_transpose=True)
+                    nc.tensor.matmul(both[:, b, :], by_partner[c][:, tb], ident[:], start=False, stop=True, is_transpose=True)
+                both_sb = ring.tile([P, 2, P], F32, name="both_sb")
+                nc.scalar.copy(both_sb[:], both[:])
+                back = psum.tile([P, 2, P], F32, name="back", tag="turned")
+                for b in range(2):
+                    nc.tensor.transpose(back[:, b, :], both_sb[:, b, :], ident[:])
+                total = keep.tile([P, T // 2], F32, name="total%d_%d" % (c, h))
+                nc.scalar.copy(total[:], back[:].rearrange("p b t -> p (b t)"))
+                nc.scalar.dma_start(out=out[c * P : (c + 1) * P, h * T // 2 : (h + 1) * T // 2], in_=total[:])
 
         def finish_on_vector(c):
             for h in range(2):

@@ -18,11 +18,14 @@ ALU = mybir.AluOpType
 
 P = 128
 PACK = 4
+QUADRANTS = 4
+PER_COLUMN = 16
 PASSES = N // (P * PACK)
 SLOTS = E * C
 TILES = SLOTS // P
 TILES_PER_EXPERT = C // P
 CHUNKS = K // P
+LAST = CHUNKS - 1
 WIDE = 768
 
 
@@ -35,31 +38,30 @@ def tile_moe_dub_relu_kernel(
         ring = ctx.enter_context(tc.tile_pool(name="ring", bufs=2))
         psum = ctx.enter_context(tc.psum_pool(name="psum", bufs=2))
 
-        def words(name, width):
-            return keep.tile([P, width], I32, name=name, align_bytes=64)
-
-        def plane(name):
-            return keep.tile([P, 512], U8, name=name, align_bytes=64)
-
-        offs_sb = keep.tile([P, SLOTS // 16], U16, name="offs_sb")
-        offs2_sb = keep.tile([P, SLOTS // 16], U16, name="offs2_sb")
-        dy_w = words("dy_w", PASSES * T)
+        offs_sb = keep.tile([P, SLOTS // PER_COLUMN], U16, name="offs_sb")
+        offs2_sb = keep.tile([P, SLOTS // PER_COLUMN], U16, name="offs2_sb")
+        dy_w = keep.tile([P, PASSES * T], I32, name="dy_w")
         dy_s = keep.tile([P, WIDE], U8, name="dy_s")
-        w2_w = [words("w2_w%d" % e, PASSES * H) for e in range(E)]
-        w2_s = plane("w2_s")
-        w1_w = [words("w1_w%d" % e, K) for e in range(E)]
-        w1_s = plane("w1_s")
+        w2_w = [keep.tile([P, PASSES * H], I32, name="w2_w%d" % e, align_bytes=64) for e in range(E)]
+        w2_s = keep.tile([P, H], U8, name="w2_s", align_bytes=64)
+        w1_w = [keep.tile([P, K], I32, name="w1_w%d" % e, align_bytes=64) for e in range(E)]
+        w1_s = keep.tile([P, K], U8, name="w1_s", align_bytes=64)
         gate_rows = keep.tile([P, P], F32, name="gate_rows")
-        gate_col = keep.tile([P, TILES], F32, name="gate_col")
         a_sb = [keep.tile([P, PACK, C], F32, name="a_sb%d" % e) for e in range(E)]
-        wp_raw = [keep.tile([P, PACK, K], F32, name="wp_raw%d" % e) for e in range(E)]
+        wp_raw = [keep.tile([P, PACK, K], F32, name="wp_raw", tag="wp_raw%d" % e) for e in range(E)]
 
-        def load_scales(queue, dst, src):
-            planes = src.shape[0]
-            for q in range(4):
-                queue.dma_start(
-                    out=dst[32 * q : 32 * q + 4 * planes, 0:512].bitcast(I32),
-                    in_=src[:, 4 * q : 4 * q + 4, :].bitcast(I32),
+        for plane in (dy_s, w2_s, w1_s):
+            nc.gpsimd.memset(plane[:].bitcast(I32), 0)
+        nc.gpsimd.memset(gate_rows[:], 0.0)
+        ident = keep.tile([P, P], F32, name="ident")
+        make_identity(nc, ident[:])
+
+        def load_scales(plane, rows):
+            passes, width = rows.shape[0], rows.shape[2]
+            for q in range(QUADRANTS):
+                nc.sync.dma_start(
+                    out=plane[32 * q : 32 * q + 4 * passes, 0:width].bitcast(I32),
+                    in_=rows[:, 4 * q : 4 * q + 4, :].bitcast(I32),
                 )
 
         def load_w2(e):
@@ -74,189 +76,188 @@ def tile_moe_dub_relu_kernel(
         def load_a(e):
             nc.sync.dma_start(out=a_sb[e][:], in_=a[:, e * C : (e + 1) * C].rearrange("(p t) j -> p t j", t=PACK))
 
-        for pl in (dy_s, w2_s, w1_s):
-            nc.gpsimd.memset(pl[:].bitcast(I32), 0)
-        nc.gpsimd.memset(gate_rows[:], 0.0)
-        ident = keep.tile([P, P], F32, name="ident")
-        make_identity(nc, ident[:])
-
         nc.sync.dma_start(offs_sb[:], offs)
-        load_scales(nc.sync, dy_s, dy_scales)
+        load_scales(dy_s, dy_scales)
         nc.sync.dma_start(
             out=dy_w[:].rearrange("p (s t) -> p s t", s=PASSES),
             in_=dy_words.rearrange("s p t d -> p s (t d)").bitcast(I32),
         )
         load_w2(0)
-        nc.sync.dma_start(out=gate_rows[0:TILES, :], in_=gate[0].rearrange("(c j) -> c j", j=P))
-        load_scales(nc.sync, w2_s, w2t_scales.rearrange("e s b i -> (e s) b i"))
+        nc.sync.dma_start(out=gate_rows[0:TILES, :], in_=gate[0].rearrange("(j x) -> j x", x=P))
+        load_scales(w2_s, w2t_scales.rearrange("e s b i -> (e s) b i"))
         load_a(0)
         load_w1(0)
         load_a(1)
-        load_scales(nc.sync, w1_s, w1t_scales.rearrange("e s b k -> (e s) b k"))
+        load_scales(w1_s, w1t_scales.rearrange("e s b k -> (e s) b k"))
         load_w2(1)
         load_w1(1)
         nc.sync.dma_start(offs2_sb[:], offs2)
         for e in range(E):
             nc.sync.dma_start(out=wp_raw[e][:], in_=wpt[e].rearrange("(p t) k -> p t k", t=PACK))
 
-
         gate_turned = psum.tile([P, P], F32, name="gate_turned", tag="turned")
         nc.tensor.transpose(gate_turned[:], gate_rows[:], ident[:])
+        gate_col = keep.tile([P, TILES], F32, name="gate_col")
         nc.scalar.activation(gate_col[:], gate_turned[:, 0:TILES], ACT.Copy)
 
-        g_w = [keep.tile([P, SLOTS], U32, name="g_w%d" % s, align_bytes=64) for s in range(PASSES)]
-        g_s = plane("g_s")
+        slot_w = [keep.tile([P, SLOTS], U32, name="slot_w%d" % s, align_bytes=64) for s in range(PASSES)]
+        slot_s = keep.tile([P, SLOTS], U8, name="slot_s", align_bytes=64)
+        active = [keep.tile([P, C, PACK], BF16, name="active%d" % e) for e in range(E)]
         dh_w = keep.tile([P, SLOTS], U32, name="dh_w", align_bytes=64)
-        dh_s = plane("dh_s")
-        dx_sb = keep.tile([P, CHUNKS, SLOTS], F32, name="dx_sb")
-        dp_sb = keep.tile([P, CHUNKS, SLOTS], F32, name="dp_sb")
+        dh_s = keep.tile([P, SLOTS], U8, name="dh_s", align_bytes=64)
 
-        def gather(lo, hi):
-            picks = offs_sb[:, lo // 16 : hi // 16]
+        def entries(offsets, lo, hi):
+            return offsets[:, lo // PER_COLUMN : hi // PER_COLUMN]
+
+        def gather_words(lo, hi):
             for s in range(PASSES):
-                nc.vector.tensor_copy(g_w[s][:, lo:hi], dy_w[:, s * T : (s + 1) * T].bitcast(U32).indirect(picks))
+                window = dy_w[:, s * T : (s + 1) * T].bitcast(U32)
+                nc.vector.tensor_copy(slot_w[s][:, lo:hi], window.indirect(entries(offs_sb, lo, hi)))
 
-        active = [keep.tile([P, C, PACK], BF16, name="mask%d" % e) for e in range(E)]
-
-        def make_mask(e):
-            nc.vector.tensor_scalar(active[e][:], a_sb[e][:].rearrange("p t j -> p j t"), 0.0, None, ALU.is_gt)
+        def relu_mask(e):
+            nc.vector.tensor_scalar(active[e][:], a_sb[e][:].rearrange("p t x -> p x t"), 0.0, None, ALU.is_gt)
 
         def hidden_gradient(j, dh):
             e = j // TILES_PER_EXPERT
             cols = slice(j * P, (j + 1) * P)
-            own = slice((j % TILES_PER_EXPERT) * P, (j % TILES_PER_EXPERT + 1) * P)
-
+            own = slice(j * P - e * C, (j + 1) * P - e * C)
             sums = psum.tile([P, H], F32, name="sums", tag="sums")
             for s in range(PASSES):
                 nc.tensor.matmul_mx(
                     out=sums[:],
-                    lhsT=g_w[s][:, cols].bitcast(FP8X4),
-                    lhsT_scale=g_s[4 * s : P, cols],
+                    lhsT=slot_w[s][:, cols].bitcast(FP8X4),
+                    lhsT_scale=slot_s[4 * s : P, cols],
                     rhs=w2_w[e][:, s * H : (s + 1) * H].bitcast(FP8X4),
                     rhs_scale=w2_s[4 * (PASSES * e + s) : P, :],
                     start=(s == 0),
                     stop=(s == PASSES - 1),
                 )
-            gated = ring.tile([P, 2, P, 2], BF16, name="gated", align_bytes=64)
+            gated = ring.tile([P, 2, P, 2], BF16, name="gated")
             turned = psum.tile([P, 2, P], F32, name="turned", tag="turned")
             for u in range(2):
                 nc.scalar.activation(
                     gated[:, u, :, :],
-                    sums[:].rearrange("j (p u d) -> j u p d", u=2, d=2)[:, u, :, :],
+                    sums[:].rearrange("x (p u d) -> x u p d", u=2, d=2)[:, u, :, :],
                     ACT.Copy,
                     scale=gate_col[:, j : j + 1],
                 )
-                nc.tensor.transpose(turned[:, u, :], gated[:, u, :, :].rearrange("j p d -> j (p d)").bitcast(F32), ident[:])
-
+                pairs = gated[:, u, :, :].rearrange("x p d -> x (p d)").bitcast(F32)
+                nc.tensor.transpose(turned[:, u, :], pairs, ident[:])
             nc.vector.tensor_tensor(
-                dh.rearrange("p (j u d) -> p j u d", u=2, d=2),
-                turned[:].bitcast(BF16).rearrange("p u (j d) -> p j u d", d=2),
-                active[e][:, own, :].rearrange("p j (u d) -> p j u d", d=2),
+                dh.rearrange("p (x u d) -> p x u d", u=2, d=2),
+                turned[:].bitcast(BF16).rearrange("p u (x d) -> p x u d", d=2),
+                active[e][:, own, :].rearrange("p x (u d) -> p x u d", d=2),
                 ALU.mult,
             )
 
-        def product(weights, scales, cols, chunks, dst):
-            width = cols.stop - cols.start
-            acc = psum.tile([P, len(chunks), width], F32, name="acc", tag="product", bufs=4)
-            for b, c in enumerate(chunks):
-                kc = slice(c * P, (c + 1) * P)
-                nc.tensor.matmul_mx(
-                    out=acc[:, b, :],
-                    lhsT=weights[:, kc].bitcast(FP8X4),
-                    lhsT_scale=scales[:, kc],
-                    rhs=dh_w[:, cols].bitcast(FP8X4),
-                    rhs_scale=dh_s[:, cols],
-                    start=True,
-                    stop=True,
-                )
-            nc.scalar.copy(dst[:, chunks[0] : chunks[-1] + 1, cols], acc[:])
-
-        def token_product(tiles, groups):
-            e = tiles[0] // TILES_PER_EXPERT
+        def quantised_gradient(tiles, tag):
             cols = slice(tiles[0] * P, (tiles[-1] + 1) * P)
-            dh = keep.tile([P, len(tiles) * P * PACK], BF16, name="dh", tag="dh%d" % tiles[-1], align_bytes=64)
+            dh = keep.tile([P, len(tiles) * P * PACK], BF16, name="dh", tag=tag, align_bytes=64)
             for n, j in enumerate(tiles):
                 hidden_gradient(j, dh[:, n * P * PACK : (n + 1) * P * PACK])
             nc.vector.quantize_mx(out=dh_w[:, cols].bitcast(FP8X4), scales=dh_s[:, cols], in_=dh[:])
-            for chunks in groups:
-                product(w1_w[e], w1_s[4 * e : P, :], cols, chunks, dx_sb)
 
-        nc.vector.tensor_copy(g_s[:], dy_s[:].indirect(offs_sb[:]))
-        gather(0, P)
-        gather(P, C)
-        make_mask(0)
-        token_product([0], [[0], [1, 2, 3]])
-        token_product([1], [[0, 1, 2, 3]])
-        gather(C, SLOTS)
-        make_mask(1)
-        token_product([2, 3], [[0, 1], [2, 3]])
+        def products(dst, parts):
+            width = parts[0][4] - parts[0][3]
+            acc = psum.tile([P, len(parts), width], F32, name="acc", tag="product", bufs=4)
+            for b, (weights, plane, column, lo, hi) in enumerate(parts):
+                nc.tensor.matmul_mx(
+                    out=acc[:, b, :],
+                    lhsT=weights[:, column : column + P].bitcast(FP8X4),
+                    lhsT_scale=plane[:, column : column + P],
+                    rhs=dh_w[:, lo:hi].bitcast(FP8X4),
+                    rhs_scale=dh_s[:, lo:hi],
+                    start=True,
+                    stop=True,
+                )
+            nc.scalar.copy(dst, acc[:])
 
-        by_token = [keep.tile([P, T], F32, name="by_token%d" % c) for c in range(2)]
-        by_token.append(keep.tile([P, T], F32, name="by_token2", tag="dh%d" % (TILES - 1), align_bytes=64))
-        by_partner = []
+        def token_products(dst, chunks, lo, hi):
+            e = lo // C
+            products(dst, [(w1_w[e], w1_s[4 * e : P, :], c * P, lo, hi) for c in chunks])
 
-        def scatter_dx(c, lo, hi):
-            nc.vector.tensor_copy(by_token[c][:].indirect(offs_sb[:, lo // 16 : hi // 16]), dx_sb[:, c, lo:hi])
+        nc.vector.tensor_copy(slot_s[:], dy_s[:].indirect(offs_sb[:]))
+        gather_words(0, P)
+        gather_words(P, C)
+        relu_mask(0)
+        dx_first = keep.tile([P, CHUNKS, C], F32, name="dx_first")
+        quantised_gradient([0], "dh0")
+        token_products(dx_first[:, 0:1, 0:P], [0], 0, P)
+        token_products(dx_first[:, 1:CHUNKS, 0:P], range(1, CHUNKS), 0, P)
+        quantised_gradient([1], "dh1")
+        token_products(dx_first[:, :, P:C], range(CHUNKS), P, C)
+        gather_words(C, SLOTS)
+        relu_mask(1)
+        quantised_gradient([2, 3], "dh2")
 
-        def partner_product(e):
-            grouped = keep.tile([P, K, PACK], BF16, name="grouped", tag="grouped%d" % e, align_bytes=64)
+        wp_grouped = keep.tile([P, E, K, PACK], BF16, name="wp_grouped", align_bytes=64)
+
+        def round_partner_weights(e):
             for c in range(CHUNKS):
                 kc = slice(c * P, (c + 1) * P)
-                nc.scalar.copy(grouped[:, kc, :], wp_raw[e][:, :, kc].rearrange("p t k -> p k t"))
-            wp_w = ring.tile([P, K], U32, name="wp_w", align_bytes=64)
-            wp_s = ring.tile([P, K], U8, name="wp_s", align_bytes=64)
-            nc.vector.quantize_mx(
-                out=wp_w[:].bitcast(FP8X4), scales=wp_s[:], in_=grouped[:].rearrange("p k t -> p (k t)")
-            )
-            for chunks in ([0], [1], [2, 3]):
-                product(wp_w, wp_s, slice(e * C, (e + 1) * C), chunks, dp_sb)
+                nc.scalar.copy(wp_grouped[:, e, kc, :], wp_raw[e][:, :, kc].rearrange("p t k -> p k t"))
 
-        for lo in (0, P):
-            for c in range(2):
-                scatter_dx(c, lo, lo + P)
-        scatter_dx(2, 0, C)
-        for c in range(3):
-            scatter_dx(c, C, SLOTS)
-        partner_product(0)
-        by_token.append(keep.tile([P, WIDE], F32, name="by_token3", tag="grouped0", align_bytes=64))
-        scatter_dx(3, 0, SLOTS)
+        round_partner_weights(0)
+        dx_second = keep.tile([P, LAST, C], F32, name="dx_second", tag="wp_raw0")
+        token_products(dx_second[:, 0:1, :], [0], C, SLOTS)
+        token_products(dx_second[:, 1:LAST, :], range(1, LAST), C, SLOTS)
 
-        def scatter_dp(c, lo, hi):
-            nc.vector.tensor_copy(by_partner[c][:].indirect(offs2_sb[:, lo // 16 : hi // 16]), dp_sb[:, c, lo:hi])
+        by_token = [keep.tile([P, T], F32, name="by_token%d" % c) for c in range(LAST)]
+        by_token.append(keep.tile([P, T], F32, name="by_token_last", tag="dh2", align_bytes=64))
 
-        def finish_on_tensor(c):
-            for h in range(2):
+        def scatter_dx(c, lo, hi, values):
+            nc.vector.tensor_copy(by_token[c][:].indirect(entries(offs_sb, lo, hi)), values)
+
+        for lo in range(0, C, P):
+            for c in range(LAST):
+                scatter_dx(c, lo, lo + P, dx_first[:, c, lo : lo + P])
+        scatter_dx(LAST, 0, C, dx_first[:, LAST, :])
+        for c in range(LAST):
+            scatter_dx(c, C, SLOTS, dx_second[:, c, :])
+
+        round_partner_weights(1)
+        wp_w = keep.tile([P, E * K], U32, name="wp_w", align_bytes=64)
+        wp_s = keep.tile([P, E * K], U8, name="wp_s", align_bytes=64)
+        nc.vector.quantize_mx(
+            out=wp_w[:].bitcast(FP8X4), scales=wp_s[:], in_=wp_grouped[:].rearrange("p e k t -> p (e k t)")
+        )
+        dx_last = keep.tile([P, 1, C], F32, name="dx_last", tag="wp_raw1")
+        token_products(dx_last[:], [LAST], C, SLOTS)
+        scatter_dx(LAST, C, SLOTS, dx_last[:, 0, :])
+
+        dp_sb = keep.tile([P, CHUNKS, E, C], F32, name="dp_sb")
+        for c in range(CHUNKS):
+            products(dp_sb[:, c, :, :], [(wp_w, wp_s, e * K + c * P, e * C, (e + 1) * C) for e in range(E)])
+
+        def add_on_tensor(c, by_partner):
+            for lo in range(0, T, 2 * P):
                 both = psum.tile([P, 2, P], F32, name="both", tag="sums")
                 for b in range(2):
-                    tb = slice((2 * h + b) * P, (2 * h + b + 1) * P)
-                    nc.tensor.matmul(both[:, b, :], by_token[c][:, tb], ident[:], start=True, stop=False, is_transpose=True)
-                    nc.tensor.matmul(both[:, b, :], by_partner[c][:, tb], ident[:], start=False, stop=True, is_transpose=True)
+                    block = slice(lo + b * P, lo + (b + 1) * P)
+                    for first, source in ((True, by_token[c]), (False, by_partner)):
+                        nc.tensor.matmul(
+                            both[:, b, :], source[:, block], ident[:], start=first, stop=not first, is_transpose=True
+                        )
                 both_sb = ring.tile([P, 2, P], F32, name="both_sb")
                 nc.scalar.copy(both_sb[:], both[:])
                 back = psum.tile([P, 2, P], F32, name="back", tag="turned")
                 for b in range(2):
                     nc.tensor.transpose(back[:, b, :], both_sb[:, b, :], ident[:])
-                total = keep.tile([P, T // 2], F32, name="total%d_%d" % (c, h))
+                total = keep.tile([P, 2 * P], F32, name="total%d_%d" % (c, lo))
                 nc.scalar.copy(total[:], back[:].rearrange("p b t -> p (b t)"))
-                nc.scalar.dma_start(out=out[c * P : (c + 1) * P, h * T // 2 : (h + 1) * T // 2], in_=total[:])
+                nc.scalar.dma_start(out=out[c * P : (c + 1) * P, lo : lo + 2 * P], in_=total[:])
 
-        def finish_on_vector(c):
-            for h in range(2):
-                half = slice(h * T // 2, (h + 1) * T // 2)
-                part = ring.tile([P, T // 2], F32, name="part")
-                nc.vector.tensor_tensor(part[:], by_token[c][:, half], by_partner[c][:, half], ALU.add)
-                nc.sync.dma_start(out=out[c * P : (c + 1) * P, half], in_=part[:])
+        def add_on_vector(c, by_partner):
+            for lo in range(0, T, 2 * P):
+                half = slice(lo, lo + 2 * P)
+                total = ring.tile([P, 2 * P], F32, name="total")
+                nc.vector.tensor_tensor(total[:], by_token[c][:, half], by_partner[:, half], ALU.add)
+                nc.sync.dma_start(out=out[c * P : (c + 1) * P, half], in_=total[:])
 
-        by_partner.append(keep.tile([P, T], F32, name="by_partner0"))
-        scatter_dp(0, 0, C)
-        partner_product(1)
-        by_partner.append(keep.tile([P, T], F32, name="by_partner1", tag="grouped1", align_bytes=64))
-        scatter_dp(1, 0, C)
-        for c in range(2):
-            scatter_dp(c, C, SLOTS)
-            finish_on_tensor(c)
-        by_partner.extend([keep.tile([P, WIDE], F32, name="by_partner%d" % c) for c in (2, 3)])
-        scatter_dp(2, 0, SLOTS)
-        finish_on_tensor(2)
-        scatter_dp(3, 0, SLOTS)
-        finish_on_vector(3)
+        for c in range(CHUNKS):
+            by_partner = keep.tile([P, WIDE], F32, name="by_partner%d" % c)
+            nc.vector.tensor_copy(by_partner[:].indirect(offs2_sb[:]), dp_sb[:, c, :, :].rearrange("p e x -> p (e x)"))
+            if c < LAST:
+                add_on_tensor(c, by_partner)
+            else:
+                add_on_vector(c, by_partner)

@@ -102,7 +102,7 @@ def tile_moe_dub_relu_kernel(
 
         slot_w = [keep.tile([P, SLOTS], U32, name="slot_w%d" % s, align_bytes=64) for s in range(PASSES)]
         slot_s = keep.tile([P, SLOTS], U8, name="slot_s", align_bytes=64)
-        active = [keep.tile([P, C, PACK], BF16, name="active%d" % e) for e in range(E)]
+        active = [keep.tile([P, C, PACK], BF16, name="active", tag="active%d" % e) for e in range(E)]
         dh_w = keep.tile([P, SLOTS], U32, name="dh_w", align_bytes=64)
         dh_s = keep.tile([P, SLOTS], U8, name="dh_s", align_bytes=64)
 
@@ -203,7 +203,7 @@ def tile_moe_dub_relu_kernel(
         token_products(dx_second[:, 1:LAST, :], range(1, LAST), C, SLOTS)
 
         by_token = [keep.tile([P, T], F32, name="by_token%d" % c) for c in range(LAST)]
-        by_token.append(keep.tile([P, T], F32, name="by_token_last", tag="dh2", align_bytes=64))
+        by_token.append(keep.tile([P, T], F32, name="by_token_last", tag="active1"))
 
         def scatter_dx(c, lo, hi, values):
             nc.vector.tensor_copy(by_token[c][:].indirect(entries(offs_sb, lo, hi)), values)
@@ -226,7 +226,10 @@ def tile_moe_dub_relu_kernel(
         scatter_dx(LAST, C, SLOTS, dx_last[:, 0, :])
 
         dp_sb = keep.tile([P, CHUNKS, E, C], F32, name="dp_sb")
-        for c in range(CHUNKS):
+        for e in range(E):
+            for c in range(2):
+                products(dp_sb[:, c, e : e + 1, :], [(wp_w, wp_s, e * K + c * P, e * C, (e + 1) * C)])
+        for c in range(2, CHUNKS):
             products(dp_sb[:, c, :, :], [(wp_w, wp_s, e * K + c * P, e * C, (e + 1) * C) for e in range(E)])
 
         def add_on_tensor(c, by_partner):
@@ -254,7 +257,14 @@ def tile_moe_dub_relu_kernel(
                 nc.vector.tensor_tensor(total[:], by_token[c][:, half], by_partner[:, half], ALU.add)
                 nc.sync.dma_start(out=out[c * P : (c + 1) * P, half], in_=total[:])
 
-        for c in range(CHUNKS):
+        early = [keep.tile([P, T], F32, name="by_partner%d" % c) for c in range(2)]
+        for e in range(E):
+            for c in range(2):
+                picks = entries(offs2_sb, e * C, (e + 1) * C)
+                nc.vector.tensor_copy(early[c][:].indirect(picks), dp_sb[:, c, e, :])
+                if e == E - 1:
+                    add_on_tensor(c, early[c])
+        for c in range(2, CHUNKS):
             by_partner = keep.tile([P, WIDE], F32, name="by_partner%d" % c)
             nc.vector.tensor_copy(by_partner[:].indirect(offs2_sb[:]), dp_sb[:, c, :, :].rearrange("p e x -> p (e x)"))
             if c < LAST:

@@ -114,8 +114,12 @@ def tile_moe_dub_relu_kernel(
                 window = dy_w[:, s * T : (s + 1) * T].bitcast(U32)
                 nc.vector.tensor_copy(slot_w[s][:, lo:hi], window.indirect(entries(offs_sb, lo, hi)))
 
+        def by_fours(natural, grouped):
+            return grouped.rearrange("p (c i) t -> p c t i", i=4), natural.rearrange("p t (c i) -> p c t i", i=4)
+
         def relu_mask(e):
-            nc.vector.tensor_scalar(active[e][:], a_sb[e][:].rearrange("p t x -> p x t"), 0.0, None, ALU.is_gt)
+            dst, src = by_fours(a_sb[e][:], active[e][:])
+            nc.vector.tensor_scalar(dst, src, 0.0, None, ALU.is_gt)
 
         def hidden_gradient(j, dh):
             e = j // TILES_PER_EXPERT
@@ -133,7 +137,7 @@ def tile_moe_dub_relu_kernel(
                     stop=(s == PASSES - 1),
                 )
             gated = ring.tile([P, 2, P, 2], BF16, name="gated")
-            turned = psum.tile([P, 2, P], F32, name="turned", tag="turned")
+            turned = psum.tile([P, P, 2], F32, name="turned", tag="turned")
             for u in range(2):
                 nc.scalar.activation(
                     gated[:, u, :, :],
@@ -142,11 +146,11 @@ def tile_moe_dub_relu_kernel(
                     scale=gate_col[:, j : j + 1],
                 )
                 pairs = gated[:, u, :, :].rearrange("x p d -> x (p d)").bitcast(F32)
-                nc.tensor.transpose(turned[:, u, :], pairs, ident[:])
+                nc.tensor.transpose(turned[:, :, u], pairs, ident[:])
             nc.vector.tensor_tensor(
-                dh.rearrange("p (x u d) -> p x u d", u=2, d=2),
-                turned[:].bitcast(BF16).rearrange("p u (x d) -> p x u d", d=2),
-                active[e][:, own, :].rearrange("p x (u d) -> p x u d", d=2),
+                dh,
+                turned[:].rearrange("p x u -> p (x u)").bitcast(BF16),
+                active[e][:, own, :].rearrange("p x t -> p (x t)"),
                 ALU.mult,
             )
 
@@ -195,7 +199,7 @@ def tile_moe_dub_relu_kernel(
         def round_partner_weights(e):
             for c in range(CHUNKS):
                 kc = slice(c * P, (c + 1) * P)
-                nc.scalar.copy(wp_grouped[:, e, kc, :], wp_raw[e][:, :, kc].rearrange("p t k -> p k t"))
+                nc.scalar.copy(*by_fours(wp_raw[e][:, :, kc], wp_grouped[:, e, kc, :]))
 
         round_partner_weights(0)
         dx_second = keep.tile([P, LAST, C], F32, name="dx_second", tag="wp_raw0")

@@ -121,10 +121,9 @@ def tile_moe_dub_relu_kernel(
             dst, src = by_fours(a_sb[e][:], active[e][:])
             nc.vector.tensor_scalar(dst, src, 0.0, None, ALU.is_gt)
 
-        def hidden_gradient(j, dh):
+        def turn_sums(j, turned):
             e = j // TILES_PER_EXPERT
             cols = slice(j * P, (j + 1) * P)
-            own = slice(j * P - e * C, (j + 1) * P - e * C)
             sums = psum.tile([P, H], F32, name="sums", tag="sums")
             for s in range(PASSES):
                 nc.tensor.matmul_mx(
@@ -137,7 +136,6 @@ def tile_moe_dub_relu_kernel(
                     stop=(s == PASSES - 1),
                 )
             gated = ring.tile([P, 2, P, 2], BF16, name="gated")
-            turned = psum.tile([P, P, 2], F32, name="turned", tag="turned")
             for u in range(2):
                 nc.scalar.activation(
                     gated[:, u, :, :],
@@ -147,18 +145,20 @@ def tile_moe_dub_relu_kernel(
                 )
                 pairs = gated[:, u, :, :].rearrange("x p d -> x (p d)").bitcast(F32)
                 nc.tensor.transpose(turned[:, :, u], pairs, ident[:])
-            nc.vector.tensor_tensor(
-                dh,
-                turned[:].rearrange("p x u -> p (x u)").bitcast(BF16),
-                active[e][:, own, :].rearrange("p x t -> p (x t)"),
-                ALU.mult,
-            )
 
         def quantised_gradient(tiles, tag):
+            e = tiles[0] // TILES_PER_EXPERT
             cols = slice(tiles[0] * P, (tiles[-1] + 1) * P)
-            dh = keep.tile([P, len(tiles) * P * PACK], BF16, name="dh", tag=tag, align_bytes=64)
+            turned = psum.tile([P, len(tiles) * P, 2], F32, name="turned", tag="turned")
             for n, j in enumerate(tiles):
-                hidden_gradient(j, dh[:, n * P * PACK : (n + 1) * P * PACK])
+                turn_sums(j, turned[:, n * P : (n + 1) * P, :])
+            dh = keep.tile([P, len(tiles) * P * PACK], BF16, name="dh", tag=tag, align_bytes=64)
+            nc.vector.tensor_tensor(
+                dh[:],
+                turned[:].rearrange("p x u -> p (x u)").bitcast(BF16),
+                active[e][:, cols.start - e * C : cols.stop - e * C, :].rearrange("p x t -> p (x t)"),
+                ALU.mult,
+            )
             nc.vector.quantize_mx(out=dh_w[:, cols].bitcast(FP8X4), scales=dh_s[:, cols], in_=dh[:])
 
         def products(dst, parts):
@@ -212,9 +212,11 @@ def tile_moe_dub_relu_kernel(
         def scatter_dx(c, lo, hi, values):
             nc.vector.tensor_copy(by_token[c][:].indirect(entries(offs_sb, lo, hi)), values)
 
-        for lo in range(0, C, P):
-            for c in range(LAST):
-                scatter_dx(c, lo, lo + P, dx_first[:, c, lo : lo + P])
+        for c in range(2):
+            scatter_dx(c, 0, P, dx_first[:, c, 0:P])
+        scatter_dx(2, 0, C, dx_first[:, 2, :])
+        for c in range(2):
+            scatter_dx(c, P, C, dx_first[:, c, P:C])
         scatter_dx(LAST, 0, C, dx_first[:, LAST, :])
         for c in range(LAST):
             scatter_dx(c, C, SLOTS, dx_second[:, c, :])
@@ -231,9 +233,8 @@ def tile_moe_dub_relu_kernel(
 
         dp_sb = keep.tile([P, CHUNKS, E, C], F32, name="dp_sb")
         for e in range(E):
-            for c in range(2):
-                products(dp_sb[:, c, e : e + 1, :], [(wp_w, wp_s, e * K + c * P, e * C, (e + 1) * C)])
-        for c in range(2, CHUNKS):
+            products(dp_sb[:, 0, e : e + 1, :], [(wp_w, wp_s, e * K, e * C, (e + 1) * C)])
+        for c in range(1, CHUNKS):
             products(dp_sb[:, c, :, :], [(wp_w, wp_s, e * K + c * P, e * C, (e + 1) * C) for e in range(E)])
 
         def add_on_tensor(c, by_partner):
@@ -261,14 +262,7 @@ def tile_moe_dub_relu_kernel(
                 nc.vector.tensor_tensor(total[:], by_token[c][:, half], by_partner[:, half], ALU.add)
                 nc.sync.dma_start(out=out[c * P : (c + 1) * P, half], in_=total[:])
 
-        early = [keep.tile([P, T], F32, name="by_partner%d" % c) for c in range(2)]
-        for e in range(E):
-            for c in range(2):
-                picks = entries(offs2_sb, e * C, (e + 1) * C)
-                nc.vector.tensor_copy(early[c][:].indirect(picks), dp_sb[:, c, e, :])
-                if e == E - 1:
-                    add_on_tensor(c, early[c])
-        for c in range(2, CHUNKS):
+        for c in range(CHUNKS):
             by_partner = keep.tile([P, WIDE], F32, name="by_partner%d" % c)
             nc.vector.tensor_copy(by_partner[:].indirect(offs2_sb[:]), dp_sb[:, c, :, :].rearrange("p e x -> p (e x)"))
             if c < LAST:

@@ -27,6 +27,8 @@ TILES_PER_EXPERT = C // P
 CHUNKS = K // P
 LAST = CHUNKS - 1
 WIDE = 768
+WARM_UPS = 4
+WP_PIECES = ((0, 0, 3 * P), (0, 3 * P, K), (1, 0, K))
 
 
 def tile_moe_dub_relu_kernel(
@@ -45,14 +47,20 @@ def tile_moe_dub_relu_kernel(
         w2_w = [keep.tile([P, PASSES * H], I32, name="w2_w%d" % e, align_bytes=64) for e in range(E)]
         w2_s = keep.tile([P, H], U8, name="w2_s", align_bytes=64)
         w1_w = [keep.tile([P, K], I32, name="w1_w%d" % e, align_bytes=64) for e in range(E)]
-        w1_s = keep.tile([P, K], U8, name="w1_s", align_bytes=64)
+        w1_s_and_zeros = keep.tile([P, K + 2 * H * PACK], U8, name="w1_s_and_zeros", align_bytes=64)
+        w1_s = w1_s_and_zeros[:, 0:K]
+        zeros = w1_s_and_zeros[:, K:].bitcast(BF16)
         gate_rows = keep.tile([P, P], F32, name="gate_rows")
         a_sb = [keep.tile([P, PACK, C], F32, name="a_sb%d" % e) for e in range(E)]
-        wp_raw = [keep.tile([P, PACK, K], F32, name="wp_raw", tag="wp_raw%d" % e) for e in range(E)]
+        wp_raw = [
+            keep.tile([P, PACK, hi - lo], F32, name="wp_raw", tag="wp_raw%d" % n)
+            for n, (e, lo, hi) in enumerate(WP_PIECES)
+        ]
 
-        for plane in (dy_s, w2_s, w1_s):
-            nc.gpsimd.memset(plane[:].bitcast(I32), 0)
+        nc.gpsimd.memset(dy_s[:].bitcast(I32), 0)
         nc.gpsimd.memset(gate_rows[:], 0.0)
+        nc.gpsimd.memset(w2_s[:].bitcast(I32), 0)
+        nc.gpsimd.memset(w1_s_and_zeros[:].bitcast(I32), 0)
         ident = keep.tile([P, P], F32, name="ident")
         make_identity(nc, ident[:])
 
@@ -78,22 +86,22 @@ def tile_moe_dub_relu_kernel(
 
         nc.sync.dma_start(offs_sb[:], offs)
         load_scales(dy_s, dy_scales)
+        nc.sync.dma_start(out=gate_rows[0:TILES, :], in_=gate[0].rearrange("(j x) -> j x", x=P))
         nc.sync.dma_start(
             out=dy_w[:].rearrange("p (s t) -> p s t", s=PASSES),
             in_=dy_words.rearrange("s p t d -> p s (t d)").bitcast(I32),
         )
         load_w2(0)
-        nc.sync.dma_start(out=gate_rows[0:TILES, :], in_=gate[0].rearrange("(j x) -> j x", x=P))
         load_scales(w2_s, w2t_scales.rearrange("e s b i -> (e s) b i"))
         load_a(0)
         load_w1(0)
-        load_a(1)
         load_scales(w1_s, w1t_scales.rearrange("e s b k -> (e s) b k"))
         load_w2(1)
+        load_a(1)
         load_w1(1)
         nc.sync.dma_start(offs2_sb[:], offs2)
-        for e in range(E):
-            nc.sync.dma_start(out=wp_raw[e][:], in_=wpt[e].rearrange("(p t) k -> p t k", t=PACK))
+        for n, (e, lo, hi) in enumerate(WP_PIECES):
+            nc.sync.dma_start(out=wp_raw[n][:], in_=wpt[e, :, lo:hi].rearrange("(p t) k -> p t k", t=PACK))
 
         gate_turned = psum.tile([P, P], F32, name="gate_turned", tag="turned")
         nc.tensor.transpose(gate_turned[:], gate_rows[:], ident[:])
@@ -102,7 +110,7 @@ def tile_moe_dub_relu_kernel(
 
         slot_w = [keep.tile([P, SLOTS], U32, name="slot_w%d" % s, align_bytes=64) for s in range(PASSES)]
         slot_s = keep.tile([P, SLOTS], U8, name="slot_s", align_bytes=64)
-        active = [keep.tile([P, C, PACK], BF16, name="active", tag="active%d" % e) for e in range(E)]
+        active = []
         dh_w = keep.tile([P, SLOTS], U32, name="dh_w", align_bytes=64)
         dh_s = keep.tile([P, SLOTS], U8, name="dh_s", align_bytes=64)
 
@@ -118,8 +126,13 @@ def tile_moe_dub_relu_kernel(
             return grouped.rearrange("p (c i) t -> p c t i", i=4), natural.rearrange("p t (c i) -> p c t i", i=4)
 
         def relu_mask(e):
+            active.append(keep.tile([P, C, PACK], BF16, name="active", tag="active%d" % e, align_bytes=64))
             dst, src = by_fours(a_sb[e][:], active[e][:])
-            nc.vector.tensor_scalar(dst, src, 0.0, None, ALU.is_gt)
+            if e == 0:
+                nc.vector.tensor_scalar(dst, src, 0.0, None, ALU.is_gt)
+            else:
+                nc.scalar.activation(dst, src, ACT.Sign)
+                nc.scalar.activation(active[e][:], active[e][:], ACT.Relu)
 
         def turn_sums(j, turned):
             e = j // TILES_PER_EXPERT
@@ -180,6 +193,21 @@ def tile_moe_dub_relu_kernel(
             e = lo // C
             products(dst, [(w1_w[e], w1_s[4 * e : P, :], c * P, lo, hi) for c in chunks])
 
+        zero_w = keep.tile([P, H], U32, name="zero_w", align_bytes=64)
+        zero_s = keep.tile([P, H], U8, name="zero_s", align_bytes=64)
+        nc.vector.quantize_mx(out=zero_w[:].bitcast(FP8X4), scales=zero_s[:], in_=zeros)
+        unread = psum.tile([P, H], F32, name="unread", tag="product", bufs=4)
+        for n in range(WARM_UPS):
+            nc.tensor.matmul_mx(
+                out=unread[:],
+                lhsT=zero_w[:, 0:P].bitcast(FP8X4),
+                lhsT_scale=zero_s[:, 0:P],
+                rhs=zero_w[:].bitcast(FP8X4),
+                rhs_scale=zero_s[:],
+                start=True,
+                stop=True,
+            )
+
         nc.vector.tensor_copy(slot_s[:], dy_s[:].indirect(offs_sb[:]))
         gather_words(0, P)
         gather_words(P, C)
@@ -188,7 +216,7 @@ def tile_moe_dub_relu_kernel(
         quantised_gradient([0], "dh0")
         token_products(dx_first[:, 0:1, 0:P], [0], 0, P)
         token_products(dx_first[:, 1:CHUNKS, 0:P], range(1, CHUNKS), 0, P)
-        quantised_gradient([1], "dh1")
+        quantised_gradient([1], "active1")
         token_products(dx_first[:, :, P:C], range(CHUNKS), P, C)
         gather_words(C, SLOTS)
         relu_mask(1)
@@ -196,10 +224,10 @@ def tile_moe_dub_relu_kernel(
 
         wp_grouped = keep.tile([P, E, K, PACK], BF16, name="wp_grouped", align_bytes=64)
 
-        def round_partner_weights(e):
-            for c in range(CHUNKS):
-                kc = slice(c * P, (c + 1) * P)
-                nc.scalar.copy(*by_fours(wp_raw[e][:, :, kc], wp_grouped[:, e, kc, :]))
+        def round_partner_weights(n):
+            e, lo, hi = WP_PIECES[n]
+            for k in range(lo, hi, P):
+                nc.scalar.copy(*by_fours(wp_raw[n][:, :, k - lo : k - lo + P], wp_grouped[:, e, k : k + P, :]))
 
         round_partner_weights(0)
         dx_second = keep.tile([P, LAST, C], F32, name="dx_second", tag="wp_raw0")
@@ -207,7 +235,7 @@ def tile_moe_dub_relu_kernel(
         token_products(dx_second[:, 1:LAST, :], range(1, LAST), C, SLOTS)
 
         by_token = [keep.tile([P, T], F32, name="by_token%d" % c) for c in range(LAST)]
-        by_token.append(keep.tile([P, T], F32, name="by_token_last", tag="active1"))
+        by_token.append(keep.tile([P, T], F32, name="by_token_last", tag="active1", align_bytes=64))
 
         def scatter_dx(c, lo, hi, values):
             nc.vector.tensor_copy(by_token[c][:].indirect(entries(offs_sb, lo, hi)), values)
@@ -222,12 +250,13 @@ def tile_moe_dub_relu_kernel(
             scatter_dx(c, C, SLOTS, dx_second[:, c, :])
 
         round_partner_weights(1)
+        round_partner_weights(2)
         wp_w = keep.tile([P, E * K], U32, name="wp_w", align_bytes=64)
         wp_s = keep.tile([P, E * K], U8, name="wp_s", align_bytes=64)
         nc.vector.quantize_mx(
             out=wp_w[:].bitcast(FP8X4), scales=wp_s[:], in_=wp_grouped[:].rearrange("p e k t -> p (e k t)")
         )
-        dx_last = keep.tile([P, 1, C], F32, name="dx_last", tag="wp_raw1")
+        dx_last = keep.tile([P, 1, C], F32, name="dx_last", tag="wp_raw2")
         token_products(dx_last[:], [LAST], C, SLOTS)
         scatter_dx(LAST, C, SLOTS, dx_last[:, 0, :])
 

@@ -28,6 +28,7 @@ CHUNKS = K // P
 LAST = CHUNKS - 1
 WIDE = 768
 WARM_UPS = 4
+W2_PIECES = ((0, 0, H // 2), (0, H // 2, H), (1, 0, H))
 WP_PIECES = ((0, 0, 3 * P), (0, 3 * P, K), (1, 0, K))
 
 
@@ -44,12 +45,17 @@ def tile_moe_dub_relu_kernel(
         offs2_sb = keep.tile([P, SLOTS // PER_COLUMN], U16, name="offs2_sb")
         dy_w = keep.tile([P, PASSES * T], I32, name="dy_w")
         dy_s = keep.tile([P, WIDE], U8, name="dy_s")
-        w2_w = [keep.tile([P, PASSES * H], I32, name="w2_w%d" % e, align_bytes=64) for e in range(E)]
+        w2_w = [
+            keep.tile([P, PASSES * (hi - lo)], I32, name="w2_w%d" % n, align_bytes=64)
+            for n, (e, lo, hi) in enumerate(W2_PIECES)
+        ]
         w2_s = keep.tile([P, H], U8, name="w2_s", align_bytes=64)
         w1_w = [keep.tile([P, K], I32, name="w1_w%d" % e, align_bytes=64) for e in range(E)]
-        w1_s_and_zeros = keep.tile([P, K + 2 * H * PACK], U8, name="w1_s_and_zeros", align_bytes=64)
+        w1_s_and_zeros = keep.tile([P, K + H + H * PACK + 2 * H], U8, name="w1_s_and_zeros", align_bytes=64)
         w1_s = w1_s_and_zeros[:, 0:K]
-        zeros = w1_s_and_zeros[:, K:].bitcast(BF16)
+        zero_s = w1_s_and_zeros[:, K : K + H]
+        zero_w = w1_s_and_zeros[:, K + H : K + H + H * PACK].bitcast(U32)
+        zeros = w1_s_and_zeros[:, K + H + H * PACK :].bitcast(BF16)
         gate_rows = keep.tile([P, P], F32, name="gate_rows")
         a_sb = [keep.tile([P, PACK, C], F32, name="a_sb%d" % e) for e in range(E)]
         wp_raw = [
@@ -58,9 +64,9 @@ def tile_moe_dub_relu_kernel(
         ]
 
         nc.gpsimd.memset(dy_s[:].bitcast(I32), 0)
-        nc.gpsimd.memset(gate_rows[:], 0.0)
-        nc.gpsimd.memset(w2_s[:].bitcast(I32), 0)
-        nc.gpsimd.memset(w1_s_and_zeros[:].bitcast(I32), 0)
+        nc.vector.memset(gate_rows[:], 0.0)
+        nc.vector.memset(w2_s[:].bitcast(I32), 0)
+        nc.vector.memset(w1_s_and_zeros[:].bitcast(I32), 0)
         ident = keep.tile([P, P], F32, name="ident")
         make_identity(nc, ident[:])
 
@@ -72,10 +78,11 @@ def tile_moe_dub_relu_kernel(
                     in_=rows[:, 4 * q : 4 * q + 4, :].bitcast(I32),
                 )
 
-        def load_w2(e):
+        def load_w2(n):
+            e, lo, hi = W2_PIECES[n]
             nc.sync.dma_start(
-                out=w2_w[e][:].rearrange("p (s i) -> p s i", s=PASSES),
-                in_=w2t_words[e].rearrange("s p i d -> p s (i d)").bitcast(I32),
+                out=w2_w[n][:].rearrange("p (s i) -> p s i", s=PASSES),
+                in_=w2t_words[e, :, :, lo:hi, :].rearrange("s p i d -> p s (i d)").bitcast(I32),
             )
 
         def load_w1(e):
@@ -93,90 +100,98 @@ def tile_moe_dub_relu_kernel(
         )
         load_w2(0)
         load_scales(w2_s, w2t_scales.rearrange("e s b i -> (e s) b i"))
+        load_w2(1)
         load_a(0)
+        load_a(1)
         load_w1(0)
         load_scales(w1_s, w1t_scales.rearrange("e s b k -> (e s) b k"))
-        load_w2(1)
-        load_a(1)
+        load_w2(2)
         load_w1(1)
         nc.sync.dma_start(offs2_sb[:], offs2)
         for n, (e, lo, hi) in enumerate(WP_PIECES):
             nc.sync.dma_start(out=wp_raw[n][:], in_=wpt[e, :, lo:hi].rearrange("(p t) k -> p t k", t=PACK))
 
-        gate_turned = psum.tile([P, P], F32, name="gate_turned", tag="turned")
-        nc.tensor.transpose(gate_turned[:], gate_rows[:], ident[:])
-        gate_col = keep.tile([P, TILES], F32, name="gate_col")
-        nc.scalar.activation(gate_col[:], gate_turned[:, 0:TILES], ACT.Copy)
-
-        slot_w = [keep.tile([P, SLOTS], U32, name="slot_w%d" % s, align_bytes=64) for s in range(PASSES)]
+        slot_w = {}
         slot_s = keep.tile([P, SLOTS], U8, name="slot_s", align_bytes=64)
-        active = []
         dh_w = keep.tile([P, SLOTS], U32, name="dh_w", align_bytes=64)
         dh_s = keep.tile([P, SLOTS], U8, name="dh_s", align_bytes=64)
 
         def entries(offsets, lo, hi):
             return offsets[:, lo // PER_COLUMN : hi // PER_COLUMN]
 
-        def gather_words(lo, hi):
-            for s in range(PASSES):
-                window = dy_w[:, s * T : (s + 1) * T].bitcast(U32)
-                nc.vector.tensor_copy(slot_w[s][:, lo:hi], window.indirect(entries(offs_sb, lo, hi)))
+        def gather_words(tiles, s, tag):
+            lo, hi = tiles[0] * P, (tiles[-1] + 1) * P
+            words = keep.tile([P, hi - lo], U32, name="slot_w", tag=tag, align_bytes=64)
+            window = dy_w[:, s * T : (s + 1) * T].bitcast(U32)
+            nc.vector.tensor_copy(words[:], window.indirect(entries(offs_sb, lo, hi)))
+            for n, j in enumerate(tiles):
+                slot_w[(j, s)] = words[:, n * P : (n + 1) * P]
 
         def by_fours(natural, grouped):
             return grouped.rearrange("p (c i) t -> p c t i", i=4), natural.rearrange("p t (c i) -> p c t i", i=4)
 
-        def relu_mask(e):
-            active.append(keep.tile([P, C, PACK], BF16, name="active", tag="active%d" % e, align_bytes=64))
-            dst, src = by_fours(a_sb[e][:], active[e][:])
-            if e == 0:
-                nc.vector.tensor_scalar(dst, src, 0.0, None, ALU.is_gt)
-            else:
-                nc.scalar.activation(dst, src, ACT.Sign)
-                nc.scalar.activation(active[e][:], active[e][:], ACT.Relu)
+        def mask_on_vector(j, tag):
+            active = keep.tile([P, P, PACK], BF16, name="active", tag=tag, align_bytes=64)
+            dst, src = by_fours(a_sb[0][:, :, j * P : (j + 1) * P], active[:])
+            nc.vector.tensor_scalar(dst, src, 0.0, None, ALU.is_gt)
+            return active
+
+        def mask_on_scalar():
+            signs = keep.tile([P, C, PACK], BF16, name="signs", align_bytes=64)
+            nc.scalar.activation(*by_fours(a_sb[1][:], signs[:]), ACT.Sign)
+            active = keep.tile([P, C, PACK], BF16, name="active", tag="gated3", align_bytes=64)
+            nc.scalar.activation(active[:], signs[:], ACT.Relu)
+            return active
+
+        gate_col = keep.tile([P, TILES], F32, name="gate_col")
 
         def turn_sums(j, turned):
-            e = j // TILES_PER_EXPERT
             cols = slice(j * P, (j + 1) * P)
-            sums = psum.tile([P, H], F32, name="sums", tag="sums")
-            for s in range(PASSES):
-                nc.tensor.matmul_mx(
-                    out=sums[:],
-                    lhsT=slot_w[s][:, cols].bitcast(FP8X4),
-                    lhsT_scale=slot_s[4 * s : P, cols],
-                    rhs=w2_w[e][:, s * H : (s + 1) * H].bitcast(FP8X4),
-                    rhs_scale=w2_s[4 * (PASSES * e + s) : P, :],
-                    start=(s == 0),
-                    stop=(s == PASSES - 1),
-                )
-            gated = ring.tile([P, 2, P, 2], BF16, name="gated")
-            for u in range(2):
+            gated = keep.tile([P, 2, P, 2], BF16, name="gated", tag="gated%d" % j, align_bytes=64)
+            for n, (e, lo, hi) in enumerate(W2_PIECES):
+                if e != j // TILES_PER_EXPERT:
+                    continue
+                sums = psum.tile([P, hi - lo], F32, name="sums", tag="sums", bufs=3)
+                for s in range(PASSES):
+                    nc.tensor.matmul_mx(
+                        out=sums[:],
+                        lhsT=slot_w[(j, s)].bitcast(FP8X4),
+                        lhsT_scale=slot_s[4 * s : P, cols],
+                        rhs=w2_w[n][:, s * (hi - lo) : (s + 1) * (hi - lo)].bitcast(FP8X4),
+                        rhs_scale=w2_s[4 * (PASSES * e + s) : P, lo:hi],
+                        start=(s == 0),
+                        stop=(s == PASSES - 1),
+                    )
                 nc.scalar.activation(
-                    gated[:, u, :, :],
-                    sums[:].rearrange("x (p u d) -> x u p d", u=2, d=2)[:, u, :, :],
+                    gated[:, :, lo // PACK : hi // PACK, :],
+                    sums[:].rearrange("x (p u d) -> x u p d", u=2, d=2),
                     ACT.Copy,
                     scale=gate_col[:, j : j + 1],
                 )
+            for u in range(2):
                 pairs = gated[:, u, :, :].rearrange("x p d -> x (p d)").bitcast(F32)
                 nc.tensor.transpose(turned[:, :, u], pairs, ident[:])
 
-        def quantised_gradient(tiles, tag):
-            e = tiles[0] // TILES_PER_EXPERT
-            cols = slice(tiles[0] * P, (tiles[-1] + 1) * P)
+        def turned_sums(tiles):
             turned = psum.tile([P, len(tiles) * P, 2], F32, name="turned", tag="turned")
             for n, j in enumerate(tiles):
                 turn_sums(j, turned[:, n * P : (n + 1) * P, :])
+            return turned
+
+        def quantised_gradient(tiles, turned, active, tag):
+            cols = slice(tiles[0] * P, (tiles[-1] + 1) * P)
             dh = keep.tile([P, len(tiles) * P * PACK], BF16, name="dh", tag=tag, align_bytes=64)
             nc.vector.tensor_tensor(
                 dh[:],
                 turned[:].rearrange("p x u -> p (x u)").bitcast(BF16),
-                active[e][:, cols.start - e * C : cols.stop - e * C, :].rearrange("p x t -> p (x t)"),
+                active[:].rearrange("p x t -> p (x t)"),
                 ALU.mult,
             )
             nc.vector.quantize_mx(out=dh_w[:, cols].bitcast(FP8X4), scales=dh_s[:, cols], in_=dh[:])
 
         def products(dst, parts):
             width = parts[0][4] - parts[0][3]
-            acc = psum.tile([P, len(parts), width], F32, name="acc", tag="product", bufs=4)
+            acc = psum.tile([P, len(parts), width], F32, name="acc", tag="product", bufs=3)
             for b, (weights, plane, column, lo, hi) in enumerate(parts):
                 nc.tensor.matmul_mx(
                     out=acc[:, b, :],
@@ -193,34 +208,44 @@ def tile_moe_dub_relu_kernel(
             e = lo // C
             products(dst, [(w1_w[e], w1_s[4 * e : P, :], c * P, lo, hi) for c in chunks])
 
-        zero_w = keep.tile([P, H], U32, name="zero_w", align_bytes=64)
-        zero_s = keep.tile([P, H], U8, name="zero_s", align_bytes=64)
-        nc.vector.quantize_mx(out=zero_w[:].bitcast(FP8X4), scales=zero_s[:], in_=zeros)
-        unread = psum.tile([P, H], F32, name="unread", tag="product", bufs=4)
+        nc.vector.quantize_mx(out=zero_w[:, 0:P].bitcast(FP8X4), scales=zero_s[:, 0:P], in_=zeros)
+        unread = psum.tile([P, H], F32, name="unread", tag="product", bufs=3)
         for n in range(WARM_UPS):
             nc.tensor.matmul_mx(
                 out=unread[:],
                 lhsT=zero_w[:, 0:P].bitcast(FP8X4),
                 lhsT_scale=zero_s[:, 0:P],
-                rhs=zero_w[:].bitcast(FP8X4),
-                rhs_scale=zero_s[:],
+                rhs=zero_w.bitcast(FP8X4),
+                rhs_scale=zero_s,
                 start=True,
                 stop=True,
             )
 
+        nc.tensor.transpose(unread[:, 0:P], gate_rows[:], ident[:])
+        nc.scalar.activation(gate_col[:], unread[:, 0:TILES], ACT.Copy)
+
         nc.vector.tensor_copy(slot_s[:], dy_s[:].indirect(offs_sb[:]))
-        gather_words(0, P)
-        gather_words(P, C)
-        relu_mask(0)
+        for j in range(TILES_PER_EXPERT):
+            for s in range(PASSES):
+                gather_words([j], s, "slot_w%d%d" % (j, s))
+        gather_words([2, 3], 0, "slot_w20")
         dx_first = keep.tile([P, CHUNKS, C], F32, name="dx_first")
-        quantised_gradient([0], "dh0")
-        token_products(dx_first[:, 0:1, 0:P], [0], 0, P)
+        turned_first = [turned_sums([j]) for j in range(TILES_PER_EXPERT)]
+        quantised_gradient([0], turned_first[0], mask_on_vector(0, "active0"), "dh0")
+        quantised_gradient([1], turned_first[1], mask_on_vector(1, "gated0"), "dh1")
+        gather_words([2, 3], 1, "gated1")
+        dx_head = keep.tile([P, 1, P], F32, name="dx_head")
+        token_products(dx_head[:], [0], 0, P)
         token_products(dx_first[:, 1:CHUNKS, 0:P], range(1, CHUNKS), 0, P)
-        quantised_gradient([1], "active1")
         token_products(dx_first[:, :, P:C], range(CHUNKS), P, C)
-        gather_words(C, SLOTS)
-        relu_mask(1)
-        quantised_gradient([2, 3], "dh2")
+        by_token = [keep.tile([P, T], F32, name="by_token%d" % c) for c in range(LAST)]
+
+        def scatter_dx(c, lo, hi, values):
+            nc.vector.tensor_copy(by_token[c][:].indirect(entries(offs_sb, lo, hi)), values)
+
+        scatter_dx(0, 0, P, dx_head[:, 0, :])
+        turned_second = turned_sums([2, 3])
+        quantised_gradient([2, 3], turned_second, mask_on_scalar(), "dh2")
 
         wp_grouped = keep.tile([P, E, K, PACK], BF16, name="wp_grouped", align_bytes=64)
 
@@ -234,14 +259,9 @@ def tile_moe_dub_relu_kernel(
         token_products(dx_second[:, 0:1, :], [0], C, SLOTS)
         token_products(dx_second[:, 1:LAST, :], range(1, LAST), C, SLOTS)
 
-        by_token = [keep.tile([P, T], F32, name="by_token%d" % c) for c in range(LAST)]
-        by_token.append(keep.tile([P, T], F32, name="by_token_last", tag="active1", align_bytes=64))
+        by_token.append(keep.tile([P, T], F32, name="by_token_last", tag="gated3", align_bytes=64))
 
-        def scatter_dx(c, lo, hi, values):
-            nc.vector.tensor_copy(by_token[c][:].indirect(entries(offs_sb, lo, hi)), values)
-
-        for c in range(2):
-            scatter_dx(c, 0, P, dx_first[:, c, 0:P])
+        scatter_dx(1, 0, P, dx_first[:, 1, 0:P])
         scatter_dx(2, 0, C, dx_first[:, 2, :])
         for c in range(2):
             scatter_dx(c, P, C, dx_first[:, c, P:C])
@@ -268,7 +288,7 @@ def tile_moe_dub_relu_kernel(
 
         def add_on_tensor(c, by_partner):
             for lo in range(0, T, 2 * P):
-                both = psum.tile([P, 2, P], F32, name="both", tag="sums")
+                both = psum.tile([P, 2, P], F32, name="both", tag="sums", bufs=3)
                 for b in range(2):
                     block = slice(lo + b * P, lo + (b + 1) * P)
                     for first, source in ((True, by_token[c]), (False, by_partner)):

@@ -28,8 +28,7 @@ CHUNKS = K // P
 LAST = CHUNKS - 1
 WIDE = 768
 WARM_UPS = 4
-W2_PIECES = ((0, 0, H // 2), (0, H // 2, H), (1, 0, H))
-WP_PIECES = ((0, 0, 3 * P), (0, 3 * P, K), (1, 0, K))
+W2_PIECES = ((0, 0, H), (1, 0, H))
 
 
 def tile_moe_dub_relu_kernel(
@@ -51,24 +50,21 @@ def tile_moe_dub_relu_kernel(
         ]
         w2_s = keep.tile([P, H], U8, name="w2_s", align_bytes=64)
         w1_w = [keep.tile([P, K], I32, name="w1_w%d" % e, align_bytes=64) for e in range(E)]
-        w1_s_and_zeros = keep.tile([P, K + H + H * PACK + 2 * H], U8, name="w1_s_and_zeros", align_bytes=64)
+        w1_s_and_zeros = keep.tile([P, K + H + H * PACK + 2 * P], U8, name="w1_s_and_zeros", align_bytes=64)
         w1_s = w1_s_and_zeros[:, 0:K]
         zero_s = w1_s_and_zeros[:, K : K + H]
         zero_w = w1_s_and_zeros[:, K + H : K + H + H * PACK].bitcast(U32)
         zeros = w1_s_and_zeros[:, K + H + H * PACK :].bitcast(BF16)
         gate_rows = keep.tile([P, P], F32, name="gate_rows")
         a_sb = [keep.tile([P, PACK, C], F32, name="a_sb%d" % e) for e in range(E)]
-        wp_raw = [
-            keep.tile([P, PACK, hi - lo], F32, name="wp_raw", tag="wp_raw%d" % n)
-            for n, (e, lo, hi) in enumerate(WP_PIECES)
-        ]
+        wp_raw = [keep.tile([P, PACK, K], F32, name="wp_raw", tag="wp_raw%d" % e) for e in range(E)]
 
         nc.gpsimd.memset(dy_s[:].bitcast(I32), 0)
-        nc.vector.memset(gate_rows[:], 0.0)
-        nc.vector.memset(w2_s[:].bitcast(I32), 0)
-        nc.vector.memset(w1_s_and_zeros[:].bitcast(I32), 0)
+        nc.gpsimd.memset(gate_rows[:], 0.0)
+        nc.gpsimd.memset(w2_s[:].bitcast(I32), 0)
         ident = keep.tile([P, P], F32, name="ident")
         make_identity(nc, ident[:])
+        nc.gpsimd.memset(w1_s_and_zeros[:].bitcast(I32), 0)
 
         def load_scales(plane, rows):
             passes, width = rows.shape[0], rows.shape[2]
@@ -88,6 +84,9 @@ def tile_moe_dub_relu_kernel(
         def load_w1(e):
             nc.sync.dma_start(out=w1_w[e][:], in_=w1t_words[e, 0].rearrange("p k d -> p (k d)").bitcast(I32))
 
+        def load_wp(e):
+            nc.sync.dma_start(out=wp_raw[e][:], in_=wpt[e].rearrange("(p t) k -> p t k", t=PACK))
+
         def load_a(e):
             nc.sync.dma_start(out=a_sb[e][:], in_=a[:, e * C : (e + 1) * C].rearrange("(p t) j -> p t j", t=PACK))
 
@@ -100,16 +99,15 @@ def tile_moe_dub_relu_kernel(
         )
         load_w2(0)
         load_scales(w2_s, w2t_scales.rearrange("e s b i -> (e s) b i"))
-        load_w2(1)
         load_a(0)
-        load_a(1)
         load_w1(0)
         load_scales(w1_s, w1t_scales.rearrange("e s b k -> (e s) b k"))
-        load_w2(2)
-        load_w1(1)
+        load_wp(0)
+        load_w2(1)
         nc.sync.dma_start(offs2_sb[:], offs2)
-        for n, (e, lo, hi) in enumerate(WP_PIECES):
-            nc.sync.dma_start(out=wp_raw[n][:], in_=wpt[e, :, lo:hi].rearrange("(p t) k -> p t k", t=PACK))
+        load_a(1)
+        load_w1(1)
+        load_wp(1)
 
         slot_w = {}
         slot_s = keep.tile([P, SLOTS], U8, name="slot_s", align_bytes=64)
@@ -139,7 +137,7 @@ def tile_moe_dub_relu_kernel(
         def mask_on_scalar():
             signs = keep.tile([P, C, PACK], BF16, name="signs", align_bytes=64)
             nc.scalar.activation(*by_fours(a_sb[1][:], signs[:]), ACT.Sign)
-            active = keep.tile([P, C, PACK], BF16, name="active", tag="gated3", align_bytes=64)
+            active = keep.tile([P, C, PACK], BF16, name="active", tag="active1", align_bytes=64)
             nc.scalar.activation(active[:], signs[:], ACT.Relu)
             return active
 
@@ -151,7 +149,7 @@ def tile_moe_dub_relu_kernel(
             for n, (e, lo, hi) in enumerate(W2_PIECES):
                 if e != j // TILES_PER_EXPERT:
                     continue
-                sums = psum.tile([P, hi - lo], F32, name="sums", tag="sums", bufs=3)
+                sums = psum.tile([P, hi - lo], F32, name="sums", tag="sums")
                 for s in range(PASSES):
                     nc.tensor.matmul_mx(
                         out=sums[:],
@@ -162,12 +160,13 @@ def tile_moe_dub_relu_kernel(
                         start=(s == 0),
                         stop=(s == PASSES - 1),
                     )
-                nc.scalar.activation(
-                    gated[:, :, lo // PACK : hi // PACK, :],
-                    sums[:].rearrange("x (p u d) -> x u p d", u=2, d=2),
-                    ACT.Copy,
-                    scale=gate_col[:, j : j + 1],
-                )
+                for us in ((slice(0, 1), slice(1, 2)) if e == 0 else (slice(0, 2),)):
+                    nc.scalar.activation(
+                        gated[:, us, lo // PACK : hi // PACK, :],
+                        sums[:].rearrange("x (p u d) -> x u p d", u=2, d=2)[:, us, :, :],
+                        ACT.Copy,
+                        scale=gate_col[:, j : j + 1],
+                    )
             for u in range(2):
                 pairs = gated[:, u, :, :].rearrange("x p d -> x (p d)").bitcast(F32)
                 nc.tensor.transpose(turned[:, :, u], pairs, ident[:])
@@ -191,7 +190,7 @@ def tile_moe_dub_relu_kernel(
 
         def products(dst, parts):
             width = parts[0][4] - parts[0][3]
-            acc = psum.tile([P, len(parts), width], F32, name="acc", tag="product", bufs=3)
+            acc = psum.tile([P, len(parts), width], F32, name="acc", tag="product", bufs=4)
             for b, (weights, plane, column, lo, hi) in enumerate(parts):
                 nc.tensor.matmul_mx(
                     out=acc[:, b, :],
@@ -204,12 +203,8 @@ def tile_moe_dub_relu_kernel(
                 )
             nc.scalar.copy(dst, acc[:])
 
-        def token_products(dst, chunks, lo, hi):
-            e = lo // C
-            products(dst, [(w1_w[e], w1_s[4 * e : P, :], c * P, lo, hi) for c in chunks])
-
-        nc.vector.quantize_mx(out=zero_w[:, 0:P].bitcast(FP8X4), scales=zero_s[:, 0:P], in_=zeros)
-        unread = psum.tile([P, H], F32, name="unread", tag="product", bufs=3)
+        nc.vector.quantize_mx(out=zero_w[:, 0 : P // PACK].bitcast(FP8X4), scales=zero_s[:, 0 : P // PACK], in_=zeros)
+        unread = psum.tile([P, H], F32, name="unread", tag="product", bufs=4)
         for n in range(WARM_UPS):
             nc.tensor.matmul_mx(
                 out=unread[:],
@@ -228,67 +223,80 @@ def tile_moe_dub_relu_kernel(
         for j in range(TILES_PER_EXPERT):
             for s in range(PASSES):
                 gather_words([j], s, "slot_w%d%d" % (j, s))
-        gather_words([2, 3], 0, "slot_w20")
-        dx_first = keep.tile([P, CHUNKS, C], F32, name="dx_first")
+        for s in range(PASSES):
+            gather_words([2, 3], s, "slot_w2%d" % s)
         turned_first = [turned_sums([j]) for j in range(TILES_PER_EXPERT)]
         quantised_gradient([0], turned_first[0], mask_on_vector(0, "active0"), "dh0")
         quantised_gradient([1], turned_first[1], mask_on_vector(1, "gated0"), "dh1")
-        gather_words([2, 3], 1, "gated1")
-        dx_head = keep.tile([P, 1, P], F32, name="dx_head")
-        token_products(dx_head[:], [0], 0, P)
-        token_products(dx_first[:, 1:CHUNKS, 0:P], range(1, CHUNKS), 0, P)
-        token_products(dx_first[:, :, P:C], range(CHUNKS), P, C)
-        by_token = [keep.tile([P, T], F32, name="by_token%d" % c) for c in range(LAST)]
+
+        by_token = [keep.tile([P, T], F32, name="by_token%d" % c) for c in range(CHUNKS)]
 
         def scatter_dx(c, lo, hi, values):
             nc.vector.tensor_copy(by_token[c][:].indirect(entries(offs_sb, lo, hi)), values)
 
-        scatter_dx(0, 0, P, dx_head[:, 0, :])
+        def token_part(c, lo, hi):
+            e = lo // C
+            return (w1_w[e], w1_s[4 * e : P, :], c * P, lo, hi)
+
+        wp_w = [keep.tile([P, K], U32, name="wp_w%d" % e, align_bytes=64) for e in range(E)]
+        wp_s = [keep.tile([P, K], U8, name="wp_s%d" % e, align_bytes=64) for e in range(E)]
+
+        def partner_part(c, e):
+            return (wp_w[e], wp_s[e], c * P, e * C, (e + 1) * C)
+
+        def quantised_partner_weights(e):
+            grouped = keep.tile([P, K, PACK], BF16, name="grouped%d" % e, align_bytes=64)
+            for k in range(0, K, P):
+                nc.scalar.copy(*by_fours(wp_raw[e][:, :, k : k + P], grouped[:, k : k + P, :]))
+            nc.vector.quantize_mx(
+                out=wp_w[e][:].bitcast(FP8X4), scales=wp_s[e][:], in_=grouped[:].rearrange("p k t -> p (k t)")
+            )
+
+        dx_early = keep.tile([P, 5, P], F32, name="dx_early")
+        products(dx_early[:, 0:1, :], [token_part(0, 0, P)])
+        products(dx_early[:, 1:3, :], [token_part(c, 0, P) for c in (1, 2)])
+        products(dx_early[:, 3:5, :], [token_part(c, P, C) for c in (0, 1)])
+        for c in range(3):
+            scatter_dx(c, 0, P, dx_early[:, c, :])
+        for c in range(2):
+            scatter_dx(c, P, C, dx_early[:, 3 + c, :])
+
+        quantised_partner_weights(0)
+        dx_late = keep.tile([P, 3, P], F32, name="dx_late", tag="wp_raw0")
+        products(dx_late[:], [token_part(2, P, C), token_part(LAST, 0, P), token_part(LAST, P, C)])
+        scatter_dx(2, P, C, dx_late[:, 0, :])
+        scatter_dx(LAST, 0, C, dx_late[:, 1:3, :].rearrange("p b x -> p (b x)"))
+
+        dp_first = keep.tile([P, CHUNKS, C], F32, name="dp_first")
+        products(dp_first[:, 0:1, :], [partner_part(0, 0)])
+        products(dp_first[:, 1:3, :], [partner_part(c, 0) for c in (1, 2)])
+        products(dp_first[:, LAST:CHUNKS, :], [partner_part(LAST, 0)])
+        by_partner = []
+
+        def scatter_dp(c, e, values):
+            nc.vector.tensor_copy(by_partner[c][:].indirect(entries(offs2_sb, e * C, (e + 1) * C)), values)
+
+        for c in range(2):
+            by_partner.append(keep.tile([P, T], F32, name="by_partner%d" % c))
+            scatter_dp(c, 0, dp_first[:, c, :])
+
         turned_second = turned_sums([2, 3])
         quantised_gradient([2, 3], turned_second, mask_on_scalar(), "dh2")
+        by_partner.append(keep.tile([P, T], F32, name="by_partner2", tag="active1", align_bytes=64))
+        scatter_dp(2, 0, dp_first[:, 2, :])
+        quantised_partner_weights(1)
+        by_partner.append(keep.tile([P, T], F32, name="by_partner3", tag="wp_raw1"))
+        scatter_dp(LAST, 0, dp_first[:, LAST, :])
 
-        wp_grouped = keep.tile([P, E, K, PACK], BF16, name="wp_grouped", align_bytes=64)
-
-        def round_partner_weights(n):
-            e, lo, hi = WP_PIECES[n]
-            for k in range(lo, hi, P):
-                nc.scalar.copy(*by_fours(wp_raw[n][:, :, k - lo : k - lo + P], wp_grouped[:, e, k : k + P, :]))
-
-        round_partner_weights(0)
-        dx_second = keep.tile([P, LAST, C], F32, name="dx_second", tag="wp_raw0")
-        token_products(dx_second[:, 0:1, :], [0], C, SLOTS)
-        token_products(dx_second[:, 1:LAST, :], range(1, LAST), C, SLOTS)
-
-        by_token.append(keep.tile([P, T], F32, name="by_token_last", tag="gated3", align_bytes=64))
-
-        scatter_dx(1, 0, P, dx_first[:, 1, 0:P])
-        scatter_dx(2, 0, C, dx_first[:, 2, :])
-        for c in range(2):
-            scatter_dx(c, P, C, dx_first[:, c, P:C])
-        scatter_dx(LAST, 0, C, dx_first[:, LAST, :])
-        for c in range(LAST):
-            scatter_dx(c, C, SLOTS, dx_second[:, c, :])
-
-        round_partner_weights(1)
-        round_partner_weights(2)
-        wp_w = keep.tile([P, E * K], U32, name="wp_w", align_bytes=64)
-        wp_s = keep.tile([P, E * K], U8, name="wp_s", align_bytes=64)
-        nc.vector.quantize_mx(
-            out=wp_w[:].bitcast(FP8X4), scales=wp_s[:], in_=wp_grouped[:].rearrange("p e k t -> p (e k t)")
-        )
-        dx_last = keep.tile([P, 1, C], F32, name="dx_last", tag="wp_raw2")
-        token_products(dx_last[:], [LAST], C, SLOTS)
-        scatter_dx(LAST, C, SLOTS, dx_last[:, 0, :])
-
-        dp_sb = keep.tile([P, CHUNKS, E, C], F32, name="dp_sb")
-        for e in range(E):
-            products(dp_sb[:, 0, e : e + 1, :], [(wp_w, wp_s, e * K, e * C, (e + 1) * C)])
+        second = keep.tile([P, CHUNKS, 2, C], F32, name="second")
+        products(second[:, 0, 0:1, :], [token_part(0, C, SLOTS)])
+        products(second[:, 0, 1:2, :], [partner_part(0, 1)])
         for c in range(1, CHUNKS):
-            products(dp_sb[:, c, :, :], [(wp_w, wp_s, e * K + c * P, e * C, (e + 1) * C) for e in range(E)])
+            products(second[:, c, :, :], [token_part(c, C, SLOTS), partner_part(c, 1)])
 
         def add_on_tensor(c, by_partner):
             for lo in range(0, T, 2 * P):
-                both = psum.tile([P, 2, P], F32, name="both", tag="sums", bufs=3)
+                both = psum.tile([P, 2, P], F32, name="both", tag="sums")
                 for b in range(2):
                     block = slice(lo + b * P, lo + (b + 1) * P)
                     for first, source in ((True, by_token[c]), (False, by_partner)):
@@ -312,9 +320,9 @@ def tile_moe_dub_relu_kernel(
                 nc.sync.dma_start(out=out[c * P : (c + 1) * P, half], in_=total[:])
 
         for c in range(CHUNKS):
-            by_partner = keep.tile([P, WIDE], F32, name="by_partner%d" % c)
-            nc.vector.tensor_copy(by_partner[:].indirect(offs2_sb[:]), dp_sb[:, c, :, :].rearrange("p e x -> p (e x)"))
+            scatter_dx(c, C, SLOTS, second[:, c, 0, :])
+            scatter_dp(c, 1, second[:, c, 1, :])
             if c < LAST:
-                add_on_tensor(c, by_partner)
+                add_on_tensor(c, by_partner[c])
             else:
-                add_on_vector(c, by_partner)
+                add_on_vector(c, by_partner[c])

@@ -180,12 +180,13 @@ def tile_moe_dub_relu_kernel(
         def quantised_gradient(tiles, turned, active, tag):
             cols = slice(tiles[0] * P, (tiles[-1] + 1) * P)
             dh = keep.tile([P, len(tiles) * P * PACK], BF16, name="dh", tag=tag, align_bytes=64)
-            nc.vector.tensor_tensor(
-                dh[:],
-                turned[:].rearrange("p x u -> p (x u)").bitcast(BF16),
-                active[:].rearrange("p x t -> p (x t)"),
-                ALU.mult,
-            )
+            pairs = turned[:].rearrange("p x u -> p (x u)")
+            engine = nc.vector
+            if len(tiles) > 1:
+                unmasked = keep.tile([P, len(tiles) * P * 2], F32, name="unmasked")
+                nc.scalar.copy(unmasked[:], pairs)
+                pairs, engine = unmasked[:], nc.gpsimd
+            engine.tensor_tensor(dh[:], pairs.bitcast(BF16), active[:].rearrange("p x t -> p (x t)"), ALU.mult)
             nc.vector.quantize_mx(out=dh_w[:, cols].bitcast(FP8X4), scales=dh_s[:, cols], in_=dh[:])
 
         def products(dst, parts):
@@ -270,7 +271,6 @@ def tile_moe_dub_relu_kernel(
         dp_first = keep.tile([P, CHUNKS, C], F32, name="dp_first")
         products(dp_first[:, 0:1, :], [partner_part(0, 0)])
         products(dp_first[:, 1:3, :], [partner_part(c, 0) for c in (1, 2)])
-        products(dp_first[:, LAST:CHUNKS, :], [partner_part(LAST, 0)])
         by_partner = []
 
         def scatter_dp(c, e, values):
@@ -282,8 +282,9 @@ def tile_moe_dub_relu_kernel(
 
         turned_second = turned_sums([2, 3])
         quantised_gradient([2, 3], turned_second, mask_on_scalar(), "dh2")
-        by_partner.append(keep.tile([P, T], F32, name="by_partner2", tag="active1", align_bytes=64))
+        by_partner.append(keep.tile([P, T], F32, name="by_partner2"))
         scatter_dp(2, 0, dp_first[:, 2, :])
+        products(dp_first[:, LAST:CHUNKS, :], [partner_part(LAST, 0)])
         quantised_partner_weights(1)
         by_partner.append(keep.tile([P, T], F32, name="by_partner3", tag="wp_raw1"))
         scatter_dp(LAST, 0, dp_first[:, LAST, :])

@@ -268,6 +268,7 @@ def tile_moe_dub_relu_kernel(
         scatter_dx(2, P, C, dx_late[:, 0, :])
         scatter_dx(LAST, 0, C, dx_late[:, 1:3, :].rearrange("p b x -> p (b x)"))
 
+        turned_second = turned_sums([2, 3])
         dp_first = keep.tile([P, CHUNKS, C], F32, name="dp_first")
         products(dp_first[:, 0:1, :], [partner_part(0, 0)])
         products(dp_first[:, 1:3, :], [partner_part(c, 0) for c in (1, 2)])
@@ -280,7 +281,6 @@ def tile_moe_dub_relu_kernel(
             by_partner.append(keep.tile([P, T], F32, name="by_partner%d" % c))
             scatter_dp(c, 0, dp_first[:, c, :])
 
-        turned_second = turned_sums([2, 3])
         quantised_gradient([2, 3], turned_second, mask_on_scalar(), "dh2")
         by_partner.append(keep.tile([P, T], F32, name="by_partner2"))
         scatter_dp(2, 0, dp_first[:, 2, :])

@@ -295,23 +295,10 @@ def tile_moe_dub_relu_kernel(
         for c in range(1, CHUNKS):
             products(second[:, c, :, :], [token_part(c, C, SLOTS), partner_part(c, 1)])
 
-        def add_on_tensor(c, by_partner):
-            for lo in range(0, T, 2 * P):
-                both = psum.tile([P, 2, P], F32, name="both", tag="sums")
-                for b in range(2):
-                    block = slice(lo + b * P, lo + (b + 1) * P)
-                    for first, source in ((True, by_token[c]), (False, by_partner)):
-                        nc.tensor.matmul(
-                            both[:, b, :], source[:, block], ident[:], start=first, stop=not first, is_transpose=True
-                        )
-                both_sb = ring.tile([P, 2, P], F32, name="both_sb")
-                nc.scalar.copy(both_sb[:], both[:])
-                back = psum.tile([P, 2, P], F32, name="back", tag="turned")
-                for b in range(2):
-                    nc.tensor.transpose(back[:, b, :], both_sb[:, b, :], ident[:])
-                total = keep.tile([P, 2 * P], F32, name="total%d_%d" % (c, lo))
-                nc.scalar.copy(total[:], back[:].rearrange("p b t -> p (b t)"))
-                nc.scalar.dma_start(out=out[c * P : (c + 1) * P, lo : lo + 2 * P], in_=total[:])
+        def add_on_gpsimd(c, by_partner):
+            total = keep.tile([P, T], F32, name="total%d" % c)
+            nc.gpsimd.tensor_tensor(total[:], by_token[c][:], by_partner[:], ALU.add)
+            nc.scalar.dma_start(out=out[c * P : (c + 1) * P, :], in_=total[:])
 
         def add_on_vector(c, by_partner):
             for lo in range(0, T, 2 * P):
@@ -324,6 +311,6 @@ def tile_moe_dub_relu_kernel(
             scatter_dx(c, C, SLOTS, second[:, c, 0, :])
             scatter_dp(c, 1, second[:, c, 1, :])
             if c < LAST:
-                add_on_tensor(c, by_partner[c])
+                add_on_gpsimd(c, by_partner[c])
             else:
                 add_on_vector(c, by_partner[c])

@@ -26,9 +26,6 @@ TILES = SLOTS // P
 TILES_PER_EXPERT = C // P
 CHUNKS = K // P
 LAST = CHUNKS - 1
-WIDE = 768
-WARM_UPS = 4
-W2_PIECES = ((0, 0, H), (1, 0, H))
 
 
 def tile_moe_dub_relu_kernel(
@@ -43,28 +40,23 @@ def tile_moe_dub_relu_kernel(
         offs_sb = keep.tile([P, SLOTS // PER_COLUMN], U16, name="offs_sb")
         offs2_sb = keep.tile([P, SLOTS // PER_COLUMN], U16, name="offs2_sb")
         dy_w = keep.tile([P, PASSES * T], I32, name="dy_w")
-        dy_s = keep.tile([P, WIDE], U8, name="dy_s")
-        w2_w = [
-            keep.tile([P, PASSES * (hi - lo)], I32, name="w2_w%d" % n, align_bytes=64)
-            for n, (e, lo, hi) in enumerate(W2_PIECES)
-        ]
+        dy_s = keep.tile([P, T], U8, name="dy_s")
+        w2_first = [keep.tile([P, H], I32, name="w2_first%d" % s, align_bytes=64) for s in range(PASSES)]
+        w2_second = keep.tile([P, PASSES * H], I32, name="w2_second", align_bytes=64)
+        w2_w = [[w2_first[s][:] for s in range(PASSES)], [w2_second[:, s * H : (s + 1) * H] for s in range(PASSES)]]
         w2_s = keep.tile([P, H], U8, name="w2_s", align_bytes=64)
         w1_w = [keep.tile([P, K], I32, name="w1_w%d" % e, align_bytes=64) for e in range(E)]
-        w1_s_and_zeros = keep.tile([P, K + H + H * PACK + 2 * P], U8, name="w1_s_and_zeros", align_bytes=64)
-        w1_s = w1_s_and_zeros[:, 0:K]
-        zero_s = w1_s_and_zeros[:, K : K + H]
-        zero_w = w1_s_and_zeros[:, K + H : K + H + H * PACK].bitcast(U32)
-        zeros = w1_s_and_zeros[:, K + H + H * PACK :].bitcast(BF16)
-        gate_rows = keep.tile([P, P], F32, name="gate_rows")
+        w1_s = keep.tile([P, K], U8, name="w1_s", align_bytes=64)
+        gate_apart = keep.tile([P, TILES, 8], F32, name="gate_apart")
+        gate_col = keep.tile([P, TILES], F32, name="gate_col")
         a_sb = [keep.tile([P, PACK, C], F32, name="a_sb%d" % e) for e in range(E)]
         wp_raw = [keep.tile([P, PACK, K], F32, name="wp_raw", tag="wp_raw%d" % e) for e in range(E)]
 
         nc.gpsimd.memset(dy_s[:].bitcast(I32), 0)
-        nc.gpsimd.memset(gate_rows[:], 0.0)
         nc.gpsimd.memset(w2_s[:].bitcast(I32), 0)
         ident = keep.tile([P, P], F32, name="ident")
         make_identity(nc, ident[:])
-        nc.gpsimd.memset(w1_s_and_zeros[:].bitcast(I32), 0)
+        nc.gpsimd.memset(w1_s[:].bitcast(I32), 0)
 
         def load_scales(plane, rows):
             passes, width = rows.shape[0], rows.shape[2]
@@ -74,12 +66,9 @@ def tile_moe_dub_relu_kernel(
                     in_=rows[:, 4 * q : 4 * q + 4, :].bitcast(I32),
                 )
 
-        def load_w2(n):
-            e, lo, hi = W2_PIECES[n]
-            nc.sync.dma_start(
-                out=w2_w[n][:].rearrange("p (s i) -> p s i", s=PASSES),
-                in_=w2t_words[e, :, :, lo:hi, :].rearrange("s p i d -> p s (i d)").bitcast(I32),
-            )
+
+        def load_w2_first(s):
+            nc.sync.dma_start(out=w2_first[s][:], in_=w2t_words[0, s].rearrange("p i d -> p (i d)").bitcast(I32))
 
         def load_w1(e):
             nc.sync.dma_start(out=w1_w[e][:], in_=w1t_words[e, 0].rearrange("p k d -> p (k d)").bitcast(I32))
@@ -92,25 +81,30 @@ def tile_moe_dub_relu_kernel(
 
         nc.sync.dma_start(offs_sb[:], offs)
         load_scales(dy_s, dy_scales)
-        nc.sync.dma_start(out=gate_rows[0:TILES, :], in_=gate[0].rearrange("(j x) -> j x", x=P))
         nc.sync.dma_start(
             out=dy_w[:].rearrange("p (s t) -> p s t", s=PASSES),
             in_=dy_words.rearrange("s p t d -> p s (t d)").bitcast(I32),
         )
-        load_w2(0)
+        load_w2_first(0)
         load_scales(w2_s, w2t_scales.rearrange("e s b i -> (e s) b i"))
+        load_w2_first(1)
+        with nc.allow_non_contiguous_dma(reason="one gate value a partition and slot tile"):
+            nc.sync.dma_start(out=gate_apart[:, :, 0:1], in_=gate[0].rearrange("(j x o) -> x j o", x=P, o=1))
         load_a(0)
         load_w1(0)
         load_scales(w1_s, w1t_scales.rearrange("e s b k -> (e s) b k"))
         load_wp(0)
-        load_w2(1)
+        nc.sync.dma_start(
+            out=w2_second[:].rearrange("p (s i) -> p s i", s=PASSES),
+            in_=w2t_words[1].rearrange("s p i d -> p s (i d)").bitcast(I32),
+        )
         nc.sync.dma_start(offs2_sb[:], offs2)
         load_a(1)
         load_w1(1)
         load_wp(1)
 
         slot_w = {}
-        slot_s = keep.tile([P, SLOTS], U8, name="slot_s", align_bytes=64)
+        slot_s = {}
         dh_w = keep.tile([P, SLOTS], U32, name="dh_w", align_bytes=64)
         dh_s = keep.tile([P, SLOTS], U8, name="dh_s", align_bytes=64)
 
@@ -141,32 +135,29 @@ def tile_moe_dub_relu_kernel(
             nc.scalar.activation(active[:], signs[:], ACT.Relu)
             return active
 
-        gate_col = keep.tile([P, TILES], F32, name="gate_col")
-
         def turn_sums(j, turned):
-            cols = slice(j * P, (j + 1) * P)
+            cols = slice(j % TILES_PER_EXPERT * P, (j % TILES_PER_EXPERT + 1) * P)
             gated = keep.tile([P, 2, P, 2], BF16, name="gated", tag="gated%d" % j, align_bytes=64)
-            for n, (e, lo, hi) in enumerate(W2_PIECES):
-                if e != j // TILES_PER_EXPERT:
-                    continue
-                sums = psum.tile([P, hi - lo], F32, name="sums", tag="sums")
-                for s in range(PASSES):
-                    nc.tensor.matmul_mx(
-                        out=sums[:],
-                        lhsT=slot_w[(j, s)].bitcast(FP8X4),
-                        lhsT_scale=slot_s[4 * s : P, cols],
-                        rhs=w2_w[n][:, s * (hi - lo) : (s + 1) * (hi - lo)].bitcast(FP8X4),
-                        rhs_scale=w2_s[4 * (PASSES * e + s) : P, lo:hi],
-                        start=(s == 0),
-                        stop=(s == PASSES - 1),
-                    )
-                for us in ((slice(0, 1), slice(1, 2)) if e == 0 else (slice(0, 2),)):
-                    nc.scalar.activation(
-                        gated[:, us, lo // PACK : hi // PACK, :],
-                        sums[:].rearrange("x (p u d) -> x u p d", u=2, d=2)[:, us, :, :],
-                        ACT.Copy,
-                        scale=gate_col[:, j : j + 1],
-                    )
+            e = j // TILES_PER_EXPERT
+            sums = psum.tile([P, H], F32, name="sums", tag="sums")
+            order = range(PASSES) if j == 0 else reversed(range(PASSES))
+            for n, s in enumerate(order):
+                nc.tensor.matmul_mx(
+                    out=sums[:],
+                    lhsT=slot_w[(j, s)].bitcast(FP8X4),
+                    lhsT_scale=slot_s[e][4 * s : P, cols],
+                    rhs=w2_w[e][s].bitcast(FP8X4),
+                    rhs_scale=w2_s[4 * (PASSES * e + s) : P, :],
+                    start=(n == 0),
+                    stop=(n == PASSES - 1),
+                )
+            for us in ((slice(0, 1), slice(1, 2)) if e == 0 else (slice(0, 2),)):
+                nc.scalar.activation(
+                    gated[:, us, :, :],
+                    sums[:].rearrange("x (p u d) -> x u p d", u=2, d=2)[:, us, :, :],
+                    ACT.Copy,
+                    scale=gate_col[:, j : j + 1],
+                )
             for u in range(2):
                 pairs = gated[:, u, :, :].rearrange("x p d -> x (p d)").bitcast(F32)
                 nc.tensor.transpose(turned[:, :, u], pairs, ident[:])
@@ -204,31 +195,22 @@ def tile_moe_dub_relu_kernel(
                 )
             nc.scalar.copy(dst, acc[:])
 
-        nc.vector.quantize_mx(out=zero_w[:, 0 : P // PACK].bitcast(FP8X4), scales=zero_s[:, 0 : P // PACK], in_=zeros)
-        unread = psum.tile([P, H], F32, name="unread", tag="product", bufs=4)
-        for n in range(WARM_UPS):
-            nc.tensor.matmul_mx(
-                out=unread[:],
-                lhsT=zero_w[:, 0:P].bitcast(FP8X4),
-                lhsT_scale=zero_s[:, 0:P],
-                rhs=zero_w.bitcast(FP8X4),
-                rhs_scale=zero_s,
-                start=True,
-                stop=True,
-            )
+        nc.scalar.activation(gate_col[:], gate_apart[:, :, 0], ACT.Copy)
 
-        nc.tensor.transpose(unread[:, 0:P], gate_rows[:], ident[:])
-        nc.scalar.activation(gate_col[:], unread[:, 0:TILES], ACT.Copy)
+        def gather_scales(e, tag):
+            slot_s[e] = keep.tile([P, C], U8, name="slot_s", tag=tag, align_bytes=64)
+            nc.vector.tensor_copy(slot_s[e][:], dy_s[:].indirect(entries(offs_sb, e * C, (e + 1) * C)))
 
-        nc.vector.tensor_copy(slot_s[:], dy_s[:].indirect(offs_sb[:]))
+        gather_scales(0, "slot_s0")
         for j in range(TILES_PER_EXPERT):
             for s in range(PASSES):
                 gather_words([j], s, "slot_w%d%d" % (j, s))
         for s in range(PASSES):
             gather_words([2, 3], s, "slot_w2%d" % s)
         turned_first = [turned_sums([j]) for j in range(TILES_PER_EXPERT)]
+        gather_scales(1, "slot_w00")
         quantised_gradient([0], turned_first[0], mask_on_vector(0, "active0"), "dh0")
-        quantised_gradient([1], turned_first[1], mask_on_vector(1, "gated0"), "dh1")
+        quantised_gradient([1], turned_first[1], mask_on_vector(1, "gated0"), "dh0")
 
         by_token = [keep.tile([P, T], F32, name="by_token%d" % c) for c in range(CHUNKS)]
 

@@ -26,6 +26,8 @@ TILES = SLOTS // P
 TILES_PER_EXPERT = C // P
 CHUNKS = K // P
 LAST = CHUNKS - 1
+LEAD = 64
+SUM_BANKS = ((("sums", 2),), (("sums", 2), ("product", 4)), (("sums", 2),), (("sums", 2),))
 
 
 def tile_moe_dub_relu_kernel(
@@ -136,28 +138,30 @@ def tile_moe_dub_relu_kernel(
             return active
 
         def turn_sums(j, turned):
-            cols = slice(j % TILES_PER_EXPERT * P, (j % TILES_PER_EXPERT + 1) * P)
             gated = keep.tile([P, 2, P, 2], BF16, name="gated", tag="gated%d" % j, align_bytes=64)
             e = j // TILES_PER_EXPERT
-            sums = psum.tile([P, H], F32, name="sums", tag="sums")
-            order = range(PASSES) if j == 0 else reversed(range(PASSES))
-            for n, s in enumerate(order):
-                nc.tensor.matmul_mx(
-                    out=sums[:],
-                    lhsT=slot_w[(j, s)].bitcast(FP8X4),
-                    lhsT_scale=slot_s[e][4 * s : P, cols],
-                    rhs=w2_w[e][s].bitcast(FP8X4),
-                    rhs_scale=w2_s[4 * (PASSES * e + s) : P, :],
-                    start=(n == 0),
-                    stop=(n == PASSES - 1),
-                )
-            for us in ((slice(0, 1), slice(1, 2)) if e == 0 else (slice(0, 2),)):
-                nc.scalar.activation(
-                    gated[:, us, :, :],
-                    sums[:].rearrange("x (p u d) -> x u p d", u=2, d=2)[:, us, :, :],
-                    ACT.Copy,
-                    scale=gate_col[:, j : j + 1],
-                )
+            banks = SUM_BANKS[j]
+            width = H // len(banks)
+            for h, (tag, bufs) in enumerate(banks):
+                sums = psum.tile([P, width], F32, name="sums", tag=tag, bufs=bufs)
+                order = range(PASSES) if j == 0 else reversed(range(PASSES))
+                for n, s in enumerate(order):
+                    nc.tensor.matmul_mx(
+                        out=sums[:],
+                        lhsT=slot_w[(j, s)].bitcast(FP8X4),
+                        lhsT_scale=slot_s[j][4 * s : P, :],
+                        rhs=w2_w[e][s][:, h * width : (h + 1) * width].bitcast(FP8X4),
+                        rhs_scale=w2_s[4 * (PASSES * e + s) : P, h * width : (h + 1) * width],
+                        start=(n == 0),
+                        stop=(n == PASSES - 1),
+                    )
+                for us in ((slice(0, 1), slice(1, 2)) if j == 0 else (slice(0, 2),)):
+                    nc.scalar.activation(
+                        gated[:, us, h * width // PACK : (h + 1) * width // PACK, :],
+                        sums[:].rearrange("x (p u d) -> x u p d", u=2, d=2)[:, us, :, :],
+                        ACT.Copy,
+                        scale=gate_col[:, j : j + 1],
+                    )
             for u in range(2):
                 pairs = gated[:, u, :, :].rearrange("x p d -> x (p d)").bitcast(F32)
                 nc.tensor.transpose(turned[:, :, u], pairs, ident[:])
@@ -168,24 +172,22 @@ def tile_moe_dub_relu_kernel(
                 turn_sums(j, turned[:, n * P : (n + 1) * P, :])
             return turned
 
-        def quantised_gradient(tiles, turned, active, tag):
-            cols = slice(tiles[0] * P, (tiles[-1] + 1) * P)
-            dh = keep.tile([P, len(tiles) * P * PACK], BF16, name="dh", tag=tag, align_bytes=64)
-            pairs = turned[:].rearrange("p x u -> p (x u)")
-            engine = nc.vector
-            if len(tiles) > 1:
-                unmasked = keep.tile([P, len(tiles) * P * 2], F32, name="unmasked")
-                nc.scalar.copy(unmasked[:], pairs)
-                pairs, engine = unmasked[:], nc.gpsimd
-            engine.tensor_tensor(dh[:], pairs.bitcast(BF16), active[:].rearrange("p x t -> p (x t)"), ALU.mult)
-            nc.vector.quantize_mx(out=dh_w[:, cols].bitcast(FP8X4), scales=dh_s[:, cols], in_=dh[:])
+        def masked(engine, pairs, active, tag):
+            dh = keep.tile([P, pairs.shape[1] * PACK], BF16, name="dh", tag=tag, align_bytes=64)
+            engine.tensor_tensor(
+                dh[:], pairs.rearrange("p x u -> p (x u)").bitcast(BF16), active.rearrange("p x t -> p (x t)"), ALU.mult
+            )
+            return dh
+
+        def quantise_gradient(dh, lo, hi):
+            nc.vector.quantize_mx(out=dh_w[:, lo:hi].bitcast(FP8X4), scales=dh_s[:, lo:hi], in_=dh[:])
 
         def products(dst, parts):
-            width = parts[0][4] - parts[0][3]
-            acc = psum.tile([P, len(parts), width], F32, name="acc", tag="product", bufs=4)
-            for b, (weights, plane, column, lo, hi) in enumerate(parts):
+            acc = psum.tile([P, sum(part[4] - part[3] for part in parts)], F32, name="acc", tag="product", bufs=4)
+            at = 0
+            for weights, plane, column, lo, hi in parts:
                 nc.tensor.matmul_mx(
-                    out=acc[:, b, :],
+                    out=acc[:, at : at + hi - lo],
                     lhsT=weights[:, column : column + P].bitcast(FP8X4),
                     lhsT_scale=plane[:, column : column + P],
                     rhs=dh_w[:, lo:hi].bitcast(FP8X4),
@@ -193,24 +195,32 @@ def tile_moe_dub_relu_kernel(
                     start=True,
                     stop=True,
                 )
+                at += hi - lo
             nc.scalar.copy(dst, acc[:])
 
         nc.scalar.activation(gate_col[:], gate_apart[:, :, 0], ACT.Copy)
 
-        def gather_scales(e, tag):
-            slot_s[e] = keep.tile([P, C], U8, name="slot_s", tag=tag, align_bytes=64)
-            nc.vector.tensor_copy(slot_s[e][:], dy_s[:].indirect(entries(offs_sb, e * C, (e + 1) * C)))
+        def gather_scales(tiles, tag):
+            lo, hi = tiles[0] * P, (tiles[-1] + 1) * P
+            scales = keep.tile([P, hi - lo], U8, name="slot_s", tag=tag, align_bytes=64)
+            nc.vector.tensor_copy(scales[:], dy_s[:].indirect(entries(offs_sb, lo, hi)))
+            for n, j in enumerate(tiles):
+                slot_s[j] = scales[:, n * P : (n + 1) * P]
 
-        gather_scales(0, "slot_s0")
+        gather_scales([0, 1, 2], "slot_s0")
         for j in range(TILES_PER_EXPERT):
             for s in range(PASSES):
                 gather_words([j], s, "slot_w%d%d" % (j, s))
         for s in range(PASSES):
             gather_words([2, 3], s, "slot_w2%d" % s)
         turned_first = [turned_sums([j]) for j in range(TILES_PER_EXPERT)]
-        gather_scales(1, "slot_w00")
-        quantised_gradient([0], turned_first[0], mask_on_vector(0, "active0"), "dh0")
-        quantised_gradient([1], turned_first[1], mask_on_vector(1, "gated0"), "dh0")
+        gather_scales([3], "slot_w00")
+        active_first = [mask_on_vector(j, "active0%d" % j) for j in range(TILES_PER_EXPERT)]
+        lead = masked(nc.vector, turned_first[0][:, 0:LEAD, :], active_first[0][:, 0:LEAD, :], "dh_lead")
+        rest = masked(nc.vector, turned_first[0][:, LEAD:P, :], active_first[0][:, LEAD:P, :], "dh_rest")
+        quantise_gradient(lead, 0, LEAD)
+        quantise_gradient(rest, LEAD, P)
+        quantise_gradient(masked(nc.vector, turned_first[1][:], active_first[1][:], "dh_lead"), P, C)
 
         by_token = [keep.tile([P, T], F32, name="by_token%d" % c) for c in range(CHUNKS)]
 
@@ -235,25 +245,26 @@ def tile_moe_dub_relu_kernel(
                 out=wp_w[e][:].bitcast(FP8X4), scales=wp_s[e][:], in_=grouped[:].rearrange("p k t -> p (k t)")
             )
 
-        dx_early = keep.tile([P, 5, P], F32, name="dx_early")
-        products(dx_early[:, 0:1, :], [token_part(0, 0, P)])
-        products(dx_early[:, 1:3, :], [token_part(c, 0, P) for c in (1, 2)])
-        products(dx_early[:, 3:5, :], [token_part(c, P, C) for c in (0, 1)])
-        for c in range(3):
-            scatter_dx(c, 0, P, dx_early[:, c, :])
-        for c in range(2):
-            scatter_dx(c, P, C, dx_early[:, 3 + c, :])
+        for c, hi in enumerate((LEAD, P)):
+            dx_first = keep.tile([P, hi], F32, name="dx_first", tag="dx_first%d" % c)
+            products(dx_first[:], [token_part(c, 0, hi)])
+            scatter_dx(c, 0, hi, dx_first[:])
+        dx_early = keep.tile([P, 2 * C - LEAD], F32, name="dx_early")
+        products(dx_early[:, 0:C], [token_part(2, 0, C)])
+        products(dx_early[:, C:], [token_part(0, LEAD, P), token_part(0, P, C)])
+        scatter_dx(2, 0, C, dx_early[:, 0:C])
+        scatter_dx(0, LEAD, C, dx_early[:, C:])
 
         quantised_partner_weights(0)
-        dx_late = keep.tile([P, 3, P], F32, name="dx_late", tag="wp_raw0")
-        products(dx_late[:], [token_part(2, P, C), token_part(LAST, 0, P), token_part(LAST, P, C)])
-        scatter_dx(2, P, C, dx_late[:, 0, :])
-        scatter_dx(LAST, 0, C, dx_late[:, 1:3, :].rearrange("p b x -> p (b x)"))
+        dx_late = keep.tile([P, 3 * P], F32, name="dx_late", tag="wp_raw0")
+        products(dx_late[:], [token_part(1, P, C), token_part(LAST, 0, P), token_part(LAST, P, C)])
+        scatter_dx(1, P, C, dx_late[:, 0:P])
+        scatter_dx(LAST, 0, C, dx_late[:, P:])
 
         turned_second = turned_sums([2, 3])
         dp_first = keep.tile([P, CHUNKS, C], F32, name="dp_first")
-        products(dp_first[:, 0:1, :], [partner_part(0, 0)])
-        products(dp_first[:, 1:3, :], [partner_part(c, 0) for c in (1, 2)])
+        products(dp_first[:, 0, :], [partner_part(0, 0)])
+        products(dp_first[:, 1:3, :].rearrange("p c x -> p (c x)"), [partner_part(c, 0) for c in (1, 2)])
         by_partner = []
 
         def scatter_dp(c, e, values):
@@ -263,19 +274,22 @@ def tile_moe_dub_relu_kernel(
             by_partner.append(keep.tile([P, T], F32, name="by_partner%d" % c))
             scatter_dp(c, 0, dp_first[:, c, :])
 
-        quantised_gradient([2, 3], turned_second, mask_on_scalar(), "dh2")
+        active_second = mask_on_scalar()
+        unmasked = keep.tile([P, C, 2], F32, name="unmasked")
+        nc.scalar.copy(unmasked[:], turned_second[:])
+        quantise_gradient(masked(nc.gpsimd, unmasked[:], active_second[:], "dh2"), C, SLOTS)
         by_partner.append(keep.tile([P, T], F32, name="by_partner2"))
         scatter_dp(2, 0, dp_first[:, 2, :])
-        products(dp_first[:, LAST:CHUNKS, :], [partner_part(LAST, 0)])
+        products(dp_first[:, LAST, :], [partner_part(LAST, 0)])
         quantised_partner_weights(1)
         by_partner.append(keep.tile([P, T], F32, name="by_partner3", tag="wp_raw1"))
         scatter_dp(LAST, 0, dp_first[:, LAST, :])
 
         second = keep.tile([P, CHUNKS, 2, C], F32, name="second")
-        products(second[:, 0, 0:1, :], [token_part(0, C, SLOTS)])
-        products(second[:, 0, 1:2, :], [partner_part(0, 1)])
+        products(second[:, 0, 0, :], [token_part(0, C, SLOTS)])
+        products(second[:, 0, 1, :], [partner_part(0, 1)])
         for c in range(1, CHUNKS):
-            products(second[:, c, :, :], [token_part(c, C, SLOTS), partner_part(c, 1)])
+            products(second[:, c, :, :].rearrange("p b x -> p (b x)"), [token_part(c, C, SLOTS), partner_part(c, 1)])
 
         def add_on_gpsimd(c, by_partner):
             total = keep.tile([P, T], F32, name="total%d" % c)

@@ -27,7 +27,7 @@ TILES_PER_EXPERT = C // P
 CHUNKS = K // P
 LAST = CHUNKS - 1
 LEAD = 64
-SUM_BANKS = ((("sums", 2),), (("sums", 2), ("product", 4)), (("sums", 2),), (("sums", 2),))
+SUM_BANKS = ((("sums", 2), ("sums", 2)), (("product", 4), ("product", 4)), (("sums", 2),), (("sums", 2),))
 
 
 def tile_moe_dub_relu_kernel(
@@ -36,7 +36,6 @@ def tile_moe_dub_relu_kernel(
     nc = tc.nc
     with ExitStack() as ctx:
         keep = ctx.enter_context(tc.tile_pool(name="keep", bufs=1))
-        ring = ctx.enter_context(tc.tile_pool(name="ring", bufs=2))
         psum = ctx.enter_context(tc.psum_pool(name="psum", bufs=2))
 
         offs_sb = keep.tile([P, SLOTS // PER_COLUMN], U16, name="offs_sb")
@@ -60,10 +59,10 @@ def tile_moe_dub_relu_kernel(
         make_identity(nc, ident[:])
         nc.gpsimd.memset(w1_s[:].bitcast(I32), 0)
 
-        def load_scales(plane, rows):
+        def load_scales(plane, rows, on_scalar=()):
             passes, width = rows.shape[0], rows.shape[2]
             for q in range(QUADRANTS):
-                nc.sync.dma_start(
+                (nc.scalar if q in on_scalar else nc.sync).dma_start(
                     out=plane[32 * q : 32 * q + 4 * passes, 0:width].bitcast(I32),
                     in_=rows[:, 4 * q : 4 * q + 4, :].bitcast(I32),
                 )
@@ -82,13 +81,13 @@ def tile_moe_dub_relu_kernel(
             nc.sync.dma_start(out=a_sb[e][:], in_=a[:, e * C : (e + 1) * C].rearrange("(p t) j -> p t j", t=PACK))
 
         nc.sync.dma_start(offs_sb[:], offs)
-        load_scales(dy_s, dy_scales)
+        load_scales(dy_s, dy_scales, (2, 3))
         nc.sync.dma_start(
             out=dy_w[:].rearrange("p (s t) -> p s t", s=PASSES),
             in_=dy_words.rearrange("s p t d -> p s (t d)").bitcast(I32),
         )
         load_w2_first(0)
-        load_scales(w2_s, w2t_scales.rearrange("e s b i -> (e s) b i"))
+        load_scales(w2_s, w2t_scales.rearrange("e s b i -> (e s) b i"), (0,))
         load_w2_first(1)
         with nc.allow_non_contiguous_dma(reason="one gate value a partition and slot tile"):
             nc.sync.dma_start(out=gate_apart[:, :, 0:1], in_=gate[0].rearrange("(j x o) -> x j o", x=P, o=1))
@@ -155,13 +154,12 @@ def tile_moe_dub_relu_kernel(
                         start=(n == 0),
                         stop=(n == PASSES - 1),
                     )
-                for us in ((slice(0, 1), slice(1, 2)) if j == 0 else (slice(0, 2),)):
-                    nc.scalar.activation(
-                        gated[:, us, h * width // PACK : (h + 1) * width // PACK, :],
-                        sums[:].rearrange("x (p u d) -> x u p d", u=2, d=2)[:, us, :, :],
-                        ACT.Copy,
-                        scale=gate_col[:, j : j + 1],
-                    )
+                nc.scalar.activation(
+                    gated[:, :, h * width // PACK : (h + 1) * width // PACK, :],
+                    sums[:].rearrange("x (p u d) -> x u p d", u=2, d=2),
+                    ACT.Copy,
+                    scale=gate_col[:, j : j + 1],
+                )
             for u in range(2):
                 pairs = gated[:, u, :, :].rearrange("x p d -> x (p d)").bitcast(F32)
                 nc.tensor.transpose(turned[:, :, u], pairs, ident[:])
@@ -297,9 +295,9 @@ def tile_moe_dub_relu_kernel(
             nc.scalar.dma_start(out=out[c * P : (c + 1) * P, :], in_=total[:])
 
         def add_on_vector(c, by_partner):
-            for lo in range(0, T, 2 * P):
-                half = slice(lo, lo + 2 * P)
-                total = ring.tile([P, 2 * P], F32, name="total")
+            for lo, hi in ((0, 2 * P), (2 * P, 3 * P), (3 * P, T)):
+                half = slice(lo, hi)
+                total = keep.tile([P, hi - lo], F32, name="total", tag="last%d" % lo)
                 nc.vector.tensor_tensor(total[:], by_token[c][:, half], by_partner[:, half], ALU.add)
                 nc.sync.dma_start(out=out[c * P : (c + 1) * P, half], in_=total[:])
 

@@ -247,22 +247,22 @@ def tile_moe_dub_relu_kernel(
             dx_first = keep.tile([P, hi], F32, name="dx_first", tag="dx_first%d" % c)
             products(dx_first[:], [token_part(c, 0, hi)])
             scatter_dx(c, 0, hi, dx_first[:])
-        dx_early = keep.tile([P, 2 * C - LEAD], F32, name="dx_early")
+        dx_early = keep.tile([P, 2 * C - LEAD + P], F32, name="dx_early")
         products(dx_early[:, 0:C], [token_part(2, 0, C)])
-        products(dx_early[:, C:], [token_part(0, LEAD, P), token_part(0, P, C)])
+        products(dx_early[:, C:], [token_part(0, LEAD, P), token_part(0, P, C), token_part(1, P, C)])
         scatter_dx(2, 0, C, dx_early[:, 0:C])
-        scatter_dx(0, LEAD, C, dx_early[:, C:])
+        scatter_dx(0, LEAD, C, dx_early[:, C : 2 * C - LEAD])
+        scatter_dx(1, P, C, dx_early[:, 2 * C - LEAD :])
 
         quantised_partner_weights(0)
-        dx_late = keep.tile([P, 3 * P], F32, name="dx_late", tag="wp_raw0")
-        products(dx_late[:], [token_part(1, P, C), token_part(LAST, 0, P), token_part(LAST, P, C)])
-        scatter_dx(1, P, C, dx_late[:, 0:P])
-        scatter_dx(LAST, 0, C, dx_late[:, P:])
+        dx_late = keep.tile([P, C], F32, name="dx_late", tag="wp_raw0")
+        products(dx_late[:], [token_part(LAST, 0, C)])
+        scatter_dx(LAST, 0, C, dx_late[:])
 
         turned_second = turned_sums([2, 3])
         dp_first = keep.tile([P, CHUNKS, C], F32, name="dp_first")
-        products(dp_first[:, 0, :], [partner_part(0, 0)])
-        products(dp_first[:, 1:3, :].rearrange("p c x -> p (c x)"), [partner_part(c, 0) for c in (1, 2)])
+        for c in range(LAST):
+            products(dp_first[:, c, :], [partner_part(c, 0)])
         by_partner = []
 
         def scatter_dp(c, e, values):

@@ -27,7 +27,8 @@ TILES_PER_EXPERT = C // P
 CHUNKS = K // P
 LAST = CHUNKS - 1
 LEAD = 64
-SUM_BANKS = ((("sums", 2), ("sums", 2)), (("product", 4), ("product", 4)), (("sums", 2),), (("sums", 2),))
+HALF = K // 2
+SUM_BANKS = (("sums", "sums"), ("for_vector", "for_scalar"), ("sums",), ("sums",))
 
 
 def tile_moe_dub_relu_kernel(
@@ -51,7 +52,10 @@ def tile_moe_dub_relu_kernel(
         gate_apart = keep.tile([P, TILES, 8], F32, name="gate_apart")
         gate_col = keep.tile([P, TILES], F32, name="gate_col")
         a_sb = [keep.tile([P, PACK, C], F32, name="a_sb%d" % e) for e in range(E)]
-        wp_raw = [keep.tile([P, PACK, K], F32, name="wp_raw", tag="wp_raw%d" % e) for e in range(E)]
+        wp_raw = [
+            [keep.tile([P, PACK, HALF], F32, name="wp_raw", tag="wp_raw%d%d" % (e, h), align_bytes=64) for h in range(2)]
+            for e in range(E)
+        ]
 
         nc.gpsimd.memset(dy_s[:].bitcast(I32), 0)
         nc.gpsimd.memset(w2_s[:].bitcast(I32), 0)
@@ -74,8 +78,9 @@ def tile_moe_dub_relu_kernel(
         def load_w1(e):
             nc.sync.dma_start(out=w1_w[e][:], in_=w1t_words[e, 0].rearrange("p k d -> p (k d)").bitcast(I32))
 
-        def load_wp(e):
-            nc.sync.dma_start(out=wp_raw[e][:], in_=wpt[e].rearrange("(p t) k -> p t k", t=PACK))
+        def load_wp(e, h):
+            rows = wpt[e][:, h * HALF : (h + 1) * HALF]
+            nc.sync.dma_start(out=wp_raw[e][h][:], in_=rows.rearrange("(p t) k -> p t k", t=PACK))
 
         def load_a(e):
             nc.sync.dma_start(out=a_sb[e][:], in_=a[:, e * C : (e + 1) * C].rearrange("(p t) j -> p t j", t=PACK))
@@ -94,15 +99,17 @@ def tile_moe_dub_relu_kernel(
         load_a(0)
         load_w1(0)
         load_scales(w1_s, w1t_scales.rearrange("e s b k -> (e s) b k"))
-        load_wp(0)
+        load_wp(0, 0)
         nc.sync.dma_start(
             out=w2_second[:].rearrange("p (s i) -> p s i", s=PASSES),
             in_=w2t_words[1].rearrange("s p i d -> p s (i d)").bitcast(I32),
         )
-        nc.sync.dma_start(offs2_sb[:], offs2)
+        load_wp(0, 1)
         load_a(1)
         load_w1(1)
-        load_wp(1)
+        nc.sync.dma_start(offs2_sb[:], offs2)
+        load_wp(1, 0)
+        load_wp(1, 1)
 
         slot_w = {}
         slot_s = {}
@@ -123,17 +130,10 @@ def tile_moe_dub_relu_kernel(
         def by_fours(natural, grouped):
             return grouped.rearrange("p (c i) t -> p c t i", i=4), natural.rearrange("p t (c i) -> p c t i", i=4)
 
-        def mask_on_vector(j, tag):
-            active = keep.tile([P, P, PACK], BF16, name="active", tag=tag, align_bytes=64)
-            dst, src = by_fours(a_sb[0][:, :, j * P : (j + 1) * P], active[:])
+        def mask_on_vector(e, lo, hi, tag):
+            active = keep.tile([P, hi - lo, PACK], BF16, name="active", tag=tag, align_bytes=64)
+            dst, src = by_fours(a_sb[e][:, :, lo:hi], active[:])
             nc.vector.tensor_scalar(dst, src, 0.0, None, ALU.is_gt)
-            return active
-
-        def mask_on_scalar():
-            signs = keep.tile([P, C, PACK], BF16, name="signs", align_bytes=64)
-            nc.scalar.activation(*by_fours(a_sb[1][:], signs[:]), ACT.Sign)
-            active = keep.tile([P, C, PACK], BF16, name="active", tag="active1", align_bytes=64)
-            nc.scalar.activation(active[:], signs[:], ACT.Relu)
             return active
 
         def turn_sums(j, turned):
@@ -141,8 +141,8 @@ def tile_moe_dub_relu_kernel(
             e = j // TILES_PER_EXPERT
             banks = SUM_BANKS[j]
             width = H // len(banks)
-            for h, (tag, bufs) in enumerate(banks):
-                sums = psum.tile([P, width], F32, name="sums", tag=tag, bufs=bufs)
+            for h, tag in enumerate(banks):
+                sums = psum.tile([P, width], F32, name="sums", tag=tag)
                 order = range(PASSES) if j == 0 else reversed(range(PASSES))
                 for n, s in enumerate(order):
                     nc.tensor.matmul_mx(
@@ -180,8 +180,9 @@ def tile_moe_dub_relu_kernel(
         def quantise_gradient(dh, lo, hi):
             nc.vector.quantize_mx(out=dh_w[:, lo:hi].bitcast(FP8X4), scales=dh_s[:, lo:hi], in_=dh[:])
 
-        def products(dst, parts):
-            acc = psum.tile([P, sum(part[4] - part[3] for part in parts)], F32, name="acc", tag="product", bufs=4)
+        def products(copier, parts, tag):
+            width = sum(part[4] - part[3] for part in parts)
+            acc = psum.tile([P, width], F32, name="acc", tag="for_" + copier)
             at = 0
             for weights, plane, column, lo, hi in parts:
                 nc.tensor.matmul_mx(
@@ -194,7 +195,12 @@ def tile_moe_dub_relu_kernel(
                     stop=True,
                 )
                 at += hi - lo
-            nc.scalar.copy(dst, acc[:])
+            values = keep.tile([P, width], F32, name="values", tag=tag, align_bytes=64)
+            if copier == "vector":
+                nc.vector.tensor_copy(values[:], acc[:])
+            else:
+                nc.scalar.copy(values[:], acc[:])
+            return values
 
         nc.scalar.activation(gate_col[:], gate_apart[:, :, 0], ACT.Copy)
 
@@ -213,7 +219,7 @@ def tile_moe_dub_relu_kernel(
             gather_words([2, 3], s, "slot_w2%d" % s)
         turned_first = [turned_sums([j]) for j in range(TILES_PER_EXPERT)]
         gather_scales([3], "slot_w00")
-        active_first = [mask_on_vector(j, "active0%d" % j) for j in range(TILES_PER_EXPERT)]
+        active_first = [mask_on_vector(0, j * P, (j + 1) * P, "active0%d" % j) for j in range(TILES_PER_EXPERT)]
         lead = masked(nc.vector, turned_first[0][:, 0:LEAD, :], active_first[0][:, 0:LEAD, :], "dh_lead")
         rest = masked(nc.vector, turned_first[0][:, LEAD:P, :], active_first[0][:, LEAD:P, :], "dh_rest")
         quantise_gradient(lead, 0, LEAD)
@@ -221,9 +227,20 @@ def tile_moe_dub_relu_kernel(
         quantise_gradient(masked(nc.vector, turned_first[1][:], active_first[1][:], "dh_lead"), P, C)
 
         by_token = [keep.tile([P, T], F32, name="by_token%d" % c) for c in range(CHUNKS)]
+        by_partner = [keep.tile([P, T], F32, name="by_partner%d" % c) for c in range(CHUNKS)]
 
-        def scatter_dx(c, lo, hi, values):
-            nc.vector.tensor_copy(by_token[c][:].indirect(entries(offs_sb, lo, hi)), values)
+        def scatter(engine, window, offsets, lo, hi, values):
+            target = window[:].indirect(entries(offsets, lo, hi))
+            if engine == "vector":
+                nc.vector.tensor_copy(target, values)
+            else:
+                nc.scalar.activation(target, values, ACT.Copy)
+
+        def scatter_dx(engine, c, lo, hi, values):
+            scatter(engine, by_token[c], offs_sb, lo, hi, values)
+
+        def scatter_dp(engine, c, lo, hi, values):
+            scatter(engine, by_partner[c], offs2_sb, lo, hi, values)
 
         def token_part(c, lo, hi):
             e = lo // C
@@ -235,76 +252,80 @@ def tile_moe_dub_relu_kernel(
         def partner_part(c, e):
             return (wp_w[e], wp_s[e], c * P, e * C, (e + 1) * C)
 
-        def quantised_partner_weights(e):
+        def rounded_partner_weights(e):
             grouped = keep.tile([P, K, PACK], BF16, name="grouped%d" % e, align_bytes=64)
             for k in range(0, K, P):
-                nc.scalar.copy(*by_fours(wp_raw[e][:, :, k : k + P], grouped[:, k : k + P, :]))
+                src = wp_raw[e][k // HALF][:, :, k % HALF : k % HALF + P].rearrange("p t k -> p k t")
+                nc.gpsimd.tensor_scalar(grouped[:, k : k + P, :], src, 1.0, 0.0, ALU.mult, ALU.add)
+            return grouped
+
+        def quantise_partner_weights(e, lo, hi):
             nc.vector.quantize_mx(
-                out=wp_w[e][:].bitcast(FP8X4), scales=wp_s[e][:], in_=grouped[:].rearrange("p k t -> p (k t)")
+                out=wp_w[e][:, lo:hi].bitcast(FP8X4),
+                scales=wp_s[e][:, lo:hi],
+                in_=grouped[e][:, lo:hi, :].rearrange("p k t -> p (k t)"),
             )
 
-        for c, hi in enumerate((LEAD, P)):
-            dx_first = keep.tile([P, hi], F32, name="dx_first", tag="dx_first%d" % c)
-            products(dx_first[:], [token_part(c, 0, hi)])
-            scatter_dx(c, 0, hi, dx_first[:])
-        dx_early = keep.tile([P, 2 * C - LEAD + P], F32, name="dx_early")
-        products(dx_early[:, 0:C], [token_part(2, 0, C)])
-        products(dx_early[:, C:], [token_part(0, LEAD, P), token_part(0, P, C), token_part(1, P, C)])
-        scatter_dx(2, 0, C, dx_early[:, 0:C])
-        scatter_dx(0, LEAD, C, dx_early[:, C : 2 * C - LEAD])
-        scatter_dx(1, P, C, dx_early[:, 2 * C - LEAD :])
+        grouped = [rounded_partner_weights(e) for e in range(E)]
 
-        quantised_partner_weights(0)
-        dx_late = keep.tile([P, C], F32, name="dx_late", tag="wp_raw0")
-        products(dx_late[:], [token_part(LAST, 0, C)])
-        scatter_dx(LAST, 0, C, dx_late[:])
+        lead_values = products("scalar", [token_part(0, 0, LEAD), token_part(2, 0, LEAD)], "dx_lead")
+        tile_values = products("scalar", [token_part(1, 0, P), token_part(3, 0, P)], "dx_tile0")
+        scatter_dx("vector", 0, 0, LEAD, lead_values[:, 0:LEAD])
+        scatter_dx("scalar", 2, 0, LEAD, lead_values[:, LEAD:])
+        scatter_dx("vector", 1, 0, P, tile_values[:, 0:P])
+        rest0 = products("vector", [token_part(0, LEAD, P), token_part(0, P, C)], "dx_rest0")
+        rest2 = products("scalar", [token_part(2, LEAD, P), token_part(2, P, C), token_part(3, P, C)], "dx_rest2")
+        scatter_dx("scalar", 3, 0, P, tile_values[:, P:])
+        scatter_dx("vector", 0, LEAD, C, rest0[:])
 
+        active_second = mask_on_vector(1, 0, C, "active1")
         turned_second = turned_sums([2, 3])
-        dp_first = keep.tile([P, CHUNKS, C], F32, name="dp_first")
-        for c in range(LAST):
-            products(dp_first[:, c, :], [partner_part(c, 0)])
-        by_partner = []
+        scatter_dx("scalar", 2, LEAD, C, rest2[:, 0 : C - LEAD])
+        dh_second = masked(nc.vector, turned_second[:], active_second[:], "dh2")
+        rest1 = products("vector", [token_part(1, P, C)], "active1")
+        quantise_gradient(dh_second, C, SLOTS)
+        scatter_dx("vector", 1, P, C, rest1[:])
+        scatter_dx("scalar", 3, P, C, rest2[:, C - LEAD :])
 
-        def scatter_dp(c, e, values):
-            nc.vector.tensor_copy(by_partner[c][:].indirect(entries(offs2_sb, e * C, (e + 1) * C)), values)
+        dx01 = products("vector", [token_part(0, C, SLOTS)], "dx01")
+        dx21 = products("scalar", [token_part(2, C, SLOTS), token_part(1, C, C + P)], "dx21")
+        scatter_dx("vector", 0, C, SLOTS, dx01[:])
+        scatter_dx("scalar", 2, C, SLOTS, dx21[:, 0:C])
+        scatter_dx("scalar", 1, C, C + P, dx21[:, C:])
+        dx11 = products("vector", [token_part(1, C + P, SLOTS)], "wp_raw01")
+        quantise_partner_weights(0, 0, K)
+        scatter_dx("vector", 1, C + P, SLOTS, dx11[:])
 
-        for c in range(2):
-            by_partner.append(keep.tile([P, T], F32, name="by_partner%d" % c))
-            scatter_dp(c, 0, dp_first[:, c, :])
+        dp00 = products("scalar", [partner_part(0, 0), partner_part(2, 0)], "dp00")
+        scatter_dp("scalar", 0, 0, C, dp00[:, 0:C])
+        scatter_dp("scalar", 2, 0, C, dp00[:, C:])
+        dp10 = products("vector", [partner_part(1, 0)], "wp_raw10")
+        quantise_partner_weights(1, 0, HALF)
+        scatter_dp("vector", 1, 0, C, dp10[:])
+        dp01 = products("scalar", [partner_part(0, 1)], "dp01")
+        dp11 = products("vector", [partner_part(1, 1)], "wp_raw11")
+        quantise_partner_weights(1, HALF, K)
+        dp3 = products("vector", [partner_part(LAST, 0), partner_part(LAST, 1)], "dp3")
+        late = products("scalar", [partner_part(2, 1), token_part(LAST, C, SLOTS)], "late")
 
-        active_second = mask_on_scalar()
-        unmasked = keep.tile([P, C, 2], F32, name="unmasked")
-        nc.scalar.copy(unmasked[:], turned_second[:])
-        quantise_gradient(masked(nc.gpsimd, unmasked[:], active_second[:], "dh2"), C, SLOTS)
-        by_partner.append(keep.tile([P, T], F32, name="by_partner2"))
-        scatter_dp(2, 0, dp_first[:, 2, :])
-        products(dp_first[:, LAST, :], [partner_part(LAST, 0)])
-        quantised_partner_weights(1)
-        by_partner.append(keep.tile([P, T], F32, name="by_partner3", tag="wp_raw1"))
-        scatter_dp(LAST, 0, dp_first[:, LAST, :])
-
-        second = keep.tile([P, CHUNKS, 2, C], F32, name="second")
-        products(second[:, 0, 0, :], [token_part(0, C, SLOTS)])
-        products(second[:, 0, 1, :], [partner_part(0, 1)])
-        for c in range(1, CHUNKS):
-            products(second[:, c, :, :].rearrange("p b x -> p (b x)"), [token_part(c, C, SLOTS), partner_part(c, 1)])
-
-        def add_on_gpsimd(c, by_partner):
+        def add_on_gpsimd(c):
             total = keep.tile([P, T], F32, name="total%d" % c)
-            nc.gpsimd.tensor_tensor(total[:], by_token[c][:], by_partner[:], ALU.add)
-            nc.scalar.dma_start(out=out[c * P : (c + 1) * P, :], in_=total[:])
+            nc.gpsimd.tensor_tensor(total[:], by_token[c][:], by_partner[c][:], ALU.add)
+            nc.sync.dma_start(out=out[c * P : (c + 1) * P, :], in_=total[:])
 
-        def add_on_vector(c, by_partner):
+        def add_on_vector(c):
             for lo, hi in ((0, 2 * P), (2 * P, 3 * P), (3 * P, T)):
-                half = slice(lo, hi)
                 total = keep.tile([P, hi - lo], F32, name="total", tag="last%d" % lo)
-                nc.vector.tensor_tensor(total[:], by_token[c][:, half], by_partner[:, half], ALU.add)
-                nc.sync.dma_start(out=out[c * P : (c + 1) * P, half], in_=total[:])
+                nc.vector.tensor_tensor(total[:], by_token[c][:, lo:hi], by_partner[c][:, lo:hi], ALU.add)
+                nc.sync.dma_start(out=out[c * P : (c + 1) * P, lo:hi], in_=total[:])
 
-        for c in range(CHUNKS):
-            scatter_dx(c, C, SLOTS, second[:, c, 0, :])
-            scatter_dp(c, 1, second[:, c, 1, :])
-            if c < LAST:
-                add_on_gpsimd(c, by_partner[c])
-            else:
-                add_on_vector(c, by_partner[c])
+        scatter_dp("vector", 1, C, SLOTS, dp11[:])
+        add_on_gpsimd(1)
+        scatter_dp("scalar", 0, C, SLOTS, dp01[:])
+        add_on_gpsimd(0)
+        scatter_dp("vector", LAST, 0, C, dp3[:, 0:C])
+        scatter_dp("scalar", 2, C, SLOTS, late[:, 0:C])
+        add_on_gpsimd(2)
+        scatter_dp("vector", LAST, C, SLOTS, dp3[:, C:])
+        scatter_dx("scalar", LAST, C, SLOTS, late[:, C:])
+        add_on_vector(LAST)

@@ -28,7 +28,8 @@ CHUNKS = K // P
 LAST = CHUNKS - 1
 LEAD = 64
 HALF = K // 2
-SUM_BANKS = (("sums", "sums"), ("for_vector", "for_scalar"), ("sums",), ("sums",))
+PIECE = 128
+SUM_BANKS = (("sums0", "sums1"), ("va", "sa"), ("sums0",), ("sums1",))
 
 
 def tile_moe_dub_relu_kernel(
@@ -37,7 +38,7 @@ def tile_moe_dub_relu_kernel(
     nc = tc.nc
     with ExitStack() as ctx:
         keep = ctx.enter_context(tc.tile_pool(name="keep", bufs=1))
-        psum = ctx.enter_context(tc.psum_pool(name="psum", bufs=2))
+        psum = ctx.enter_context(tc.psum_pool(name="psum", bufs=1))
 
         offs_sb = keep.tile([P, SLOTS // PER_COLUMN], U16, name="offs_sb")
         offs2_sb = keep.tile([P, SLOTS // PER_COLUMN], U16, name="offs2_sb")
@@ -97,16 +98,16 @@ def tile_moe_dub_relu_kernel(
         with nc.allow_non_contiguous_dma(reason="one gate value a partition and slot tile"):
             nc.sync.dma_start(out=gate_apart[:, :, 0:1], in_=gate[0].rearrange("(j x o) -> x j o", x=P, o=1))
         load_a(0)
-        load_w1(0)
         load_scales(w1_s, w1t_scales.rearrange("e s b k -> (e s) b k"))
-        load_wp(0, 0)
         nc.sync.dma_start(
             out=w2_second[:].rearrange("p (s i) -> p s i", s=PASSES),
             in_=w2t_words[1].rearrange("s p i d -> p s (i d)").bitcast(I32),
         )
-        load_wp(0, 1)
+        load_w1(0)
         load_a(1)
         load_w1(1)
+        load_wp(0, 0)
+        load_wp(0, 1)
         nc.sync.dma_start(offs2_sb[:], offs2)
         load_wp(1, 0)
         load_wp(1, 1)
@@ -165,7 +166,7 @@ def tile_moe_dub_relu_kernel(
                 nc.tensor.transpose(turned[:, :, u], pairs, ident[:])
 
         def turned_sums(tiles):
-            turned = psum.tile([P, len(tiles) * P, 2], F32, name="turned", tag="turned")
+            turned = psum.tile([P, len(tiles) * P, 2], F32, name="turned", tag="turned%d" % (tiles[0] % 2))
             for n, j in enumerate(tiles):
                 turn_sums(j, turned[:, n * P : (n + 1) * P, :])
             return turned
@@ -180,9 +181,8 @@ def tile_moe_dub_relu_kernel(
         def quantise_gradient(dh, lo, hi):
             nc.vector.quantize_mx(out=dh_w[:, lo:hi].bitcast(FP8X4), scales=dh_s[:, lo:hi], in_=dh[:])
 
-        def products(copier, parts, tag):
-            width = sum(part[4] - part[3] for part in parts)
-            acc = psum.tile([P, width], F32, name="acc", tag="for_" + copier)
+        def products(bank, parts):
+            acc = psum.tile([P, sum(part[4] - part[3] for part in parts)], F32, name="acc", tag=bank)
             at = 0
             for weights, plane, column, lo, hi in parts:
                 nc.tensor.matmul_mx(
@@ -195,11 +195,14 @@ def tile_moe_dub_relu_kernel(
                     stop=True,
                 )
                 at += hi - lo
-            values = keep.tile([P, width], F32, name="values", tag=tag, align_bytes=64)
-            if copier == "vector":
-                nc.vector.tensor_copy(values[:], acc[:])
+            return acc
+
+        def copied(engine, sums, tag):
+            values = keep.tile([P, sums.shape[1]], F32, name="values", tag=tag, align_bytes=64)
+            if engine == "vector":
+                nc.vector.tensor_copy(values[:], sums)
             else:
-                nc.scalar.copy(values[:], acc[:])
+                nc.scalar.copy(values[:], sums)
             return values
 
         nc.scalar.activation(gate_col[:], gate_apart[:, :, 0], ACT.Copy)
@@ -249,14 +252,15 @@ def tile_moe_dub_relu_kernel(
         wp_w = [keep.tile([P, K], U32, name="wp_w%d" % e, align_bytes=64) for e in range(E)]
         wp_s = [keep.tile([P, K], U8, name="wp_s%d" % e, align_bytes=64) for e in range(E)]
 
-        def partner_part(c, e):
-            return (wp_w[e], wp_s[e], c * P, e * C, (e + 1) * C)
+        def partner_part(c, lo, hi):
+            e = lo // C
+            return (wp_w[e], wp_s[e], c * P, lo, hi)
 
         def rounded_partner_weights(e):
             grouped = keep.tile([P, K, PACK], BF16, name="grouped%d" % e, align_bytes=64)
-            for k in range(0, K, P):
-                src = wp_raw[e][k // HALF][:, :, k % HALF : k % HALF + P].rearrange("p t k -> p k t")
-                nc.gpsimd.tensor_scalar(grouped[:, k : k + P, :], src, 1.0, 0.0, ALU.mult, ALU.add)
+            for k in range(0, K, PIECE):
+                src = wp_raw[e][k // HALF][:, :, k % HALF : k % HALF + PIECE].rearrange("p t k -> p k t")
+                nc.gpsimd.tensor_scalar(grouped[:, k : k + PIECE, :], src, 1.0, 0.0, ALU.mult, ALU.add)
             return grouped
 
         def quantise_partner_weights(e, lo, hi):
@@ -267,46 +271,6 @@ def tile_moe_dub_relu_kernel(
             )
 
         grouped = [rounded_partner_weights(e) for e in range(E)]
-
-        lead_values = products("scalar", [token_part(0, 0, LEAD), token_part(2, 0, LEAD)], "dx_lead")
-        tile_values = products("scalar", [token_part(1, 0, P), token_part(3, 0, P)], "dx_tile0")
-        scatter_dx("vector", 0, 0, LEAD, lead_values[:, 0:LEAD])
-        scatter_dx("scalar", 2, 0, LEAD, lead_values[:, LEAD:])
-        scatter_dx("vector", 1, 0, P, tile_values[:, 0:P])
-        rest0 = products("vector", [token_part(0, LEAD, P), token_part(0, P, C)], "dx_rest0")
-        rest2 = products("scalar", [token_part(2, LEAD, P), token_part(2, P, C), token_part(3, P, C)], "dx_rest2")
-        scatter_dx("scalar", 3, 0, P, tile_values[:, P:])
-        scatter_dx("vector", 0, LEAD, C, rest0[:])
-
-        active_second = mask_on_vector(1, 0, C, "active1")
-        turned_second = turned_sums([2, 3])
-        scatter_dx("scalar", 2, LEAD, C, rest2[:, 0 : C - LEAD])
-        dh_second = masked(nc.vector, turned_second[:], active_second[:], "dh2")
-        rest1 = products("vector", [token_part(1, P, C)], "active1")
-        quantise_gradient(dh_second, C, SLOTS)
-        scatter_dx("vector", 1, P, C, rest1[:])
-        scatter_dx("scalar", 3, P, C, rest2[:, C - LEAD :])
-
-        dx01 = products("vector", [token_part(0, C, SLOTS)], "dx01")
-        dx21 = products("scalar", [token_part(2, C, SLOTS), token_part(1, C, C + P)], "dx21")
-        scatter_dx("vector", 0, C, SLOTS, dx01[:])
-        scatter_dx("scalar", 2, C, SLOTS, dx21[:, 0:C])
-        scatter_dx("scalar", 1, C, C + P, dx21[:, C:])
-        dx11 = products("vector", [token_part(1, C + P, SLOTS)], "wp_raw01")
-        quantise_partner_weights(0, 0, K)
-        scatter_dx("vector", 1, C + P, SLOTS, dx11[:])
-
-        dp00 = products("scalar", [partner_part(0, 0), partner_part(2, 0)], "dp00")
-        scatter_dp("scalar", 0, 0, C, dp00[:, 0:C])
-        scatter_dp("scalar", 2, 0, C, dp00[:, C:])
-        dp10 = products("vector", [partner_part(1, 0)], "wp_raw10")
-        quantise_partner_weights(1, 0, HALF)
-        scatter_dp("vector", 1, 0, C, dp10[:])
-        dp01 = products("scalar", [partner_part(0, 1)], "dp01")
-        dp11 = products("vector", [partner_part(1, 1)], "wp_raw11")
-        quantise_partner_weights(1, HALF, K)
-        dp3 = products("vector", [partner_part(LAST, 0), partner_part(LAST, 1)], "dp3")
-        late = products("scalar", [partner_part(2, 1), token_part(LAST, C, SLOTS)], "late")
 
         def add_on_gpsimd(c):
             total = keep.tile([P, T], F32, name="total%d" % c)
@@ -319,13 +283,65 @@ def tile_moe_dub_relu_kernel(
                 nc.vector.tensor_tensor(total[:], by_token[c][:, lo:hi], by_partner[c][:, lo:hi], ALU.add)
                 nc.sync.dma_start(out=out[c * P : (c + 1) * P, lo:hi], in_=total[:])
 
-        scatter_dp("vector", 1, C, SLOTS, dp11[:])
-        add_on_gpsimd(1)
+        turned_second = turned_sums([2, 3])
+
+        values = copied("scalar", products("sb", [token_part(0, 0, LEAD), token_part(2, 0, LEAD)])[:], "dx_lead")
+        dx1_first = copied("scalar", products("vb", [token_part(1, 0, P)])[:], "dx1_first")
+        scatter_dx("vector", 0, 0, LEAD, values[:, 0:LEAD])
+        scatter_dx("scalar", 2, 0, LEAD, values[:, LEAD:])
+        scatter_dx("vector", 1, 0, P, dx1_first[:])
+        dx0_rest = copied("scalar", products("va", [token_part(0, LEAD, P), token_part(0, P, C)])[:], "dx0_rest")
+        sums = products("sa", [token_part(3, 0, C), token_part(2, LEAD, P), token_part(2, P, C)])
+        dx3_first = copied("scalar", sums[:, 0:C], "dx3_first")
+        dx2_rest = copied("scalar", sums[:, C:], "dx2_rest")
+        scatter_dx("vector", 0, LEAD, C, dx0_rest[:])
+        scatter_dx("scalar", 3, 0, C, dx3_first[:])
+        scatter_dx("scalar", 2, LEAD, C, dx2_rest[:])
+
+        active_second = mask_on_vector(1, 0, C, "active1")
+        dh_second = masked(nc.vector, turned_second[:], active_second[:], "dh2")
+        dx1_rest = copied("vector", products("vb", [token_part(1, P, C)])[:], "active1")
+        quantise_gradient(dh_second, C, SLOTS)
+        scatter_dx("vector", 1, P, C, dx1_rest[:])
+
+        dx11 = copied("scalar", products("sb", [token_part(1, C, SLOTS)])[:], "dx11")
+        scatter_dx("scalar", 1, C, SLOTS, dx11[:])
+        dx01 = copied("vector", products("va", [token_part(0, C, SLOTS)])[:], "wp_raw01")
+        quantise_partner_weights(0, 0, K)
+        scatter_dx("vector", 0, C, SLOTS, dx01[:])
+
+        sums = products("sa", [partner_part(0, 0, C), partner_part(2, 0, P)])
+        dp00 = copied("scalar", sums[:, 0:C], "dp00")
+        dp20 = copied("scalar", sums[:, C:], "dp20")
+        scatter_dp("scalar", 0, 0, C, dp00[:])
+        scatter_dp("scalar", 2, 0, P, dp20[:])
+
+        values = copied("vector", products("vb", [partner_part(1, 0, C), partner_part(2, P, C)])[:], "wp_raw10")
+        quantise_partner_weights(1, 0, HALF)
+        scatter_dp("vector", 1, 0, C, values[:, 0:C])
+        scatter_dp("vector", 2, P, C, values[:, C:])
+
+        sums = products("sb", [partner_part(0, C, SLOTS), partner_part(1, C, SLOTS)])
+        dp01 = copied("scalar", sums[:, 0:C], "dp01")
+        dp11 = copied("scalar", sums[:, C:], "dp11")
         scatter_dp("scalar", 0, C, SLOTS, dp01[:])
         add_on_gpsimd(0)
-        scatter_dp("vector", LAST, 0, C, dp3[:, 0:C])
-        scatter_dp("scalar", 2, C, SLOTS, late[:, 0:C])
+        scatter_dp("scalar", 1, C, SLOTS, dp11[:])
+        add_on_gpsimd(1)
+
+        dp30 = copied("vector", products("va", [partner_part(LAST, 0, C)])[:], "wp_raw11")
+        quantise_partner_weights(1, HALF, K)
+        scatter_dp("vector", LAST, 0, C, dp30[:])
+
+        sums = products("sb", [token_part(2, C, SLOTS), token_part(LAST, C, SLOTS)])
+        dx21 = copied("scalar", sums[:, 0:C], "dx21")
+        dx31 = copied("scalar", sums[:, C:], "dx31")
+        sums = products("vb", [partner_part(2, C, SLOTS), partner_part(LAST, C, SLOTS)])
+        dp21 = copied("vector", sums[:, 0:C], "dp21")
+        dp31 = copied("vector", sums[:, C:], "dp31")
+        scatter_dx("scalar", 2, C, SLOTS, dx21[:])
+        scatter_dp("vector", 2, C, SLOTS, dp21[:])
         add_on_gpsimd(2)
-        scatter_dp("vector", LAST, C, SLOTS, dp3[:, C:])
-        scatter_dx("scalar", LAST, C, SLOTS, late[:, C:])
+        scatter_dx("scalar", LAST, C, SLOTS, dx31[:])
+        scatter_dp("vector", LAST, C, SLOTS, dp31[:])
         add_on_vector(LAST)

@@ -28,7 +28,6 @@ CHUNKS = K // P
 LAST = CHUNKS - 1
 LEAD = 64
 HALF = K // 2
-PIECE = 128
 SUM_BANKS = (("sums0", "sums1"), ("va", "sa"), ("sums0",), ("sums1",))
 
 
@@ -256,21 +255,19 @@ def tile_moe_dub_relu_kernel(
             e = lo // C
             return (wp_w[e], wp_s[e], c * P, lo, hi)
 
-        def rounded_partner_weights(e):
-            grouped = keep.tile([P, K, PACK], BF16, name="grouped%d" % e, align_bytes=64)
-            for k in range(0, K, PIECE):
-                src = wp_raw[e][k // HALF][:, :, k % HALF : k % HALF + PIECE].rearrange("p t k -> p k t")
-                nc.gpsimd.tensor_scalar(grouped[:, k : k + PIECE, :], src, 1.0, 0.0, ALU.mult, ALU.add)
+        def rounded_partner_weights(e, lo, hi):
+            grouped = keep.tile([P, hi - lo, PACK], BF16, name="grouped", align_bytes=64)
+            for k in range(lo, hi, P):
+                src = wp_raw[e][k // HALF][:, :, k % HALF : k % HALF + P].rearrange("p t k -> p k t")
+                nc.gpsimd.tensor_scalar(grouped[:, k - lo : k - lo + P, :], src, 1.0, 0.0, ALU.mult, ALU.add)
             return grouped
 
-        def quantise_partner_weights(e, lo, hi):
+        def quantise_partner_weights(e, lo, hi, grouped):
             nc.vector.quantize_mx(
                 out=wp_w[e][:, lo:hi].bitcast(FP8X4),
                 scales=wp_s[e][:, lo:hi],
-                in_=grouped[e][:, lo:hi, :].rearrange("p k t -> p (k t)"),
+                in_=grouped[:].rearrange("p k t -> p (k t)"),
             )
-
-        grouped = [rounded_partner_weights(e) for e in range(E)]
 
         def add_on_gpsimd(c):
             total = keep.tile([P, T], F32, name="total%d" % c)
@@ -306,8 +303,9 @@ def tile_moe_dub_relu_kernel(
 
         dx11 = copied("scalar", products("sb", [token_part(1, C, SLOTS)])[:], "dx11")
         scatter_dx("scalar", 1, C, SLOTS, dx11[:])
+        grouped = rounded_partner_weights(0, 0, K)
         dx01 = copied("vector", products("va", [token_part(0, C, SLOTS)])[:], "wp_raw01")
-        quantise_partner_weights(0, 0, K)
+        quantise_partner_weights(0, 0, K, grouped)
         scatter_dx("vector", 0, C, SLOTS, dx01[:])
 
         sums = products("sa", [partner_part(0, 0, C), partner_part(2, 0, P)])
@@ -316,8 +314,9 @@ def tile_moe_dub_relu_kernel(
         scatter_dp("scalar", 0, 0, C, dp00[:])
         scatter_dp("scalar", 2, 0, P, dp20[:])
 
+        grouped = rounded_partner_weights(1, 0, HALF)
         values = copied("vector", products("vb", [partner_part(1, 0, C), partner_part(2, P, C)])[:], "wp_raw10")
-        quantise_partner_weights(1, 0, HALF)
+        quantise_partner_weights(1, 0, HALF, grouped)
         scatter_dp("vector", 1, 0, C, values[:, 0:C])
         scatter_dp("vector", 2, P, C, values[:, C:])
 
@@ -329,8 +328,9 @@ def tile_moe_dub_relu_kernel(
         scatter_dp("scalar", 1, C, SLOTS, dp11[:])
         add_on_gpsimd(1)
 
+        grouped = rounded_partner_weights(1, HALF, K)
         dp30 = copied("vector", products("va", [partner_part(LAST, 0, C)])[:], "wp_raw11")
-        quantise_partner_weights(1, HALF, K)
+        quantise_partner_weights(1, HALF, K, grouped)
         scatter_dp("vector", LAST, 0, C, dp30[:])
 
         sums = products("sb", [token_part(2, C, SLOTS), token_part(LAST, C, SLOTS)])

@@ -104,8 +104,8 @@ def tile_moe_dub_relu_kernel(
         )
         load_w1(0)
         load_a(1)
-        load_w1(1)
         load_wp(0, 0)
+        load_w1(1)
         load_wp(0, 1)
         nc.sync.dma_start(offs2_sb[:], offs2)
         load_wp(1, 0)
@@ -136,7 +136,7 @@ def tile_moe_dub_relu_kernel(
             nc.vector.tensor_scalar(dst, src, 0.0, None, ALU.is_gt)
             return active
 
-        def turn_sums(j, turned):
+        def gated_sums(j):
             gated = keep.tile([P, 2, P, 2], BF16, name="gated", tag="gated%d" % j, align_bytes=64)
             e = j // TILES_PER_EXPERT
             banks = SUM_BANKS[j]
@@ -160,25 +160,30 @@ def tile_moe_dub_relu_kernel(
                     ACT.Copy,
                     scale=gate_col[:, j : j + 1],
                 )
-            for u in range(2):
-                pairs = gated[:, u, :, :].rearrange("x p d -> x (p d)").bitcast(F32)
-                nc.tensor.transpose(turned[:, :, u], pairs, ident[:])
+            return gated
 
-        def turned_sums(tiles):
-            turned = psum.tile([P, len(tiles) * P, 2], F32, name="turned", tag="turned%d" % (tiles[0] % 2))
-            for n, j in enumerate(tiles):
-                turn_sums(j, turned[:, n * P : (n + 1) * P, :])
-            return turned
+        def turned(tiles, bank):
+            pairs = psum.tile([P, 2, len(tiles) * P], F32, name="pairs", tag=bank)
+            for n, gated in enumerate(tiles):
+                for u in range(2):
+                    source = gated[:, u, :, :].rearrange("x p d -> x (p d)").bitcast(F32)
+                    nc.tensor.transpose(pairs[:, u, n * P : (n + 1) * P], source, ident[:])
+            return pairs
 
-        def masked(engine, pairs, active, tag):
-            dh = keep.tile([P, pairs.shape[1] * PACK], BF16, name="dh", tag=tag, align_bytes=64)
-            engine.tensor_tensor(
-                dh[:], pairs.rearrange("p x u -> p (x u)").bitcast(BF16), active.rearrange("p x t -> p (x t)"), ALU.mult
+        def dh_tile(slots, tag):
+            return keep.tile([P, slots * PACK], BF16, name="dh", tag=tag, align_bytes=64)[:]
+
+        def masked(pairs, active, dh):
+            nc.vector.tensor_tensor(
+                dh.rearrange("p (x u d) -> p x u d", u=2, d=2),
+                pairs.bitcast(BF16).rearrange("p u (x d) -> p x u d", d=2),
+                active.rearrange("p x (u d) -> p x u d", d=2),
+                ALU.mult,
             )
             return dh
 
         def quantise_gradient(dh, lo, hi):
-            nc.vector.quantize_mx(out=dh_w[:, lo:hi].bitcast(FP8X4), scales=dh_s[:, lo:hi], in_=dh[:])
+            nc.vector.quantize_mx(out=dh_w[:, lo:hi].bitcast(FP8X4), scales=dh_s[:, lo:hi], in_=dh)
 
         def products(bank, parts):
             acc = psum.tile([P, sum(part[4] - part[3] for part in parts)], F32, name="acc", tag=bank)
@@ -219,14 +224,14 @@ def tile_moe_dub_relu_kernel(
                 gather_words([j], s, "slot_w%d%d" % (j, s))
         for s in range(PASSES):
             gather_words([2, 3], s, "slot_w2%d" % s)
-        turned_first = [turned_sums([j]) for j in range(TILES_PER_EXPERT)]
+        turned_first = [turned([gated_sums(j)], "turned%d" % j) for j in range(TILES_PER_EXPERT)]
         gather_scales([3], "slot_w00")
         active_first = [mask_on_vector(0, j * P, (j + 1) * P, "active0%d" % j) for j in range(TILES_PER_EXPERT)]
-        lead = masked(nc.vector, turned_first[0][:, 0:LEAD, :], active_first[0][:, 0:LEAD, :], "dh_lead")
-        rest = masked(nc.vector, turned_first[0][:, LEAD:P, :], active_first[0][:, LEAD:P, :], "dh_rest")
+        lead = masked(turned_first[0][:, :, 0:LEAD], active_first[0][:, 0:LEAD, :], dh_tile(LEAD, "dh_lead"))
+        rest = masked(turned_first[0][:, :, LEAD:P], active_first[0][:, LEAD:P, :], dh_tile(P - LEAD, "dh_rest"))
         quantise_gradient(lead, 0, LEAD)
         quantise_gradient(rest, LEAD, P)
-        quantise_gradient(masked(nc.vector, turned_first[1][:], active_first[1][:], "dh_lead"), P, C)
+        quantise_gradient(masked(turned_first[1][:], active_first[1][:], dh_tile(P, "dh_lead")), P, C)
 
         by_token = [keep.tile([P, T], F32, name="by_token%d" % c) for c in range(CHUNKS)]
         by_partner = [keep.tile([P, T], F32, name="by_partner%d" % c) for c in range(CHUNKS)]
@@ -255,18 +260,17 @@ def tile_moe_dub_relu_kernel(
             e = lo // C
             return (wp_w[e], wp_s[e], c * P, lo, hi)
 
-        def rounded_partner_weights(e, lo, hi):
-            grouped = keep.tile([P, hi - lo, PACK], BF16, name="grouped", align_bytes=64)
-            for k in range(lo, hi, P):
-                src = wp_raw[e][k // HALF][:, :, k % HALF : k % HALF + P].rearrange("p t k -> p k t")
-                nc.gpsimd.tensor_scalar(grouped[:, k - lo : k - lo + P, :], src, 1.0, 0.0, ALU.mult, ALU.add)
-            return grouped
+        rounded = keep.tile([P, K * PACK], BF16, name="rounded", align_bytes=64)
 
-        def quantise_partner_weights(e, lo, hi, grouped):
+        def round_partner_weights(e, h, at):
+            grouped = rounded[:, at * PACK : (at + HALF) * PACK].rearrange("p (k t) -> p k t", t=PACK)
+            nc.gpsimd.tensor_scalar(grouped, wp_raw[e][h][:].rearrange("p t k -> p k t"), 1.0, 0.0, ALU.mult, ALU.add)
+
+        def quantise_partner_weights(e, lo, hi):
             nc.vector.quantize_mx(
                 out=wp_w[e][:, lo:hi].bitcast(FP8X4),
                 scales=wp_s[e][:, lo:hi],
-                in_=grouped[:].rearrange("p k t -> p (k t)"),
+                in_=rounded[:, 0 : (hi - lo) * PACK],
             )
 
         def add_on_gpsimd(c):
@@ -280,11 +284,16 @@ def tile_moe_dub_relu_kernel(
                 nc.vector.tensor_tensor(total[:], by_token[c][:, lo:hi], by_partner[c][:, lo:hi], ALU.add)
                 nc.sync.dma_start(out=out[c * P : (c + 1) * P, lo:hi], in_=total[:])
 
-        turned_second = turned_sums([2, 3])
+        turned_second = turned([gated_sums(j) for j in (2, 3)], "turned0")
+
+        active_second = mask_on_vector(1, 0, C, "active1")
+        dh_second = masked(turned_second[:], active_second[:], rounded[:, HALF * PACK :])
+        round_partner_weights(0, 0, 0)
 
         values = copied("scalar", products("sb", [token_part(0, 0, LEAD), token_part(2, 0, LEAD)])[:], "dx_lead")
         dx1_first = copied("scalar", products("vb", [token_part(1, 0, P)])[:], "dx1_first")
         scatter_dx("vector", 0, 0, LEAD, values[:, 0:LEAD])
+        quantise_gradient(dh_second, C, SLOTS)
         scatter_dx("scalar", 2, 0, LEAD, values[:, LEAD:])
         scatter_dx("vector", 1, 0, P, dx1_first[:])
         dx0_rest = copied("scalar", products("va", [token_part(0, LEAD, P), token_part(0, P, C)])[:], "dx0_rest")
@@ -295,17 +304,14 @@ def tile_moe_dub_relu_kernel(
         scatter_dx("scalar", 3, 0, C, dx3_first[:])
         scatter_dx("scalar", 2, LEAD, C, dx2_rest[:])
 
-        active_second = mask_on_vector(1, 0, C, "active1")
-        dh_second = masked(nc.vector, turned_second[:], active_second[:], "dh2")
         dx1_rest = copied("vector", products("vb", [token_part(1, P, C)])[:], "active1")
-        quantise_gradient(dh_second, C, SLOTS)
         scatter_dx("vector", 1, P, C, dx1_rest[:])
 
         dx11 = copied("scalar", products("sb", [token_part(1, C, SLOTS)])[:], "dx11")
         scatter_dx("scalar", 1, C, SLOTS, dx11[:])
-        grouped = rounded_partner_weights(0, 0, K)
+        round_partner_weights(0, 1, HALF)
         dx01 = copied("vector", products("va", [token_part(0, C, SLOTS)])[:], "wp_raw01")
-        quantise_partner_weights(0, 0, K, grouped)
+        quantise_partner_weights(0, 0, K)
         scatter_dx("vector", 0, C, SLOTS, dx01[:])
 
         sums = products("sa", [partner_part(0, 0, C), partner_part(2, 0, P)])
@@ -314,9 +320,9 @@ def tile_moe_dub_relu_kernel(
         scatter_dp("scalar", 0, 0, C, dp00[:])
         scatter_dp("scalar", 2, 0, P, dp20[:])
 
-        grouped = rounded_partner_weights(1, 0, HALF)
+        round_partner_weights(1, 0, 0)
         values = copied("vector", products("vb", [partner_part(1, 0, C), partner_part(2, P, C)])[:], "wp_raw10")
-        quantise_partner_weights(1, 0, HALF, grouped)
+        quantise_partner_weights(1, 0, HALF)
         scatter_dp("vector", 1, 0, C, values[:, 0:C])
         scatter_dp("vector", 2, P, C, values[:, C:])
 
@@ -328,9 +334,9 @@ def tile_moe_dub_relu_kernel(
         scatter_dp("scalar", 1, C, SLOTS, dp11[:])
         add_on_gpsimd(1)
 
-        grouped = rounded_partner_weights(1, HALF, K)
+        round_partner_weights(1, 1, 0)
         dp30 = copied("vector", products("va", [partner_part(LAST, 0, C)])[:], "wp_raw11")
-        quantise_partner_weights(1, HALF, K, grouped)
+        quantise_partner_weights(1, HALF, K)
         scatter_dp("vector", LAST, 0, C, dp30[:])
 
         sums = products("sb", [token_part(2, C, SLOTS), token_part(LAST, C, SLOTS)])

@@ -26,8 +26,8 @@ TILES = SLOTS // P
 TILES_PER_EXPERT = C // P
 CHUNKS = K // P
 LAST = CHUNKS - 1
-LEAD = 64
 HALF = K // 2
+SHARE = 128
 SUM_BANKS = (("sums0", "sums1"), ("va", "sa"), ("sums0",), ("sums1",))
 
 
@@ -224,14 +224,10 @@ def tile_moe_dub_relu_kernel(
                 gather_words([j], s, "slot_w%d%d" % (j, s))
         for s in range(PASSES):
             gather_words([2, 3], s, "slot_w2%d" % s)
-        turned_first = [turned([gated_sums(j)], "turned%d" % j) for j in range(TILES_PER_EXPERT)]
+        turned_first = turned([gated_sums(j) for j in range(TILES_PER_EXPERT)], "turned0")
         gather_scales([3], "slot_w00")
-        active_first = [mask_on_vector(0, j * P, (j + 1) * P, "active0%d" % j) for j in range(TILES_PER_EXPERT)]
-        lead = masked(turned_first[0][:, :, 0:LEAD], active_first[0][:, 0:LEAD, :], dh_tile(LEAD, "dh_lead"))
-        rest = masked(turned_first[0][:, :, LEAD:P], active_first[0][:, LEAD:P, :], dh_tile(P - LEAD, "dh_rest"))
-        quantise_gradient(lead, 0, LEAD)
-        quantise_gradient(rest, LEAD, P)
-        quantise_gradient(masked(turned_first[1][:], active_first[1][:], dh_tile(P, "dh_lead")), P, C)
+        active_first = mask_on_vector(0, 0, C, "active0")
+        quantise_gradient(masked(turned_first[:], active_first[:], dh_tile(C, "dh_first")), 0, C)
 
         by_token = [keep.tile([P, T], F32, name="by_token%d" % c) for c in range(CHUNKS)]
         by_partner = [keep.tile([P, T], F32, name="by_partner%d" % c) for c in range(CHUNKS)]
@@ -284,47 +280,43 @@ def tile_moe_dub_relu_kernel(
                 nc.vector.tensor_tensor(total[:], by_token[c][:, lo:hi], by_partner[c][:, lo:hi], ALU.add)
                 nc.sync.dma_start(out=out[c * P : (c + 1) * P, lo:hi], in_=total[:])
 
-        turned_second = turned([gated_sums(j) for j in (2, 3)], "turned0")
-
+        gated_second = [gated_sums(j) for j in (2, 3)]
         active_second = mask_on_vector(1, 0, C, "active1")
-        dh_second = masked(turned_second[:], active_second[:], rounded[:, HALF * PACK :])
         round_partner_weights(0, 0, 0)
 
-        values = copied("scalar", products("sb", [token_part(0, 0, LEAD), token_part(2, 0, LEAD)])[:], "dx_lead")
-        dx1_first = copied("scalar", products("vb", [token_part(1, 0, P)])[:], "dx1_first")
-        scatter_dx("vector", 0, 0, LEAD, values[:, 0:LEAD])
+        dx0_first = copied("scalar", products("vb", [token_part(0, 0, P)])[:], "dx0_first")
+        sums = products("sb", [token_part(2, 0, C), token_part(3, 0, C)])
+        dx20 = copied("scalar", sums[:, 0:C], "dx20")
+        dx30 = copied("scalar", sums[:, C:], "dx30")
+        turned_second = turned(gated_second, "turned1")
+        scatter_dx("vector", 0, 0, P, dx0_first[:])
+        scatter_dx("scalar", 2, 0, C, dx20[:])
+        scatter_dx("scalar", 3, 0, C, dx30[:])
+        dh_second = masked(turned_second[:], active_second[:], rounded[:, HALF * PACK :])
+        values = copied("vector", products("sa", [token_part(1, 0, C), token_part(0, P, C)])[:], "active1")
         quantise_gradient(dh_second, C, SLOTS)
-        scatter_dx("scalar", 2, 0, LEAD, values[:, LEAD:])
-        scatter_dx("vector", 1, 0, P, dx1_first[:])
-        dx0_rest = copied("scalar", products("va", [token_part(0, LEAD, P), token_part(0, P, C)])[:], "dx0_rest")
-        sums = products("sa", [token_part(3, 0, C), token_part(2, LEAD, P), token_part(2, P, C)])
-        dx3_first = copied("scalar", sums[:, 0:C], "dx3_first")
-        dx2_rest = copied("scalar", sums[:, C:], "dx2_rest")
-        scatter_dx("vector", 0, LEAD, C, dx0_rest[:])
-        scatter_dx("scalar", 3, 0, C, dx3_first[:])
-        scatter_dx("scalar", 2, LEAD, C, dx2_rest[:])
+        scatter_dx("vector", 1, 0, C, values[:, 0:C])
+        scatter_dx("vector", 0, P, C, values[:, C:])
 
-        dx1_rest = copied("vector", products("vb", [token_part(1, P, C)])[:], "active1")
-        scatter_dx("vector", 1, P, C, dx1_rest[:])
-
-        dx11 = copied("scalar", products("sb", [token_part(1, C, SLOTS)])[:], "dx11")
+        sums = products("sb", [token_part(1, C, SLOTS), token_part(2, C, SLOTS)])
+        dx11 = copied("scalar", sums[:, 0:C], "dx11")
+        dx21 = copied("scalar", sums[:, C:], "dx21")
         scatter_dx("scalar", 1, C, SLOTS, dx11[:])
+        scatter_dx("scalar", 2, C, SLOTS, dx21[:])
+
         round_partner_weights(0, 1, HALF)
         dx01 = copied("vector", products("va", [token_part(0, C, SLOTS)])[:], "wp_raw01")
         quantise_partner_weights(0, 0, K)
         scatter_dx("vector", 0, C, SLOTS, dx01[:])
 
-        sums = products("sa", [partner_part(0, 0, C), partner_part(2, 0, P)])
-        dp00 = copied("scalar", sums[:, 0:C], "dp00")
-        dp20 = copied("scalar", sums[:, C:], "dp20")
+        dp00 = copied("scalar", products("sa", [partner_part(0, 0, C)])[:], "dp00")
         scatter_dp("scalar", 0, 0, C, dp00[:])
-        scatter_dp("scalar", 2, 0, P, dp20[:])
 
         round_partner_weights(1, 0, 0)
-        values = copied("vector", products("vb", [partner_part(1, 0, C), partner_part(2, P, C)])[:], "wp_raw10")
+        values = copied("vector", products("vb", [partner_part(1, 0, C), partner_part(LAST, SHARE, C)])[:], "wp_raw10")
         quantise_partner_weights(1, 0, HALF)
         scatter_dp("vector", 1, 0, C, values[:, 0:C])
-        scatter_dp("vector", 2, P, C, values[:, C:])
+        scatter_dp("vector", LAST, SHARE, C, values[:, C:])
 
         sums = products("sb", [partner_part(0, C, SLOTS), partner_part(1, C, SLOTS)])
         dp01 = copied("scalar", sums[:, 0:C], "dp01")
@@ -335,17 +327,16 @@ def tile_moe_dub_relu_kernel(
         add_on_gpsimd(1)
 
         round_partner_weights(1, 1, 0)
-        dp30 = copied("vector", products("va", [partner_part(LAST, 0, C)])[:], "wp_raw11")
+        dp20 = copied("vector", products("va", [partner_part(2, 0, C)])[:], "wp_raw11")
         quantise_partner_weights(1, HALF, K)
-        scatter_dp("vector", LAST, 0, C, dp30[:])
+        scatter_dp("vector", 2, 0, C, dp20[:])
 
-        sums = products("sb", [token_part(2, C, SLOTS), token_part(LAST, C, SLOTS)])
-        dx21 = copied("scalar", sums[:, 0:C], "dx21")
-        dx31 = copied("scalar", sums[:, C:], "dx31")
-        sums = products("vb", [partner_part(2, C, SLOTS), partner_part(LAST, C, SLOTS)])
-        dp21 = copied("vector", sums[:, 0:C], "dp21")
-        dp31 = copied("vector", sums[:, C:], "dp31")
-        scatter_dx("scalar", 2, C, SLOTS, dx21[:])
+        sums = products("sb", [token_part(LAST, C, SLOTS), partner_part(LAST, 0, SHARE)])
+        dp3_share = copied("scalar", sums[:, C:], "dp3_share")
+        dx31 = copied("scalar", sums[:, 0:C], "dx31")
+        dp21 = copied("vector", products("vb", [partner_part(2, C, SLOTS)])[:], "dp21")
+        dp31 = copied("vector", products("sums0", [partner_part(LAST, C, SLOTS)])[:], "dp31")
+        scatter_dp("scalar", LAST, 0, SHARE, dp3_share[:])
         scatter_dp("vector", 2, C, SLOTS, dp21[:])
         add_on_gpsimd(2)
         scatter_dx("scalar", LAST, C, SLOTS, dx31[:])

@@ -28,7 +28,7 @@ CHUNKS = K // P
 LAST = CHUNKS - 1
 HALF = K // 2
 SHARE = 128
-SUM_BANKS = (("sums0", "sums1"), ("va", "sa"), ("sums0",), ("sums1",))
+SUM_BANKS = (("sums0",), ("va", "sa"), ("sums0",), ("sums1",))
 
 
 def tile_moe_dub_relu_kernel(
@@ -275,7 +275,7 @@ def tile_moe_dub_relu_kernel(
             nc.sync.dma_start(out=out[c * P : (c + 1) * P, :], in_=total[:])
 
         def add_on_vector(c):
-            for lo, hi in ((0, 2 * P), (2 * P, 3 * P), (3 * P, T)):
+            for lo, hi in ((0, 3 * P), (3 * P, T)):
                 total = keep.tile([P, hi - lo], F32, name="total", tag="last%d" % lo)
                 nc.vector.tensor_tensor(total[:], by_token[c][:, lo:hi], by_partner[c][:, lo:hi], ALU.add)
                 nc.sync.dma_start(out=out[c * P : (c + 1) * P, lo:hi], in_=total[:])

@@ -28,7 +28,7 @@ CHUNKS = K // P
 LAST = CHUNKS - 1
 HALF = K // 2
 SHARE = 128
-SUM_BANKS = (("sums0",), ("va", "sa"), ("sums0",), ("sums1",))
+SUM_BANKS = (("sums0",), ("va", "sa"), ("sums0", "turned1"), ("sums1", "va"))
 
 
 def tile_moe_dub_relu_kernel(
@@ -288,7 +288,7 @@ def tile_moe_dub_relu_kernel(
         sums = products("sb", [token_part(2, 0, C), token_part(3, 0, C)])
         dx20 = copied("scalar", sums[:, 0:C], "dx20")
         dx30 = copied("scalar", sums[:, C:], "dx30")
-        turned_second = turned(gated_second, "turned1")
+        turned_second = turned(gated_second, "va")
         scatter_dx("vector", 0, 0, P, dx0_first[:])
         scatter_dx("scalar", 2, 0, C, dx20[:])
         scatter_dx("scalar", 3, 0, C, dx30[:])

@@ -275,10 +275,10 @@ def tile_moe_dub_relu_kernel(
             nc.sync.dma_start(out=out[c * P : (c + 1) * P, :], in_=total[:])
 
         def add_on_vector(c):
-            for lo, hi in ((0, 3 * P), (3 * P, T)):
+            for lo, hi, queue in ((0, T // 2, nc.sync), (T // 2, T, nc.scalar)):
                 total = keep.tile([P, hi - lo], F32, name="total", tag="last%d" % lo)
                 nc.vector.tensor_tensor(total[:], by_token[c][:, lo:hi], by_partner[c][:, lo:hi], ALU.add)
-                nc.sync.dma_start(out=out[c * P : (c + 1) * P, lo:hi], in_=total[:])
+                queue.dma_start(out=out[c * P : (c + 1) * P, lo:hi], in_=total[:])
 
         gated_second = [gated_sums(j) for j in (2, 3)]
         active_second = mask_on_vector(1, 0, C, "active1")

@@ -275,10 +275,10 @@ def tile_moe_dub_relu_kernel(
             nc.sync.dma_start(out=out[c * P : (c + 1) * P, :], in_=total[:])
 
         def add_on_vector(c):
-            for lo, hi, queue in ((0, T // 2, nc.sync), (T // 2, T, nc.scalar)):
+            for lo, hi in ((0, T // 2), (T // 2, T)):
                 total = keep.tile([P, hi - lo], F32, name="total", tag="last%d" % lo)
                 nc.vector.tensor_tensor(total[:], by_token[c][:, lo:hi], by_partner[c][:, lo:hi], ALU.add)
-                queue.dma_start(out=out[c * P : (c + 1) * P, lo:hi], in_=total[:])
+                nc.sync.dma_start(out=out[c * P : (c + 1) * P, lo:hi], in_=total[:])
 
         gated_second = [gated_sums(j) for j in (2, 3)]
         active_second = mask_on_vector(1, 0, C, "active1")

from contextlib import ExitStack

import concourse.mybir as mybir
from concourse.masks import make_identity

K, T, E, C, H, N = 512, 512, 2, 256, 512, 1024
FLOPS = 2 * E * C * (N * H + 2 * H * K)

F32 = mybir.dt.float32
BF16 = mybir.dt.bfloat16
I32 = mybir.dt.int32
U32 = mybir.dt.uint32
U16 = mybir.dt.uint16
U8 = mybir.dt.uint8
FP8X4 = mybir.dt.float8_e4m3fn_x4
ACT = mybir.ActivationFunctionType
ALU = mybir.AluOpType

P = 128
PACK = 4
QUADRANTS = 4
PER_COLUMN = 16
PASSES = N // (P * PACK)
SLOTS = E * C
TILES = SLOTS // P
TILES_PER_EXPERT = C // P
CHUNKS = K // P
LAST = CHUNKS - 1
HALF = K // 2
SHARE = 128
SUM_BANKS = (("sums0",), ("va", "sa"), ("sums0", "turned1"), ("sums1", "va"))


def tile_moe_dub_relu_kernel(
    tc, dy_words, dy_scales, w2t_words, w2t_scales, w1t_words, w1t_scales, wpt, a, gate, offs, offs2, out
):
    nc = tc.nc
    with ExitStack() as ctx:
        keep = ctx.enter_context(tc.tile_pool(name="keep", bufs=1))
        psum = ctx.enter_context(tc.psum_pool(name="psum", bufs=1))

        offs_sb = keep.tile([P, SLOTS // PER_COLUMN], U16, name="offs_sb")
        offs2_sb = keep.tile([P, SLOTS // PER_COLUMN], U16, name="offs2_sb")
        dy_w = keep.tile([P, PASSES * T], I32, name="dy_w")
        dy_s = keep.tile([P, T], U8, name="dy_s")
        w2_first = [keep.tile([P, H], I32, name="w2_first%d" % s, align_bytes=64) for s in range(PASSES)]
        w2_second = keep.tile([P, PASSES * H], I32, name="w2_second", align_bytes=64)
        w2_w = [[w2_first[s][:] for s in range(PASSES)], [w2_second[:, s * H : (s + 1) * H] for s in range(PASSES)]]
        w2_s = keep.tile([P, H], U8, name="w2_s", align_bytes=64)
        w1_w = [keep.tile([P, K], I32, name="w1_w%d" % e, align_bytes=64) for e in range(E)]
        w1_s = keep.tile([P, K], U8, name="w1_s", align_bytes=64)
        gate_apart = keep.tile([P, TILES, 8], F32, name="gate_apart")
        gate_col = keep.tile([P, TILES], F32, name="gate_col")
        a_sb = [keep.tile([P, PACK, C], F32, name="a_sb%d" % e) for e in range(E)]
        wp_raw = [
            [keep.tile([P, PACK, HALF], F32, name="wp_raw", tag="wp_raw%d%d" % (e, h), align_bytes=64) for h in range(2)]
            for e in range(E)
        ]

        nc.gpsimd.memset(dy_s[:].bitcast(I32), 0)
        nc.gpsimd.memset(w2_s[:].bitcast(I32), 0)
        ident = keep.tile([P, P], F32, name="ident")
        make_identity(nc, ident[:])
        nc.gpsimd.memset(w1_s[:].bitcast(I32), 0)

        def load_scales(plane, rows, on_scalar=()):
            passes, width = rows.shape[0], rows.shape[2]
            for q in range(QUADRANTS):
                (nc.scalar if q in on_scalar else nc.sync).dma_start(
                    out=plane[32 * q : 32 * q + 4 * passes, 0:width].bitcast(I32),
                    in_=rows[:, 4 * q : 4 * q + 4, :].bitcast(I32),
                )


        def load_w2_first(s):
            nc.sync.dma_start(out=w2_first[s][:], in_=w2t_words[0, s].rearrange("p i d -> p (i d)").bitcast(I32))

        def load_w1(e):
            nc.sync.dma_start(out=w1_w[e][:], in_=w1t_words[e, 0].rearrange("p k d -> p (k d)").bitcast(I32))

        def load_wp(e, h):
            rows = wpt[e][:, h * HALF : (h + 1) * HALF]
            nc.sync.dma_start(out=wp_raw[e][h][:], in_=rows.rearrange("(p t) k -> p t k", t=PACK))

        def load_a(e):
            nc.sync.dma_start(out=a_sb[e][:], in_=a[:, e * C : (e + 1) * C].rearrange("(p t) j -> p t j", t=PACK))

        nc.sync.dma_start(offs_sb[:], offs)
        load_scales(dy_s, dy_scales, (2, 3))
        nc.sync.dma_start(
            out=dy_w[:].rearrange("p (s t) -> p s t", s=PASSES),
            in_=dy_words.rearrange("s p t d -> p s (t d)").bitcast(I32),
        )
        load_w2_first(0)
        load_scales(w2_s, w2t_scales.rearrange("e s b i -> (e s) b i"), (0,))
        load_w2_first(1)
        with nc.allow_non_contiguous_dma(reason="one gate value a partition and slot tile"):
            nc.sync.dma_start(out=gate_apart[:, :, 0:1], in_=gate[0].rearrange("(j x o) -> x j o", x=P, o=1))
        load_a(0)
        load_scales(w1_s, w1t_scales.rearrange("e s b k -> (e s) b k"))
        nc.sync.dma_start(
            out=w2_second[:].rearrange("p (s i) -> p s i", s=PASSES),
            in_=w2t_words[1].rearrange("s p i d -> p s (i d)").bitcast(I32),
        )
        load_w1(0)
        load_a(1)
        load_wp(0, 0)
        load_w1(1)
        load_wp(0, 1)
        nc.sync.dma_start(offs2_sb[:], offs2)
        load_wp(1, 0)
        load_wp(1, 1)

        slot_w = {}
        slot_s = {}
        dh_w = keep.tile([P, SLOTS], U32, name="dh_w", align_bytes=64)
        dh_s = keep.tile([P, SLOTS], U8, name="dh_s", align_bytes=64)

        def entries(offsets, lo, hi):
            return offsets[:, lo // PER_COLUMN : hi // PER_COLUMN]

        def gather_words(tiles, s, tag):
            lo, hi = tiles[0] * P, (tiles[-1] + 1) * P
            words = keep.tile([P, hi - lo], U32, name="slot_w", tag=tag, align_bytes=64)
            window = dy_w[:, s * T : (s + 1) * T].bitcast(U32)
            nc.vector.tensor_copy(words[:], window.indirect(entries(offs_sb, lo, hi)))
            for n, j in enumerate(tiles):
                slot_w[(j, s)] = words[:, n * P : (n + 1) * P]

        def by_fours(natural, grouped):
            return grouped.rearrange("p (c i) t -> p c t i", i=4), natural.rearrange("p t (c i) -> p c t i", i=4)

        def mask_on_vector(e, lo, hi, tag):
            active = keep.tile([P, hi - lo, PACK], BF16, name="active", tag=tag, align_bytes=64)
            dst, src = by_fours(a_sb[e][:, :, lo:hi], active[:])
            nc.vector.tensor_scalar(dst, src, 0.0, None, ALU.is_gt)
            return active

        def gated_sums(j):
            gated = keep.tile([P, 2, P, 2], BF16, name="gated", tag="gated%d" % j, align_bytes=64)
            e = j // TILES_PER_EXPERT
            banks = SUM_BANKS[j]
            width = H // len(banks)
            for h, tag in enumerate(banks):
                sums = psum.tile([P, width], F32, name="sums", tag=tag)
                order = range(PASSES) if j == 0 else reversed(range(PASSES))
                for n, s in enumerate(order):
                    nc.tensor.matmul_mx(
                        out=sums[:],
                        lhsT=slot_w[(j, s)].bitcast(FP8X4),
                        lhsT_scale=slot_s[j][4 * s : P, :],
                        rhs=w2_w[e][s][:, h * width : (h + 1) * width].bitcast(FP8X4),
                        rhs_scale=w2_s[4 * (PASSES * e + s) : P, h * width : (h + 1) * width],
                        start=(n == 0),
                        stop=(n == PASSES - 1),
                    )
                nc.scalar.activation(
                    gated[:, :, h * width // PACK : (h + 1) * width // PACK, :],
                    sums[:].rearrange("x (p u d) -> x u p d", u=2, d=2),
                    ACT.Copy,
                    scale=gate_col[:, j : j + 1],
                )
            return gated

        def turned(tiles, bank):
            pairs = psum.tile([P, 2, len(tiles) * P], F32, name="pairs", tag=bank)
            for n, gated in enumerate(tiles):
                for u in range(2):
                    source = gated[:, u, :, :].rearrange("x p d -> x (p d)").bitcast(F32)
                    nc.tensor.transpose(pairs[:, u, n * P : (n + 1) * P], source, ident[:])
            return pairs

        def dh_tile(slots, tag):
            return keep.tile([P, slots * PACK], BF16, name="dh", tag=tag, align_bytes=64)[:]

        def masked(pairs, active, dh):
            nc.vector.tensor_tensor(
                dh.rearrange("p (x u d) -> p x u d", u=2, d=2),
                pairs.bitcast(BF16).rearrange("p u (x d) -> p x u d", d=2),
                active.rearrange("p x (u d) -> p x u d", d=2),
                ALU.mult,
            )
            return dh

        def quantise_gradient(dh, lo, hi):
            nc.vector.quantize_mx(out=dh_w[:, lo:hi].bitcast(FP8X4), scales=dh_s[:, lo:hi], in_=dh)

        def products(bank, parts):
            acc = psum.tile([P, sum(part[4] - part[3] for part in parts)], F32, name="acc", tag=bank)
            at = 0
            for weights, plane, column, lo, hi in parts:
                nc.tensor.matmul_mx(
                    out=acc[:, at : at + hi - lo],
                    lhsT=weights[:, column : column + P].bitcast(FP8X4),
                    lhsT_scale=plane[:, column : column + P],
                    rhs=dh_w[:, lo:hi].bitcast(FP8X4),
                    rhs_scale=dh_s[:, lo:hi],
                    start=True,
                    stop=True,
                )
                at += hi - lo
            return acc

        def copied(engine, sums, tag):
            values = keep.tile([P, sums.shape[1]], F32, name="values", tag=tag, align_bytes=64)
            if engine == "vector":
                nc.vector.tensor_copy(values[:], sums)
            else:
                nc.scalar.copy(values[:], sums)
            return values

        nc.scalar.activation(gate_col[:], gate_apart[:, :, 0], ACT.Copy)

        def gather_scales(tiles, tag):
            lo, hi = tiles[0] * P, (tiles[-1] + 1) * P
            scales = keep.tile([P, hi - lo], U8, name="slot_s", tag=tag, align_bytes=64)
            nc.vector.tensor_copy(scales[:], dy_s[:].indirect(entries(offs_sb, lo, hi)))
            for n, j in enumerate(tiles):
                slot_s[j] = scales[:, n * P : (n + 1) * P]

        gather_scales([0, 1, 2], "slot_s0")
        for j in range(TILES_PER_EXPERT):
            for s in range(PASSES):
                gather_words([j], s, "slot_w%d%d" % (j, s))
        for s in range(PASSES):
            gather_words([2, 3], s, "slot_w2%d" % s)
        turned_first = turned([gated_sums(j) for j in range(TILES_PER_EXPERT)], "turned0")
        gather_scales([3], "slot_w00")
        active_first = mask_on_vector(0, 0, C, "active0")
        quantise_gradient(masked(turned_first[:], active_first[:], dh_tile(C, "dh_first")), 0, C)

        by_token = [keep.tile([P, T], F32, name="by_token%d" % c) for c in range(CHUNKS)]
        by_partner = [keep.tile([P, T], F32, name="by_partner%d" % c) for c in range(CHUNKS)]

        def scatter(engine, window, offsets, lo, hi, values):
            target = window[:].indirect(entries(offsets, lo, hi))
            if engine == "vector":
                nc.vector.tensor_copy(target, values)
            else:
                nc.scalar.activation(target, values, ACT.Copy)

        def scatter_dx(engine, c, lo, hi, values):
            scatter(engine, by_token[c], offs_sb, lo, hi, values)

        def scatter_dp(engine, c, lo, hi, values):
            scatter(engine, by_partner[c], offs2_sb, lo, hi, values)

        def token_part(c, lo, hi):
            e = lo // C
            return (w1_w[e], w1_s[4 * e : P, :], c * P, lo, hi)

        wp_w = [keep.tile([P, K], U32, name="wp_w%d" % e, align_bytes=64) for e in range(E)]
        wp_s = [keep.tile([P, K], U8, name="wp_s%d" % e, align_bytes=64) for e in range(E)]

        def partner_part(c, lo, hi):
            e = lo // C
            return (wp_w[e], wp_s[e], c * P, lo, hi)

        rounded = keep.tile([P, K * PACK], BF16, name="rounded", align_bytes=64)

        def round_partner_weights(e, h, at):
            grouped = rounded[:, at * PACK : (at + HALF) * PACK].rearrange("p (k t) -> p k t", t=PACK)
            nc.gpsimd.tensor_scalar(grouped, wp_raw[e][h][:].rearrange("p t k -> p k t"), 1.0, 0.0, ALU.mult, ALU.add)

        def quantise_partner_weights(e, lo, hi):
            nc.vector.quantize_mx(
                out=wp_w[e][:, lo:hi].bitcast(FP8X4),
                scales=wp_s[e][:, lo:hi],
                in_=rounded[:, 0 : (hi - lo) * PACK],
            )

        def add_on_gpsimd(c):
            total = keep.tile([P, T], F32, name="total%d" % c)
            nc.gpsimd.tensor_tensor(total[:], by_token[c][:], by_partner[c][:], ALU.add)
            nc.sync.dma_start(out=out[c * P : (c + 1) * P, :], in_=total[:])

        def add_on_vector(c):
            for lo, hi in ((0, T // 2), (T // 2, T)):
                total = keep.tile([P, hi - lo], F32, name="total", tag="last%d" % lo)
                nc.vector.tensor_tensor(total[:], by_token[c][:, lo:hi], by_partner[c][:, lo:hi], ALU.add)
                nc.sync.dma_start(out=out[c * P : (c + 1) * P, lo:hi], in_=total[:])

        gated_second = [gated_sums(j) for j in (2, 3)]
        active_second = mask_on_vector(1, 0, C, "active1")
        round_partner_weights(0, 0, 0)

        dx0_first = copied("scalar", products("vb", [token_part(0, 0, P)])[:], "dx0_first")
        sums = products("sb", [token_part(2, 0, C), token_part(3, 0, C)])
        dx20 = copied("scalar", sums[:, 0:C], "dx20")
        dx30 = copied("scalar", sums[:, C:], "dx30")
        turned_second = turned(gated_second, "va")
        scatter_dx("vector", 0, 0, P, dx0_first[:])
        scatter_dx("scalar", 2, 0, C, dx20[:])
        scatter_dx("scalar", 3, 0, C, dx30[:])
        dh_second = masked(turned_second[:], active_second[:], rounded[:, HALF * PACK :])
        values = copied("vector", products("sa", [token_part(1, 0, C), token_part(0, P, C)])[:], "active1")
        quantise_gradient(dh_second, C, SLOTS)
        scatter_dx("vector", 1, 0, C, values[:, 0:C])
        scatter_dx("vector", 0, P, C, values[:, C:])

        sums = products("sb", [token_part(1, C, SLOTS), token_part(2, C, SLOTS)])
        dx11 = copied("scalar", sums[:, 0:C], "dx11")
        dx21 = copied("scalar", sums[:, C:], "dx21")
        scatter_dx("scalar", 1, C, SLOTS, dx11[:])
        scatter_dx("scalar", 2, C, SLOTS, dx21[:])

        round_partner_weights(0, 1, HALF)
        dx01 = copied("vector", products("va", [token_part(0, C, SLOTS)])[:], "wp_raw01")
        quantise_partner_weights(0, 0, K)
        scatter_dx("vector", 0, C, SLOTS, dx01[:])

        dp00 = copied("scalar", products("sa", [partner_part(0, 0, C)])[:], "dp00")
        scatter_dp("scalar", 0, 0, C, dp00[:])

        round_partner_weights(1, 0, 0)
        values = copied("vector", products("vb", [partner_part(1, 0, C), partner_part(LAST, SHARE, C)])[:], "wp_raw10")
        quantise_partner_weights(1, 0, HALF)
        scatter_dp("vector", 1, 0, C, values[:, 0:C])
        scatter_dp("vector", LAST, SHARE, C, values[:, C:])

        sums = products("sb", [partner_part(0, C, SLOTS), partner_part(1, C, SLOTS)])
        dp01 = copied("scalar", sums[:, 0:C], "dp01")
        dp11 = copied("scalar", sums[:, C:], "dp11")
        scatter_dp("scalar", 0, C, SLOTS, dp01[:])
        add_on_gpsimd(0)
        scatter_dp("scalar", 1, C, SLOTS, dp11[:])
        add_on_gpsimd(1)

        round_partner_weights(1, 1, 0)
        dp20 = copied("vector", products("va", [partner_part(2, 0, C)])[:], "wp_raw11")
        quantise_partner_weights(1, HALF, K)
        scatter_dp("vector", 2, 0, C, dp20[:])

        sums = products("sb", [token_part(LAST, C, SLOTS), partner_part(LAST, 0, SHARE)])
        dp3_share = copied("scalar", sums[:, C:], "dp3_share")
        dx31 = copied("scalar", sums[:, 0:C], "dx31")
        dp21 = copied("vector", products("vb", [partner_part(2, C, SLOTS)])[:], "dp21")
        dp31 = copied("vector", products("sums0", [partner_part(LAST, C, SLOTS)])[:], "dp31")
        scatter_dp("scalar", LAST, 0, SHARE, dp3_share[:])
        scatter_dp("vector", 2, C, SLOTS, dp21[:])
        add_on_gpsimd(2)
        scatter_dx("scalar", LAST, C, SLOTS, dx31[:])
        scatter_dp("vector", LAST, C, SLOTS, dp31[:])
        add_on_vector(LAST)
